import numpy as np
import ml_dtypes


def mxq(x, axis, fmt="e4m3"):
    dtype, down = {"e4m3": (ml_dtypes.float8_e4m3fn, 7), "e5m2": (ml_dtypes.float8_e5m2, 14)}[fmt]
    v = np.moveaxis(np.asarray(x, np.float32).astype(ml_dtypes.bfloat16).astype(np.float64), axis, -1)
    blocks = v.reshape(v.shape[:-1] + (-1, 32))
    amax = np.abs(blocks).max(-1, keepdims=True)
    byte = np.maximum(np.where(amax > 0, np.frexp(amax)[1] - 1 + 127, 0) - down, 1)
    scale = np.exp2(byte - 127.0)
    codes = (blocks / scale).astype(np.float32).astype(dtype).astype(np.float64)
    return np.moveaxis((codes * scale).reshape(v.shape), -1, axis)


WIDE = False


def mx_kscale(k):
    if not WIDE:
        return np.ones(k)
    levels = np.array([10, -10, 5, -5, 0])
    if k % 512:
        return np.exp2(np.random.permutation(np.resize(levels, k // 32))).repeat(32)
    a = np.empty((k // 512, 16))
    for p in range(k // 512):
        a[p, :8] = np.random.permutation(np.resize(levels, 8))
        for g in range(8):
            far = levels[np.abs(levels - a[p, g]) >= 10]
            a[p, g + 8] = far[np.random.randint(len(far))]
    return np.exp2(a.ravel()).repeat(32)


def f64(x):
    return np.asarray(x).astype(np.float64)


def striped(idx):
    return np.tile(idx.reshape(-1, 16).T, (8, 1)).astype(np.uint16)


def unstriped(offs):
    return offs[:16].T.reshape(-1).astype(np.int64)


def pack_weight(w):
    k, n = w.shape
    w = f64(np.asarray(w, np.float32).astype(ml_dtypes.bfloat16)).reshape(k // 32, 32, n)
    amax = np.abs(w).max(1)
    byte = np.clip(np.where(amax > 0, np.frexp(amax)[1] - 1 + 127 - 7, 1), 1, 254)
    scaled = (w * np.exp2(127.0 - byte)[:, None, :]).reshape(k, n).astype(np.float32)
    words = np.ascontiguousarray(scaled.reshape(k // 512, 128, 4, n).transpose(0, 1, 3, 2)).astype(ml_dtypes.float8_e4m3fn).view(np.uint8)
    return words, np.ascontiguousarray(byte.astype(np.uint8).reshape(k // 512, 16, n))


def unpack_weight(words, scales):
    g, p, n, _ = words.shape
    vals = np.ascontiguousarray(words).view(ml_dtypes.float8_e4m3fn).astype(np.float64) * np.repeat(np.exp2(scales.astype(np.float64) - 127.0), 8, axis=1)[..., None]
    return vals.transpose(0, 1, 3, 2).reshape(g * 512, n)


K, T, S, H, N, V = 1024, 2048, 512, 512, 128, 256
P = 2 ** 7


def setup_inputs():
    n = np.random.standard_normal
    s = mx_kscale(K)[:, None]
    u = mx_kscale(H)
    packed_xT = pack_weight(n((K, T)) * s)
    return {
        "x_words": packed_xT[0],
        "x_scales": packed_xT[1],
        "w1": (n((K, H)) / np.sqrt(K) / s).astype(np.float32),
        "m1": (np.tile(n(S) * 0.7, (P, 1))).astype(np.float32),
        "m2": (np.tile(n(V) * 0.7, (P, 1))).astype(np.float32),
        "unit": (np.random.uniform(0.5, 1.0, (H, 1)) * u[:, None]).astype(np.float32),
        "t1": (n((H, N)) / np.sqrt(2 * H) / u[:, None]).astype(np.float32),
        "t2": (n((H, N)) / np.sqrt(2 * H) / u[:, None]).astype(np.float32),
        "offs": striped(np.random.permutation(T)[:S]),
        "fa": striped(np.random.randint(0, S, S)),
        "fb": striped(np.random.randint(0, S, S)),
        "fc": striped(np.random.randint(0, V, V)),
        "fd": striped(np.random.randint(0, S, V)),
    }


def reference(x_words, x_scales, w1, m1, m2, unit, t1, t2, offs, fa, fb, fc, fd):
    xq = unpack_weight(x_words, x_scales)[:, unstriped(offs)]
    y = mxq(f64(w1), 0, "e4m3").T @ xq
    p1 = (y[:, unstriped(fa)] * y[:, unstriped(fb)]) * f64(m1)[:1]
    x1 = p1.reshape(len(p1), -1, 2).sum(axis=2)
    z0 = f64(unit) * x1
    x2 = (x1[:, unstriped(fc)] * y[:, unstriped(fd)]) * f64(m2)[:1]
    z1 = f64(unit) * x2
    return mxq(f64(t1), 0, "e4m3").T @ mxq(z0, 0, "e4m3") + mxq(f64(t2), 0, "e4m3").T @ mxq(z1, 0, "e4m3")

@@ -1,0 +1,218 @@
+from contextlib import ExitStack
+
+import concourse.mybir as mybir
+
+K, T, S, H, N, V = 1024, 2048, 512, 512, 128, 256
+FLOPS = 2 * K * H * S + 2 * 2 * H * N * V
+
+F32 = mybir.dt.float32
+BF16 = mybir.dt.bfloat16
+I32 = mybir.dt.int32
+U32 = mybir.dt.uint32
+U16 = mybir.dt.uint16
+U8 = mybir.dt.uint8
+FP8X4 = mybir.dt.float8_e4m3fn_x4
+MULT = mybir.AluOpType.mult
+ADD = mybir.AluOpType.add
+COPY = mybir.ActivationFunctionType.Copy
+
+P = 128
+PACK = 4
+PASSES = K // (P * PACK)
+SPARE = 16
+HALF_S = S // 2
+HALF_V = V // 2
+VECTOR_M = 80
+
+
+def tile_picked_ycin_both_p_kernel(
+    tc, x_words, x_scales, w1, m1, m2, unit, t1, t2, offs, fa, fb, fc, fd, out
+):
+    nc = tc.nc
+    with ExitStack() as ctx:
+        lists = ctx.enter_context(tc.tile_pool(name="lists", bufs=1))
+        keep = ctx.enter_context(tc.tile_pool(name="keep", bufs=1))
+        psum = ctx.enter_context(tc.psum_pool(name="psum", bufs=1))
+
+        offs_sb = lists.tile([P, S // 16], U16, name="offs_sb")
+        fa_sb = lists.tile([P, S // 16], U16, name="fa_sb")
+        fb_sb = lists.tile([P, S // 16], U16, name="fb_sb")
+        fc_sb = lists.tile([P, V // 16], U16, name="fc_sb")
+        fd_sb = lists.tile([P, V // 16], U16, name="fd_sb")
+
+        table_words = [keep.tile([P, T], I32, name=f"table_words{o}", align_bytes=64) for o in range(PASSES)]
+        table_scales = keep.tile([P, T], U8, name="table_scales", align_bytes=64)
+        w_raw = [keep.tile([P, PACK, H], F32, name=f"w_raw{o}", align_bytes=64) for o in range(PASSES)]
+        t_raw = [keep.tile([P, PACK, N], F32, name=f"t_raw{d}", align_bytes=64) for d in range(2)]
+        m1_sb = keep.tile([P, S], F32, name="m1_sb", align_bytes=64)
+        m2_sb = keep.tile([P, V], F32, name="m2_sb", align_bytes=64)
+        unit_sb = keep.tile([P, PACK], F32, name="unit_sb", align_bytes=64)
+        y = [keep.tile([P, S + SPARE], F32, name=f"y{t}", align_bytes=64) for t in range(PACK)]
+
+        nc.vector.memset(table_scales[:].bitcast(I32), 0)
+        for t in range(PACK):
+            nc.vector.memset(y[t][:, S:], 0.0)
+
+        def load_words(o):
+            nc.sync.dma_start(out=table_words[o][:], in_=x_words[o].rearrange("p c r -> p (c r)").bitcast(I32))
+
+        def load_w(o):
+            nc.sync.dma_start(out=w_raw[o][:], in_=w1[512 * o : 512 * (o + 1), :].rearrange("(p j) c -> p j c", j=PACK))
+
+        load_words(0)
+        for q in range(4):
+            nc.sync.dma_start(
+                out=table_scales[32 * q : 32 * q + 4 * PASSES, :].bitcast(I32),
+                in_=x_scales[:, 4 * q : 4 * q + 4, :].bitcast(I32),
+            )
+        nc.sync.dma_start(offs_sb[:], offs)
+        load_w(0)
+        load_w(1)
+        load_words(1)
+        nc.sync.dma_start(out=m1_sb[:], in_=m1)
+        nc.sync.dma_start(fa_sb[:], fa)
+        nc.sync.dma_start(fb_sb[:], fb)
+        nc.sync.dma_start(out=unit_sb[:], in_=unit.rearrange("(p t) o -> p (t o)", t=PACK))
+        nc.sync.dma_start(out=m2_sb[:], in_=m2)
+        nc.sync.dma_start(fd_sb[:], fd)
+        nc.sync.dma_start(fc_sb[:], fc)
+        for d, tm in enumerate((t1, t2)):
+            nc.sync.dma_start(out=t_raw[d][:], in_=tm.rearrange("(p j) n -> p j n", j=PACK))
+
+        x_codes0 = keep.tile([P, S], U32, name="x_codes0", align_bytes=64)
+        x_codes1 = keep.tile([P, S], U32, name="x_codes1", align_bytes=64)
+        x_planes = keep.tile([P, S], U8, name="x_planes", align_bytes=64)
+        w_grouped = [keep.tile([P, PACK, P, PACK], BF16, name=f"w_grouped{o}", align_bytes=64) for o in range(PASSES)]
+        w_codes = [keep.tile([P, H], U32, name=f"w_codes{o}", align_bytes=64) for o in range(PASSES)]
+        w_planes = [keep.tile([P, H], U8, name=f"w_planes{o}", align_bytes=64) for o in range(PASSES)]
+
+        def cast_w(o):
+            src = w_raw[o][:].rearrange("p j (m t) -> p m t j", t=PACK)
+            dst = w_grouped[o][:].rearrange("p t m j -> p m t j")
+            nc.scalar.activation(out=dst[:, VECTOR_M:], in_=src[:, VECTOR_M:], func=COPY)
+            nc.vector.tensor_copy(out=dst[:, :VECTOR_M], in_=src[:, :VECTOR_M])
+
+        def quantize_w(o):
+            nc.vector.quantize_mx(
+                out=w_codes[o][:].bitcast(FP8X4),
+                scales=w_planes[o][:],
+                in_=w_grouped[o][:].rearrange("p t m j -> p (t m j)"),
+            )
+
+        nc.vector.tensor_copy(x_codes0[:], table_words[0][:].bitcast(U32).indirect(offs_sb[:]))
+        cast_w(0)
+        nc.vector.tensor_copy(x_planes[:], table_scales[:].indirect(offs_sb[:]))
+        quantize_w(0)
+        cast_w(1)
+        quantize_w(1)
+        for h in range(2):
+            nc.vector.tensor_copy(
+                x_codes1[:, HALF_S * h : HALF_S * (h + 1)], table_words[1][:].bitcast(U32).indirect(offs_sb[:, 16 * h : 16 * (h + 1)])
+            )
+
+        x_codes = (x_codes0, x_codes1)
+        pieces = [(0, slice(0, HALF_S)), (0, slice(HALF_S, S))] + [(t, slice(0, S)) for t in range(1, PACK)]
+        y_acc = [psum.tile([P, cols.stop - cols.start], F32, name=f"y_acc{b}") for b, (t, cols) in enumerate(pieces)]
+        for o in range(PASSES):
+            for b, (t, cols) in enumerate(pieces):
+                chan = slice(P * t, P * (t + 1))
+                nc.tensor.matmul_mx(
+                    out=y_acc[b][:],
+                    lhsT=w_codes[o][:, chan].bitcast(FP8X4),
+                    lhsT_scale=w_planes[o][:, chan],
+                    rhs=x_codes[o][:, cols].bitcast(FP8X4),
+                    rhs_scale=x_planes[4 * o : P, cols],
+                    start=(o == 0),
+                    stop=(o == PASSES - 1),
+                )
+        for b, (t, cols) in enumerate(pieces):
+            nc.scalar.copy(out=y[t][:, cols], in_=y_acc[b][:])
+
+        first = [keep.tile([P, S], F32, name=f"first{t}", align_bytes=64) for t in range(PACK)]
+        p1 = [keep.tile([P, V, 2], F32, name=f"p1_{t}", align_bytes=64) for t in range(PACK)]
+        x1 = [keep.tile([P, V], F32, name=f"x1_{t}", align_bytes=64) for t in range(PACK)]
+        m2u = [keep.tile([P, V], F32, name=f"m2u{t}", align_bytes=64) for t in range(PACK)]
+        second = [keep.tile([P, V], F32, name=f"second{t}", align_bytes=64) for t in range(PACK)]
+        z0 = keep.tile([P, PACK, V], F32, name="z0", align_bytes=64)
+        z1 = [keep.tile([P, PACK, HALF_V], F32, name=f"z1_{h}", align_bytes=64) for h in range(2)]
+        z0_grouped = keep.tile([P, V, PACK], BF16, name="z0_grouped", align_bytes=64)
+        z1_grouped = [keep.tile([P, HALF_V, PACK], BF16, name=f"z1_grouped{h}", align_bytes=64) for h in range(2)]
+        t_grouped = keep.tile([P, 2, N, PACK], BF16, name="t_grouped", align_bytes=64)
+        t_codes = keep.tile([P, 2 * N], U32, name="t_codes", align_bytes=64)
+        t_planes = keep.tile([P, 2 * N], U8, name="t_planes", align_bytes=64)
+        z0_codes = keep.tile([P, V], U32, name="z0_codes", align_bytes=64)
+        z0_planes = keep.tile([P, V], U8, name="z0_planes", align_bytes=64)
+        z1_codes = [keep.tile([P, HALF_V], U32, name=f"z1_codes{h}", align_bytes=64) for h in range(2)]
+        z1_planes = [keep.tile([P, HALF_V], U8, name=f"z1_planes{h}", align_bytes=64) for h in range(2)]
+
+        for t in range(PACK):
+            nc.scalar.activation(out=m2u[t][:], in_=m2_sb[:], func=COPY, scale=unit_sb[:, t : t + 1])
+        for d in range(2):
+            nc.scalar.copy(out=t_grouped[:, d], in_=t_raw[d][:].rearrange("p j n -> p n j"))
+
+        for pair in ((0, 1), (2, 3)):
+            for t in pair:
+                nc.vector.tensor_tensor(first[t][:], y[t][:].indirect(fa_sb[:]), m1_sb[:], MULT)
+            for t in pair:
+                nc.vector.tensor_tensor(
+                    p1[t][:].rearrange("p v d -> p (v d)"), y[t][:].indirect(fb_sb[:]), first[t][:], MULT
+                )
+            for t in pair:
+                nc.vector.tensor_tensor(x1[t][:], p1[t][:, :, 0], p1[t][:, :, 1], ADD)
+                nc.scalar.activation(out=z0[:, t, :], in_=x1[t][:], func=COPY, scale=unit_sb[:, t : t + 1])
+        nc.scalar.copy(out=z0_grouped[:], in_=z0[:].rearrange("p t v -> p v t"))
+        nc.vector.quantize_mx(
+            out=t_codes[:].bitcast(FP8X4), scales=t_planes[:], in_=t_grouped[:].rearrange("p d n j -> p (d n j)")
+        )
+        for t in range(PACK):
+            nc.vector.tensor_tensor(second[t][:], y[t][:].indirect(fd_sb[:]), m2u[t][:], MULT)
+
+        def second_maps(h):
+            for t in range(PACK):
+                nc.vector.tensor_tensor(
+                    z1[h][:, t, :],
+                    x1[t][:].indirect(fc_sb[:, 8 * h : 8 * (h + 1)]),
+                    second[t][:, HALF_V * h : HALF_V * (h + 1)],
+                    MULT,
+                )
+
+        out_acc = [psum.tile([P, HALF_V], F32, name=f"out_acc{h}") for h in range(2)]
+        result = [keep.tile([P, HALF_V], F32, name=f"result{h}", align_bytes=64) for h in range(2)]
+
+        def finish(h):
+            cols = slice(HALF_V * h, HALF_V * (h + 1))
+            nc.vector.quantize_mx(
+                out=z1_codes[h][:].bitcast(FP8X4),
+                scales=z1_planes[h][:],
+                in_=z1_grouped[h][:].rearrange("p v t -> p (v t)"),
+            )
+            nc.tensor.matmul_mx(
+                out=out_acc[h][:],
+                lhsT=t_codes[:, :N].bitcast(FP8X4),
+                lhsT_scale=t_planes[:, :N],
+                rhs=z0_codes[:, cols].bitcast(FP8X4),
+                rhs_scale=z0_planes[:, cols],
+                start=True,
+                stop=False,
+            )
+            nc.tensor.matmul_mx(
+                out=out_acc[h][:],
+                lhsT=t_codes[:, N:].bitcast(FP8X4),
+                lhsT_scale=t_planes[:, N:],
+                rhs=z1_codes[h][:].bitcast(FP8X4),
+                rhs_scale=z1_planes[h][:],
+                start=False,
+                stop=True,
+            )
+            nc.scalar.copy(out=result[h][:], in_=out_acc[h][:])
+            nc.sync.dma_start(out=out[:, cols], in_=result[h][:])
+
+        second_maps(0)
+        nc.scalar.copy(out=z1_grouped[0][:], in_=z1[0][:].rearrange("p t v -> p v t"))
+        nc.vector.quantize_mx(
+            out=z0_codes[:].bitcast(FP8X4), scales=z0_planes[:], in_=z0_grouped[:].rearrange("p v t -> p (v t)")
+        )
+        second_maps(1)
+        finish(0)
+        nc.vector.tensor_copy(out=z1_grouped[1][:], in_=z1[1][:].rearrange("p t v -> p v t"))
+        finish(1)

@@ -1,6 +1,7 @@
 from contextlib import ExitStack
 
 import concourse.mybir as mybir
+from concourse.masks import make_identity
 
 K, T, S, H, N, V = 1024, 2048, 512, 512, 128, 256
 FLOPS = 2 * K * H * S + 2 * 2 * H * N * V
@@ -112,7 +113,7 @@ def tile_picked_ycin_both_p_kernel(
 
         x_codes = (x_codes0, x_codes1)
         pieces = [(0, slice(0, HALF_S)), (0, slice(HALF_S, S))] + [(t, slice(0, S)) for t in range(1, PACK)]
-        y_acc = [psum.tile([P, cols.stop - cols.start], F32, name=f"y_acc{b}") for b, (t, cols) in enumerate(pieces)]
+        y_acc = [psum.tile([P, cols.stop - cols.start], F32, name=f"y_acc{b}", tag=f"bank{b}") for b, (t, cols) in enumerate(pieces)]
         for o in range(PASSES):
             for b, (t, cols) in enumerate(pieces):
                 chan = slice(P * t, P * (t + 1))
@@ -128,13 +129,16 @@ def tile_picked_ycin_both_p_kernel(
         for b, (t, cols) in enumerate(pieces):
             nc.scalar.copy(out=y[t][:, cols], in_=y_acc[b][:])
 
+        identity = keep.tile([P, P], F32, name="identity", align_bytes=64)
+        make_identity(nc, identity[:])
         first = [keep.tile([P, S], F32, name=f"first{t}", align_bytes=64) for t in range(PACK)]
-        p1 = [keep.tile([P, V, 2], F32, name=f"p1_{t}", align_bytes=64) for t in range(PACK)]
+        p1 = [keep.tile([P, S], F32, name=f"p1_{t}", align_bytes=64) for t in range(PACK)]
+        x1_turned = [keep.tile([P, 2, P], F32, name=f"x1_turned{t}", align_bytes=64) for t in range(PACK)]
         x1 = [keep.tile([P, V], F32, name=f"x1_{t}", align_bytes=64) for t in range(PACK)]
         m2u = [keep.tile([P, V], F32, name=f"m2u{t}", align_bytes=64) for t in range(PACK)]
-        second = [keep.tile([P, V], F32, name=f"second{t}", align_bytes=64) for t in range(PACK)]
-        z0 = keep.tile([P, PACK, V], F32, name="z0", align_bytes=64)
-        z1 = [keep.tile([P, PACK, HALF_V], F32, name=f"z1_{h}", align_bytes=64) for h in range(2)]
+        second = [keep.tile([P, V], F32, name=f"second{t}", align_bytes=64) for t in range(PACK - 1)]
+        second_last0 = keep.tile([P, HALF_V], F32, name="second_last0", tag="late", align_bytes=64)
+        second_last1 = keep.tile([P, HALF_V], F32, name="second_last1", align_bytes=64)
         z0_grouped = keep.tile([P, V, PACK], BF16, name="z0_grouped", align_bytes=64)
         z1_grouped = [keep.tile([P, HALF_V, PACK], BF16, name=f"z1_grouped{h}", align_bytes=64) for h in range(2)]
         t_grouped = keep.tile([P, 2, N, PACK], BF16, name="t_grouped", align_bytes=64)
@@ -145,38 +149,57 @@ def tile_picked_ycin_both_p_kernel(
         z1_codes = [keep.tile([P, HALF_V], U32, name=f"z1_codes{h}", align_bytes=64) for h in range(2)]
         z1_planes = [keep.tile([P, HALF_V], U8, name=f"z1_planes{h}", align_bytes=64) for h in range(2)]
 
+        def pair_sum(t):
+            turned = psum.tile([P, 2, P], F32, name=f"turned{t}", tag=f"bank{5 + t % 2}")
+            for h in range(2):
+                for d in range(2):
+                    nc.tensor.matmul(
+                        out=turned[:, h, :],
+                        lhsT=p1[t][:, 2 * P * h + d : 2 * P * (h + 1) : 2],
+                        rhs=identity[:],
+                        is_transpose=True,
+                        start=(d == 0),
+                        stop=(d == 1),
+                    )
+            nc.scalar.copy(out=x1_turned[t][:], in_=turned[:])
+            back = psum.tile([P, 2, P], F32, name=f"back{t}", tag=f"bank{(7, 0)[t % 2]}")
+            for h in range(2):
+                nc.tensor.transpose(back[:, h, :], x1_turned[t][:, h, :], identity[:])
+            back_v = back[:].rearrange("p h v -> p (h v)")
+            nc.scalar.copy(out=x1[t][:], in_=back_v)
+            nc.scalar.activation(out=z0_grouped[:, :, t], in_=back_v, func=COPY, scale=unit_sb[:, t : t + 1])
+
         for t in range(PACK):
             nc.scalar.activation(out=m2u[t][:], in_=m2_sb[:], func=COPY, scale=unit_sb[:, t : t + 1])
-        for d in range(2):
-            nc.scalar.copy(out=t_grouped[:, d], in_=t_raw[d][:].rearrange("p j n -> p n j"))
-
         for pair in ((0, 1), (2, 3)):
             for t in pair:
                 nc.vector.tensor_tensor(first[t][:], y[t][:].indirect(fa_sb[:]), m1_sb[:], MULT)
             for t in pair:
-                nc.vector.tensor_tensor(
-                    p1[t][:].rearrange("p v d -> p (v d)"), y[t][:].indirect(fb_sb[:]), first[t][:], MULT
-                )
-            for t in pair:
-                nc.vector.tensor_tensor(x1[t][:], p1[t][:, :, 0], p1[t][:, :, 1], ADD)
-                nc.scalar.activation(out=z0[:, t, :], in_=x1[t][:], func=COPY, scale=unit_sb[:, t : t + 1])
-        nc.scalar.copy(out=z0_grouped[:], in_=z0[:].rearrange("p t v -> p v t"))
-        nc.vector.quantize_mx(
-            out=t_codes[:].bitcast(FP8X4), scales=t_planes[:], in_=t_grouped[:].rearrange("p d n j -> p (d n j)")
-        )
-        for t in range(PACK):
+                nc.vector.tensor_tensor(p1[t][:], y[t][:].indirect(fb_sb[:]), first[t][:], MULT)
+                pair_sum(t)
+        for d in range(2):
+            nc.scalar.copy(out=t_grouped[:, d], in_=t_raw[d][:].rearrange("p j n -> p n j"))
+        for t in range(PACK - 1):
             nc.vector.tensor_tensor(second[t][:], y[t][:].indirect(fd_sb[:]), m2u[t][:], MULT)
+        for h, dst in enumerate((second_last0, second_last1)):
+            nc.vector.tensor_tensor(
+                dst[:],
+                y[PACK - 1][:].indirect(fd_sb[:, 8 * h : 8 * (h + 1)]),
+                m2u[PACK - 1][:, HALF_V * h : HALF_V * (h + 1)],
+                MULT,
+            )
+        second_half = [
+            [second[t][:, HALF_V * h : HALF_V * (h + 1)] for t in range(PACK - 1)] + [last[:]]
+            for h, last in enumerate((second_last0, second_last1))
+        ]
 
-        def second_maps(h):
+        def second_maps(h, z1):
             for t in range(PACK):
                 nc.vector.tensor_tensor(
-                    z1[h][:, t, :],
-                    x1[t][:].indirect(fc_sb[:, 8 * h : 8 * (h + 1)]),
-                    second[t][:, HALF_V * h : HALF_V * (h + 1)],
-                    MULT,
+                    z1[:, t, :], x1[t][:].indirect(fc_sb[:, 8 * h : 8 * (h + 1)]), second_half[h][t], MULT
                 )
 
-        out_acc = [psum.tile([P, HALF_V], F32, name=f"out_acc{h}") for h in range(2)]
+        out_acc = [psum.tile([P, HALF_V], F32, name=f"out_acc{h}", tag=f"bank{1 + h}") for h in range(2)]
         result = [keep.tile([P, HALF_V], F32, name=f"result{h}", align_bytes=64) for h in range(2)]
 
         def finish(h):
@@ -204,15 +227,24 @@ def tile_picked_ycin_both_p_kernel(
                 start=False,
                 stop=True,
             )
-            nc.scalar.copy(out=result[h][:], in_=out_acc[h][:])
-            nc.sync.dma_start(out=out[:, cols], in_=result[h][:])
+            if h == 0:
+                nc.scalar.copy(out=result[h][:], in_=out_acc[h][:])
+                nc.scalar.dma_start(out=out[:, cols], in_=result[h][:])
+            else:
+                nc.vector.tensor_copy(out=result[h][:], in_=out_acc[h][:])
+                nc.sync.dma_start(out=out[:, cols], in_=result[h][:])
 
-        second_maps(0)
-        nc.scalar.copy(out=z1_grouped[0][:], in_=z1[0][:].rearrange("p t v -> p v t"))
+        z1_low = keep.tile([P, PACK, HALF_V], F32, name="z1_low", align_bytes=64)
+        second_maps(0, z1_low)
+        nc.scalar.copy(out=z1_grouped[0][:], in_=z1_low[:].rearrange("p t v -> p v t"))
+        nc.vector.quantize_mx(
+            out=t_codes[:].bitcast(FP8X4), scales=t_planes[:], in_=t_grouped[:].rearrange("p d n j -> p (d n j)")
+        )
+        z1_high = keep.tile([P, PACK, HALF_V], F32, name="z1_high", tag="late", align_bytes=64)
+        second_maps(1, z1_high)
         nc.vector.quantize_mx(
             out=z0_codes[:].bitcast(FP8X4), scales=z0_planes[:], in_=z0_grouped[:].rearrange("p v t -> p (v t)")
         )
-        second_maps(1)
+        nc.vector.tensor_copy(out=z1_grouped[1][:], in_=z1_high[:].rearrange("p t v -> p v t"))
         finish(0)
-        nc.vector.tensor_copy(out=z1_grouped[1][:], in_=z1[1][:].rearrange("p t v -> p v t"))
         finish(1)

@@ -23,7 +23,6 @@ PASSES = K // (P * PACK)
 SPARE = 16
 HALF_S = S // 2
 HALF_V = V // 2
-VECTOR_M = 80
 
 
 def tile_picked_ycin_both_p_kernel(
@@ -41,7 +40,7 @@ def tile_picked_ycin_both_p_kernel(
         fc_sb = lists.tile([P, V // 16], U16, name="fc_sb")
         fd_sb = lists.tile([P, V // 16], U16, name="fd_sb")
 
-        table_words = [keep.tile([P, T], I32, name=f"table_words{o}", align_bytes=64) for o in range(PASSES)]
+        table_words = [keep.tile([P, T], I32, name=f"table_words{o}", tag=f"table{o}", align_bytes=64) for o in range(PASSES)]
         table_scales = keep.tile([P, T], U8, name="table_scales", align_bytes=64)
         w_raw = [keep.tile([P, PACK, H], F32, name=f"w_raw{o}", align_bytes=64) for o in range(PASSES)]
         t_raw = [keep.tile([P, PACK, N], F32, name=f"t_raw{d}", align_bytes=64) for d in range(2)]
@@ -60,14 +59,18 @@ def tile_picked_ycin_both_p_kernel(
         def load_w(o):
             nc.sync.dma_start(out=w_raw[o][:], in_=w1[512 * o : 512 * (o + 1), :].rearrange("(p j) c -> p j c", j=PACK))
 
+        def load_scales(rows):
+            for r in rows:
+                for o in range(PASSES):
+                    nc.sync.dma_start(
+                        out=table_scales[4 * o + r : P : 32, :].bitcast(I32), in_=x_scales[o, r:16:4, :].bitcast(I32)
+                    )
+
         load_words(0)
-        for q in range(4):
-            nc.sync.dma_start(
-                out=table_scales[32 * q : 32 * q + 4 * PASSES, :].bitcast(I32),
-                in_=x_scales[:, 4 * q : 4 * q + 4, :].bitcast(I32),
-            )
         nc.sync.dma_start(offs_sb[:], offs)
+        load_scales((0, 1))
         load_w(0)
+        load_scales((2, 3))
         load_w(1)
         load_words(1)
         nc.sync.dma_start(out=m1_sb[:], in_=m1)
@@ -83,44 +86,53 @@ def tile_picked_ycin_both_p_kernel(
         x_codes0 = keep.tile([P, S], U32, name="x_codes0", align_bytes=64)
         x_codes1 = keep.tile([P, S], U32, name="x_codes1", align_bytes=64)
         x_planes = keep.tile([P, S], U8, name="x_planes", align_bytes=64)
-        w_grouped = [keep.tile([P, PACK, P, PACK], BF16, name=f"w_grouped{o}", align_bytes=64) for o in range(PASSES)]
-        w_codes = [keep.tile([P, H], U32, name=f"w_codes{o}", align_bytes=64) for o in range(PASSES)]
-        w_planes = [keep.tile([P, H], U8, name=f"w_planes{o}", align_bytes=64) for o in range(PASSES)]
+        w_grouped = {
+            (o, u): keep.tile([P, 2, P, PACK], BF16, name=f"w_grouped{o}_{u}", align_bytes=64)
+            for o in range(PASSES)
+            for u in range(2)
+        }
 
         def cast_w(o):
             src = w_raw[o][:].rearrange("p j (m t) -> p m t j", t=PACK)
-            dst = w_grouped[o][:].rearrange("p t m j -> p m t j")
-            nc.scalar.activation(out=dst[:, VECTOR_M:], in_=src[:, VECTOR_M:], func=COPY)
-            nc.vector.tensor_copy(out=dst[:, :VECTOR_M], in_=src[:, :VECTOR_M])
+            nc.scalar.activation(out=w_grouped[o, 1][:].rearrange("p t m j -> p m t j"), in_=src[:, :, 2:4], func=COPY)
+            nc.vector.tensor_copy(out=w_grouped[o, 0][:].rearrange("p t m j -> p m t j"), in_=src[:, :, 0:2])
 
-        def quantize_w(o):
+        w_mx = {}
+
+        def quantize_w(o, u, tag):
+            codes = keep.tile([P, 2 * P], U32, name=f"w_codes{o}_{u}", tag=tag, align_bytes=64)
+            planes = keep.tile([P, 2 * P], U8, name=f"w_planes{o}_{u}", align_bytes=64)
             nc.vector.quantize_mx(
-                out=w_codes[o][:].bitcast(FP8X4),
-                scales=w_planes[o][:],
-                in_=w_grouped[o][:].rearrange("p t m j -> p (t m j)"),
+                out=codes[:].bitcast(FP8X4),
+                scales=planes[:],
+                in_=w_grouped[o, u][:].rearrange("p t m j -> p (t m j)"),
             )
+            for i in range(2):
+                w_mx[o, 2 * u + i] = (codes[:, P * i : P * (i + 1)], planes[:, P * i : P * (i + 1)])
 
         nc.vector.tensor_copy(x_codes0[:], table_words[0][:].bitcast(U32).indirect(offs_sb[:]))
         cast_w(0)
         nc.vector.tensor_copy(x_planes[:], table_scales[:].indirect(offs_sb[:]))
-        quantize_w(0)
+        quantize_w(0, 0, "w_codes00")
         cast_w(1)
-        quantize_w(1)
+        quantize_w(0, 1, "w_codes01")
+        quantize_w(1, 0, "w_codes10")
         for h in range(2):
             nc.vector.tensor_copy(
                 x_codes1[:, HALF_S * h : HALF_S * (h + 1)], table_words[1][:].bitcast(U32).indirect(offs_sb[:, 16 * h : 16 * (h + 1)])
             )
 
+        quantize_w(1, 1, "table1")
         x_codes = (x_codes0, x_codes1)
-        pieces = [(0, slice(0, HALF_S)), (0, slice(HALF_S, S))] + [(t, slice(0, S)) for t in range(1, PACK)]
+        pieces = [(t, slice(HALF_S * h, HALF_S * (h + 1))) for h in range(2) for t in (0, 1)]
+        pieces = pieces + [(t, slice(0, S)) for t in (2, 3)]
         y_acc = [psum.tile([P, cols.stop - cols.start], F32, name=f"y_acc{b}", tag=f"bank{b}") for b, (t, cols) in enumerate(pieces)]
         for o in range(PASSES):
             for b, (t, cols) in enumerate(pieces):
-                chan = slice(P * t, P * (t + 1))
                 nc.tensor.matmul_mx(
                     out=y_acc[b][:],
-                    lhsT=w_codes[o][:, chan].bitcast(FP8X4),
-                    lhsT_scale=w_planes[o][:, chan],
+                    lhsT=w_mx[o, t][0].bitcast(FP8X4),
+                    lhsT_scale=w_mx[o, t][1],
                     rhs=x_codes[o][:, cols].bitcast(FP8X4),
                     rhs_scale=x_planes[4 * o : P, cols],
                     start=(o == 0),
@@ -129,14 +141,14 @@ def tile_picked_ycin_both_p_kernel(
         for b, (t, cols) in enumerate(pieces):
             nc.scalar.copy(out=y[t][:, cols], in_=y_acc[b][:])
 
-        identity = keep.tile([P, P], F32, name="identity", align_bytes=64)
+        identity = keep.tile([P, P], F32, name="identity", tag="table0", align_bytes=64)
         make_identity(nc, identity[:])
         first = [keep.tile([P, S], F32, name=f"first{t}", align_bytes=64) for t in range(PACK)]
         p1 = [keep.tile([P, S], F32, name=f"p1_{t}", align_bytes=64) for t in range(PACK)]
-        x1_turned = [keep.tile([P, 2, P], F32, name=f"x1_turned{t}", align_bytes=64) for t in range(PACK)]
+        x1_turned = [keep.tile([P, 2, P], F32, name=f"x1_turned{t}", align_bytes=64) for t in range(PACK - 1)]
         x1 = [keep.tile([P, V], F32, name=f"x1_{t}", align_bytes=64) for t in range(PACK)]
         m2u = [keep.tile([P, V], F32, name=f"m2u{t}", align_bytes=64) for t in range(PACK)]
-        second = [keep.tile([P, V], F32, name=f"second{t}", align_bytes=64) for t in range(PACK - 1)]
+        second = {t: keep.tile([P, V], F32, name=f"second{t}", align_bytes=64) for t in (0, 1, 3)}
         second_last0 = keep.tile([P, HALF_V], F32, name="second_last0", tag="late", align_bytes=64)
         second_last1 = keep.tile([P, HALF_V], F32, name="second_last1", align_bytes=64)
         z0_grouped = keep.tile([P, V, PACK], BF16, name="z0_grouped", align_bytes=64)
@@ -150,7 +162,7 @@ def tile_picked_ycin_both_p_kernel(
         z1_planes = [keep.tile([P, HALF_V], U8, name=f"z1_planes{h}", align_bytes=64) for h in range(2)]
 
         def pair_sum(t):
-            turned = psum.tile([P, 2, P], F32, name=f"turned{t}", tag=f"bank{5 + t % 2}")
+            turned = psum.tile([P, 2, P], F32, name=f"turned{t}", tag=f"bank{(6, 7, 1)[t]}")
             for h in range(2):
                 for d in range(2):
                     nc.tensor.matmul(
@@ -162,7 +174,7 @@ def tile_picked_ycin_both_p_kernel(
                         stop=(d == 1),
                     )
             nc.scalar.copy(out=x1_turned[t][:], in_=turned[:])
-            back = psum.tile([P, 2, P], F32, name=f"back{t}", tag=f"bank{(7, 0)[t % 2]}")
+            back = psum.tile([P, 2, P], F32, name=f"back{t}", tag=f"bank{(0, 1, 0)[t]}")
             for h in range(2):
                 nc.tensor.transpose(back[:, h, :], x1_turned[t][:, h, :], identity[:])
             back_v = back[:].rearrange("p h v -> p (h v)")
@@ -171,35 +183,34 @@ def tile_picked_ycin_both_p_kernel(
 
         for t in range(PACK):
             nc.scalar.activation(out=m2u[t][:], in_=m2_sb[:], func=COPY, scale=unit_sb[:, t : t + 1])
+        for d in range(2):
+            nc.scalar.copy(out=t_grouped[:, d], in_=t_raw[d][:].rearrange("p j n -> p n j"))
         for pair in ((0, 1), (2, 3)):
             for t in pair:
                 nc.vector.tensor_tensor(first[t][:], y[t][:].indirect(fa_sb[:]), m1_sb[:], MULT)
             for t in pair:
                 nc.vector.tensor_tensor(p1[t][:], y[t][:].indirect(fb_sb[:]), first[t][:], MULT)
-                pair_sum(t)
-        for d in range(2):
-            nc.scalar.copy(out=t_grouped[:, d], in_=t_raw[d][:].rearrange("p j n -> p n j"))
-        for t in range(PACK - 1):
-            nc.vector.tensor_tensor(second[t][:], y[t][:].indirect(fd_sb[:]), m2u[t][:], MULT)
-        for h, dst in enumerate((second_last0, second_last1)):
+                if t < PACK - 1:
+                    pair_sum(t)
+        def look_up_fd(dst, t, h0, h1):
             nc.vector.tensor_tensor(
-                dst[:],
-                y[PACK - 1][:].indirect(fd_sb[:, 8 * h : 8 * (h + 1)]),
-                m2u[PACK - 1][:, HALF_V * h : HALF_V * (h + 1)],
-                MULT,
+                dst, y[t][:].indirect(fd_sb[:, 8 * h0 : 8 * h1]), m2u[t][:, HALF_V * h0 : HALF_V * h1], MULT
             )
-        second_half = [
-            [second[t][:, HALF_V * h : HALF_V * (h + 1)] for t in range(PACK - 1)] + [last[:]]
-            for h, last in enumerate((second_last0, second_last1))
-        ]
+
+        look_up_fd(second[0][:], 0, 0, 2)
+        nc.vector.tensor_tensor(x1[3][:], p1[3][:, 0:S:2], p1[3][:, 1:S:2], ADD)
+        nc.scalar.activation(out=z0_grouped[:, :, 3], in_=x1[3][:], func=COPY, scale=unit_sb[:, 3:4])
+        look_up_fd(second[3][:], 3, 0, 2)
+        look_up_fd(second[1][:], 1, 0, 2)
+        look_up_fd(second_last0[:], 2, 0, 1)
+        look_up_fd(second_last1[:], 2, 1, 2)
 
         def second_maps(h, z1):
-            for t in range(PACK):
-                nc.vector.tensor_tensor(
-                    z1[:, t, :], x1[t][:].indirect(fc_sb[:, 8 * h : 8 * (h + 1)]), second_half[h][t], MULT
-                )
+            for t in (3, 0, 1, 2):
+                other = (second_last0, second_last1)[h][:] if t == 2 else second[t][:, HALF_V * h : HALF_V * (h + 1)]
+                nc.vector.tensor_tensor(z1[:, t, :], x1[t][:].indirect(fc_sb[:, 8 * h : 8 * (h + 1)]), other, MULT)
 
-        out_acc = [psum.tile([P, HALF_V], F32, name=f"out_acc{h}", tag=f"bank{1 + h}") for h in range(2)]
+        out_acc = [psum.tile([P, HALF_V], F32, name=f"out_acc{h}", tag=f"bank{2 + h}") for h in range(2)]
         result = [keep.tile([P, HALF_V], F32, name=f"result{h}", align_bytes=64) for h in range(2)]
 
         def finish(h):

@@ -162,7 +162,7 @@ def tile_picked_ycin_both_p_kernel(
         z1_planes = [keep.tile([P, HALF_V], U8, name=f"z1_planes{h}", align_bytes=64) for h in range(2)]
 
         def pair_sum(t):
-            turned = psum.tile([P, 2, P], F32, name=f"turned{t}", tag=f"bank{(6, 7, 1)[t]}")
+            turned = psum.tile([P, 2, P], F32, name=f"turned{t}", tag=f"bank{(6, 7, 7)[t]}")
             for h in range(2):
                 for d in range(2):
                     nc.tensor.matmul(

@@ -14,7 +14,6 @@ U16 = mybir.dt.uint16
 U8 = mybir.dt.uint8
 FP8X4 = mybir.dt.float8_e4m3fn_x4
 MULT = mybir.AluOpType.mult
-ADD = mybir.AluOpType.add
 COPY = mybir.ActivationFunctionType.Copy
 
 P = 128
@@ -23,6 +22,7 @@ PASSES = K // (P * PACK)
 SPARE = 16
 HALF_S = S // 2
 HALF_V = V // 2
+HALF_H = H // 2
 
 
 def tile_picked_ycin_both_p_kernel(
@@ -34,203 +34,199 @@ def tile_picked_ycin_both_p_kernel(
         keep = ctx.enter_context(tc.tile_pool(name="keep", bufs=1))
         psum = ctx.enter_context(tc.psum_pool(name="psum", bufs=1))
 
+        def sb(shape, dtype, name, tag=None):
+            return keep.tile(shape, dtype, name=name, tag=tag or name, align_bytes=64)
+
+        def bank(b, shape, name):
+            return psum.tile(shape, F32, name=name, tag=f"bank{b}")
+
         offs_sb = lists.tile([P, S // 16], U16, name="offs_sb")
         fa_sb = lists.tile([P, S // 16], U16, name="fa_sb")
         fb_sb = lists.tile([P, S // 16], U16, name="fb_sb")
         fc_sb = lists.tile([P, V // 16], U16, name="fc_sb")
         fd_sb = lists.tile([P, V // 16], U16, name="fd_sb")
 
-        table_words = [keep.tile([P, T], I32, name=f"table_words{o}", tag=f"table{o}", align_bytes=64) for o in range(PASSES)]
-        table_scales = keep.tile([P, T], U8, name="table_scales", align_bytes=64)
-        w_raw = [keep.tile([P, PACK, H], F32, name=f"w_raw{o}", align_bytes=64) for o in range(PASSES)]
-        t_raw = [keep.tile([P, PACK, N], F32, name=f"t_raw{d}", align_bytes=64) for d in range(2)]
-        m1_sb = keep.tile([P, S], F32, name="m1_sb", align_bytes=64)
-        m2_sb = keep.tile([P, V], F32, name="m2_sb", align_bytes=64)
-        unit_sb = keep.tile([P, PACK], F32, name="unit_sb", align_bytes=64)
-        y = [keep.tile([P, S + SPARE], F32, name=f"y{t}", align_bytes=64) for t in range(PACK)]
+        table_words = [sb([P, T], I32, f"table_words{o}") for o in range(PASSES)]
+        table_scales = sb([P, T], U8, "table_scales")
+        w_raw0 = sb([P, PACK, H], F32, "w_raw0")
+        w_raw1 = [sb([P, PACK, HALF_H], F32, f"w_raw1_{c}") for c in range(2)]
+        t_raw = [sb([P, PACK, N], F32, f"t_raw{d}") for d in range(2)]
+        m1_sb = sb([P, S], F32, "m1_sb")
+        m2_sb = sb([P, V], F32, "m2_sb")
+        unit_sb = sb([P, PACK], F32, "unit_sb")
+        y = [sb([P, S + SPARE], F32, f"y{t}") for t in range(PACK)]
+        identity = sb([P, P], F32, "identity")
 
-        nc.vector.memset(table_scales[:].bitcast(I32), 0)
+        nc.gpsimd.memset(table_scales[:].bitcast(I32), 0)
+        make_identity(nc, identity[:])
         for t in range(PACK):
-            nc.vector.memset(y[t][:, S:], 0.0)
+            nc.gpsimd.memset(y[t][:, S:], 0.0)
 
         def load_words(o):
             nc.sync.dma_start(out=table_words[o][:], in_=x_words[o].rearrange("p c r -> p (c r)").bitcast(I32))
 
-        def load_w(o):
-            nc.sync.dma_start(out=w_raw[o][:], in_=w1[512 * o : 512 * (o + 1), :].rearrange("(p j) c -> p j c", j=PACK))
-
-        def load_scales(rows):
-            for r in rows:
-                for o in range(PASSES):
-                    nc.sync.dma_start(
-                        out=table_scales[4 * o + r : P : 32, :].bitcast(I32), in_=x_scales[o, r:16:4, :].bitcast(I32)
-                    )
-
         load_words(0)
         nc.sync.dma_start(offs_sb[:], offs)
-        load_scales((0, 1))
-        load_w(0)
-        load_scales((2, 3))
-        load_w(1)
+        for q in range(4):
+            nc.sync.dma_start(
+                out=table_scales[32 * q : 32 * q + 8, :].bitcast(I32), in_=x_scales[:, 4 * q : 4 * q + 4, :].bitcast(I32)
+            )
+        nc.sync.dma_start(out=w_raw0[:], in_=w1[:512, :].rearrange("(p j) c -> p j c", j=PACK))
         load_words(1)
+        for c in range(2):
+            nc.sync.dma_start(
+                out=w_raw1[c][:], in_=w1[512:, HALF_H * c : HALF_H * (c + 1)].rearrange("(p j) c -> p j c", j=PACK)
+            )
         nc.sync.dma_start(out=m1_sb[:], in_=m1)
         nc.sync.dma_start(fa_sb[:], fa)
         nc.sync.dma_start(fb_sb[:], fb)
+        for d, tm in enumerate((t1, t2)):
+            nc.sync.dma_start(out=t_raw[d][:], in_=tm.rearrange("(p j) n -> p j n", j=PACK))
         nc.sync.dma_start(out=unit_sb[:], in_=unit.rearrange("(p t) o -> p (t o)", t=PACK))
         nc.sync.dma_start(out=m2_sb[:], in_=m2)
         nc.sync.dma_start(fd_sb[:], fd)
         nc.sync.dma_start(fc_sb[:], fc)
-        for d, tm in enumerate((t1, t2)):
-            nc.sync.dma_start(out=t_raw[d][:], in_=tm.rearrange("(p j) n -> p j n", j=PACK))
 
-        x_codes0 = keep.tile([P, S], U32, name="x_codes0", align_bytes=64)
-        x_codes1 = keep.tile([P, S], U32, name="x_codes1", align_bytes=64)
-        x_planes = keep.tile([P, S], U8, name="x_planes", align_bytes=64)
-        w_grouped = {
-            (o, u): keep.tile([P, 2, P, PACK], BF16, name=f"w_grouped{o}_{u}", align_bytes=64)
-            for o in range(PASSES)
-            for u in range(2)
-        }
-
-        def cast_w(o):
-            src = w_raw[o][:].rearrange("p j (m t) -> p m t j", t=PACK)
-            nc.scalar.activation(out=w_grouped[o, 1][:].rearrange("p t m j -> p m t j"), in_=src[:, :, 2:4], func=COPY)
-            nc.vector.tensor_copy(out=w_grouped[o, 0][:].rearrange("p t m j -> p m t j"), in_=src[:, :, 0:2])
-
+        x_codes = [sb([P, S], U32, f"x_codes{o}") for o in range(PASSES)]
+        x_planes = sb([P, S], U8, "x_planes")
+        w_grouped = {(o, u): sb([P, 2, P, PACK], BF16, f"w_grouped{o}_{u}") for o in range(PASSES) for u in range(2)}
         w_mx = {}
 
-        def quantize_w(o, u, tag):
-            codes = keep.tile([P, 2 * P], U32, name=f"w_codes{o}_{u}", tag=tag, align_bytes=64)
-            planes = keep.tile([P, 2 * P], U8, name=f"w_planes{o}_{u}", align_bytes=64)
-            nc.vector.quantize_mx(
-                out=codes[:].bitcast(FP8X4),
-                scales=planes[:],
-                in_=w_grouped[o, u][:].rearrange("p t m j -> p (t m j)"),
-            )
-            for i in range(2):
-                w_mx[o, 2 * u + i] = (codes[:, P * i : P * (i + 1)], planes[:, P * i : P * (i + 1)])
+        def cast_w(o, raw, m0):
+            src = raw[:].rearrange("p j (m t) -> p m t j", t=PACK)
+            ms = slice(m0, m0 + src.shape[1])
+            nc.vector.tensor_copy(out=w_grouped[o, 0][:, :, ms].rearrange("p t m j -> p m t j"), in_=src[:, :, 0:2])
+            nc.scalar.copy(out=w_grouped[o, 1][:, :, ms].rearrange("p t m j -> p m t j"), in_=src[:, :, 2:4])
 
-        nc.vector.tensor_copy(x_codes0[:], table_words[0][:].bitcast(U32).indirect(offs_sb[:]))
-        cast_w(0)
-        nc.vector.tensor_copy(x_planes[:], table_scales[:].indirect(offs_sb[:]))
-        quantize_w(0, 0, "w_codes00")
-        cast_w(1)
-        quantize_w(0, 1, "w_codes01")
-        quantize_w(1, 0, "w_codes10")
-        for h in range(2):
-            nc.vector.tensor_copy(
-                x_codes1[:, HALF_S * h : HALF_S * (h + 1)], table_words[1][:].bitcast(U32).indirect(offs_sb[:, 16 * h : 16 * (h + 1)])
-            )
+        def quantize(codes, planes, grouped):
+            nc.vector.quantize_mx(out=codes.bitcast(FP8X4), scales=planes, in_=grouped)
 
-        quantize_w(1, 1, "table1")
-        x_codes = (x_codes0, x_codes1)
-        pieces = [(t, slice(HALF_S * h, HALF_S * (h + 1))) for h in range(2) for t in (0, 1)]
-        pieces = pieces + [(t, slice(0, S)) for t in (2, 3)]
-        y_acc = [psum.tile([P, cols.stop - cols.start], F32, name=f"y_acc{b}", tag=f"bank{b}") for b, (t, cols) in enumerate(pieces)]
-        for o in range(PASSES):
+        def quantize_w(o, slots):
+            codes = sb([P, len(slots) * P], U32, f"w_codes{o}_{slots[0]}")
+            planes = sb([P, len(slots) * P], U8, f"w_planes{o}_{slots[0]}")
+            i0 = slots[0] % 2
+            grouped = w_grouped[o, slots[0] // 2][:, i0 : i0 + len(slots)]
+            quantize(codes[:], planes[:], grouped.rearrange("p t m j -> p (t m j)"))
+            for i, t in enumerate(slots):
+                w_mx[o, t] = (codes[:, P * i : P * (i + 1)], planes[:, P * i : P * (i + 1)])
+
+        pieces = [(0, slice(0, HALF_S)), (0, slice(HALF_S, S))] + [(t, slice(0, S)) for t in range(1, PACK)]
+        y_acc = [bank(b, [P, cols.stop - cols.start], f"y_acc{b}") for b, (t, cols) in enumerate(pieces)]
+
+        def products(o, slots):
             for b, (t, cols) in enumerate(pieces):
-                nc.tensor.matmul_mx(
-                    out=y_acc[b][:],
-                    lhsT=w_mx[o, t][0].bitcast(FP8X4),
-                    lhsT_scale=w_mx[o, t][1],
-                    rhs=x_codes[o][:, cols].bitcast(FP8X4),
-                    rhs_scale=x_planes[4 * o : P, cols],
-                    start=(o == 0),
-                    stop=(o == PASSES - 1),
-                )
+                if t in slots:
+                    nc.tensor.matmul_mx(
+                        out=y_acc[b][:],
+                        lhsT=w_mx[o, t][0].bitcast(FP8X4),
+                        lhsT_scale=w_mx[o, t][1],
+                        rhs=x_codes[o][:, cols].bitcast(FP8X4),
+                        rhs_scale=x_planes[4 * o : P, cols],
+                        start=(o == 0),
+                        stop=(o == PASSES - 1),
+                    )
+
+        nc.vector.tensor_copy(x_codes[0][:], table_words[0][:].bitcast(U32).indirect(offs_sb[:]))
+        nc.vector.tensor_copy(x_planes[:], table_scales[:].indirect(offs_sb[:]))
+        cast_w(0, w_raw0, 0)
+        quantize_w(0, (0, 1))
+        quantize_w(0, (2, 3))
+        products(0, range(PACK))
+        nc.vector.tensor_copy(x_codes[1][:], table_words[1][:].bitcast(U32).indirect(offs_sb[:]))
+        for c in range(2):
+            cast_w(1, w_raw1[c], P // 2 * c)
+        for slots in ((0,), (1,), (2, 3)):
+            quantize_w(1, slots)
+            products(1, slots)
         for b, (t, cols) in enumerate(pieces):
-            nc.scalar.copy(out=y[t][:, cols], in_=y_acc[b][:])
+            copy = nc.vector.tensor_copy if b == 1 else nc.scalar.copy
+            copy(out=y[t][:, cols], in_=y_acc[b][:])
 
-        identity = keep.tile([P, P], F32, name="identity", tag="table0", align_bytes=64)
-        make_identity(nc, identity[:])
-        first = [keep.tile([P, S], F32, name=f"first{t}", align_bytes=64) for t in range(PACK)]
-        p1 = [keep.tile([P, S], F32, name=f"p1_{t}", align_bytes=64) for t in range(PACK)]
-        x1_turned = [keep.tile([P, 2, P], F32, name=f"x1_turned{t}", align_bytes=64) for t in range(PACK - 1)]
-        x1 = [keep.tile([P, V], F32, name=f"x1_{t}", align_bytes=64) for t in range(PACK)]
-        m2u = [keep.tile([P, V], F32, name=f"m2u{t}", align_bytes=64) for t in range(PACK)]
-        second = {t: keep.tile([P, V], F32, name=f"second{t}", align_bytes=64) for t in (0, 1, 3)}
-        second_last0 = keep.tile([P, HALF_V], F32, name="second_last0", tag="late", align_bytes=64)
-        second_last1 = keep.tile([P, HALF_V], F32, name="second_last1", align_bytes=64)
-        z0_grouped = keep.tile([P, V, PACK], BF16, name="z0_grouped", align_bytes=64)
-        z1_grouped = [keep.tile([P, HALF_V, PACK], BF16, name=f"z1_grouped{h}", align_bytes=64) for h in range(2)]
-        t_grouped = keep.tile([P, 2, N, PACK], BF16, name="t_grouped", align_bytes=64)
-        t_codes = keep.tile([P, 2 * N], U32, name="t_codes", align_bytes=64)
-        t_planes = keep.tile([P, 2 * N], U8, name="t_planes", align_bytes=64)
-        z0_codes = keep.tile([P, V], U32, name="z0_codes", align_bytes=64)
-        z0_planes = keep.tile([P, V], U8, name="z0_planes", align_bytes=64)
-        z1_codes = [keep.tile([P, HALF_V], U32, name=f"z1_codes{h}", align_bytes=64) for h in range(2)]
-        z1_planes = [keep.tile([P, HALF_V], U8, name=f"z1_planes{h}", align_bytes=64) for h in range(2)]
+        first = [sb([P, S], F32, f"first{t}") for t in range(PACK)]
+        x1 = [sb([P, V], F32, f"x1_{t}") for t in range(PACK)]
+        m2u = [sb([P, V], F32, f"m2u{t}") for t in range(PACK)]
+        z0_rows = [sb([P, PACK, HALF_V], BF16, f"z0_rows{h}") for h in range(2)]
+        z0_grouped = [sb([P, HALF_V, PACK], BF16, f"z0_grouped{h}") for h in range(2)]
+        z1_grouped = [sb([P, HALF_V, PACK], BF16, f"z1_grouped{h}") for h in range(2)]
+        t_grouped = sb([P, 2, N, PACK], BF16, "t_grouped", "w_codes1_2")
+        t_codes = sb([P, 2 * N], U32, "t_codes")
+        t_planes = sb([P, 2 * N], U8, "t_planes")
+        z0_codes = [sb([P, HALF_V], U32, f"z0_codes{h}") for h in range(2)]
+        z0_planes = [sb([P, HALF_V], U8, f"z0_planes{h}") for h in range(2)]
+        z1_codes = [sb([P, HALF_V], U32, f"z1_codes{h}") for h in range(2)]
+        z1_planes = [sb([P, HALF_V], U8, f"z1_planes{h}") for h in range(2)]
+        result = [sb([P, HALF_V], F32, f"result{h}") for h in range(2)]
+        second = [sb([P, V], F32, f"second{t}") for t in range(PACK)]
+        p1 = {}
 
-        def pair_sum(t):
-            turned = psum.tile([P, 2, P], F32, name=f"turned{t}", tag=f"bank{(6, 7, 7)[t]}")
-            for h in range(2):
+        def interleave(copy, dst, src):
+            copy(out=dst.rearrange("p (c i) j -> p c j i", i=4), in_=src.rearrange("p j (c i) -> p c j i", i=4))
+
+        def look_up_fa(t):
+            nc.vector.tensor_tensor(first[t][:], y[t][:].indirect(fa_sb[:]), m1_sb[:], MULT)
+
+        def look_up_fb(t, halves, turn_bank, back_bank):
+            n = len(halves)
+            cols = slice(HALF_S * halves[0], HALF_S * (halves[-1] + 1))
+            vs = slice(cols.start // 2, cols.stop // 2)
+            name = f"{t}_{halves[0]}"
+            p1[name] = sb([P, n, HALF_S], F32, f"p1_{name}")
+            nc.vector.tensor_tensor(
+                p1[name][:].rearrange("p h s -> p (h s)"),
+                y[t][:].indirect(fb_sb[:, cols.start // 16 : cols.stop // 16]),
+                first[t][:, cols],
+                MULT,
+            )
+            turned = bank(turn_bank, [P, n, P], f"turned{name}")
+            for h in range(n):
                 for d in range(2):
                     nc.tensor.matmul(
                         out=turned[:, h, :],
-                        lhsT=p1[t][:, 2 * P * h + d : 2 * P * (h + 1) : 2],
+                        lhsT=p1[name][:, h, d::2],
                         rhs=identity[:],
                         is_transpose=True,
                         start=(d == 0),
                         stop=(d == 1),
                     )
-            nc.scalar.copy(out=x1_turned[t][:], in_=turned[:])
-            back = psum.tile([P, 2, P], F32, name=f"back{t}", tag=f"bank{(0, 1, 0)[t]}")
-            for h in range(2):
-                nc.tensor.transpose(back[:, h, :], x1_turned[t][:, h, :], identity[:])
+            x1_turned = sb([P, n, P], F32, f"x1_turned{name}")
+            nc.scalar.copy(out=x1_turned[:], in_=turned[:])
+            back = bank(back_bank, [P, n, P], f"back{name}")
+            for h in range(n):
+                nc.tensor.transpose(back[:, h, :], x1_turned[:, h, :], identity[:])
             back_v = back[:].rearrange("p h v -> p (h v)")
-            nc.scalar.copy(out=x1[t][:], in_=back_v)
-            nc.scalar.activation(out=z0_grouped[:, :, t], in_=back_v, func=COPY, scale=unit_sb[:, t : t + 1])
+            nc.scalar.copy(out=x1[t][:, vs], in_=back_v)
+            for i, h in enumerate(halves):
+                nc.scalar.activation(out=z0_rows[h][:, t, :], in_=back[:, i, :], func=COPY, scale=unit_sb[:, t : t + 1])
 
-        for t in range(PACK):
-            nc.scalar.activation(out=m2u[t][:], in_=m2_sb[:], func=COPY, scale=unit_sb[:, t : t + 1])
-        for d in range(2):
-            nc.scalar.copy(out=t_grouped[:, d], in_=t_raw[d][:].rearrange("p j n -> p n j"))
-        for pair in ((0, 1), (2, 3)):
-            for t in pair:
-                nc.vector.tensor_tensor(first[t][:], y[t][:].indirect(fa_sb[:]), m1_sb[:], MULT)
-            for t in pair:
-                nc.vector.tensor_tensor(p1[t][:], y[t][:].indirect(fb_sb[:]), first[t][:], MULT)
-                if t < PACK - 1:
-                    pair_sum(t)
-        def look_up_fd(dst, t, h0, h1):
-            nc.vector.tensor_tensor(
-                dst, y[t][:].indirect(fd_sb[:, 8 * h0 : 8 * h1]), m2u[t][:, HALF_V * h0 : HALF_V * h1], MULT
-            )
+        def look_up_fd(t):
+            nc.vector.tensor_tensor(second[t][:], y[t][:].indirect(fd_sb[:]), m2u[t][:], MULT)
 
-        look_up_fd(second[0][:], 0, 0, 2)
-        nc.vector.tensor_tensor(x1[3][:], p1[3][:, 0:S:2], p1[3][:, 1:S:2], ADD)
-        nc.scalar.activation(out=z0_grouped[:, :, 3], in_=x1[3][:], func=COPY, scale=unit_sb[:, 3:4])
-        look_up_fd(second[3][:], 3, 0, 2)
-        look_up_fd(second[1][:], 1, 0, 2)
-        look_up_fd(second_last0[:], 2, 0, 1)
-        look_up_fd(second_last1[:], 2, 1, 2)
+        def look_up_fc(h, tag):
+            z1_rows = sb([P, PACK, HALF_V], F32, f"z1_rows{h}", tag)
+            for t in range(PACK):
+                nc.vector.tensor_tensor(
+                    z1_rows[:, t, :],
+                    x1[t][:].indirect(fc_sb[:, 8 * h : 8 * (h + 1)]),
+                    second[t][:, HALF_V * h : HALF_V * (h + 1)],
+                    MULT,
+                )
+            return z1_rows
 
-        def second_maps(h, z1):
-            for t in (3, 0, 1, 2):
-                other = (second_last0, second_last1)[h][:] if t == 2 else second[t][:, HALF_V * h : HALF_V * (h + 1)]
-                nc.vector.tensor_tensor(z1[:, t, :], x1[t][:].indirect(fc_sb[:, 8 * h : 8 * (h + 1)]), other, MULT)
-
-        out_acc = [psum.tile([P, HALF_V], F32, name=f"out_acc{h}", tag=f"bank{2 + h}") for h in range(2)]
-        result = [keep.tile([P, HALF_V], F32, name=f"result{h}", align_bytes=64) for h in range(2)]
-
-        def finish(h):
+        def finish(h, copy, queue):
             cols = slice(HALF_V * h, HALF_V * (h + 1))
-            nc.vector.quantize_mx(
-                out=z1_codes[h][:].bitcast(FP8X4),
-                scales=z1_planes[h][:],
-                in_=z1_grouped[h][:].rearrange("p v t -> p (v t)"),
-            )
+            quantize(z1_codes[h][:], z1_planes[h][:], z1_grouped[h][:].rearrange("p v j -> p (v j)"))
+            acc = bank(1 + h, [P, HALF_V], f"out_acc{h}")
             nc.tensor.matmul_mx(
-                out=out_acc[h][:],
+                out=acc[:],
                 lhsT=t_codes[:, :N].bitcast(FP8X4),
                 lhsT_scale=t_planes[:, :N],
-                rhs=z0_codes[:, cols].bitcast(FP8X4),
-                rhs_scale=z0_planes[:, cols],
+                rhs=z0_codes[h][:].bitcast(FP8X4),
+                rhs_scale=z0_planes[h][:],
                 start=True,
                 stop=False,
             )
             nc.tensor.matmul_mx(
-                out=out_acc[h][:],
+                out=acc[:],
                 lhsT=t_codes[:, N:].bitcast(FP8X4),
                 lhsT_scale=t_planes[:, N:],
                 rhs=z1_codes[h][:].bitcast(FP8X4),
@@ -238,24 +234,32 @@ def tile_picked_ycin_both_p_kernel(
                 start=False,
                 stop=True,
             )
-            if h == 0:
-                nc.scalar.copy(out=result[h][:], in_=out_acc[h][:])
-                nc.scalar.dma_start(out=out[:, cols], in_=result[h][:])
-            else:
-                nc.vector.tensor_copy(out=result[h][:], in_=out_acc[h][:])
-                nc.sync.dma_start(out=out[:, cols], in_=result[h][:])
+            copy(out=result[h][:], in_=acc[:])
+            queue.dma_start(out=out[:, cols], in_=result[h][:])
 
-        z1_low = keep.tile([P, PACK, HALF_V], F32, name="z1_low", align_bytes=64)
-        second_maps(0, z1_low)
-        nc.scalar.copy(out=z1_grouped[0][:], in_=z1_low[:].rearrange("p t v -> p v t"))
-        nc.vector.quantize_mx(
-            out=t_codes[:].bitcast(FP8X4), scales=t_planes[:], in_=t_grouped[:].rearrange("p d n j -> p (d n j)")
-        )
-        z1_high = keep.tile([P, PACK, HALF_V], F32, name="z1_high", tag="late", align_bytes=64)
-        second_maps(1, z1_high)
-        nc.vector.quantize_mx(
-            out=z0_codes[:].bitcast(FP8X4), scales=z0_planes[:], in_=z0_grouped[:].rearrange("p v t -> p (v t)")
-        )
-        nc.vector.tensor_copy(out=z1_grouped[1][:], in_=z1_high[:].rearrange("p t v -> p v t"))
-        finish(0)
-        finish(1)
+        for d in range(2):
+            interleave(nc.scalar.copy, t_grouped[:, d], t_raw[d][:])
+        for t in range(PACK):
+            nc.scalar.activation(out=m2u[t][:], in_=m2_sb[:], func=COPY, scale=unit_sb[:, t : t + 1])
+        look_up_fa(0)
+        look_up_fa(1)
+        look_up_fb(0, (0, 1), 5, 7)
+        look_up_fa(2)
+        look_up_fb(1, (0, 1), 6, 0)
+        look_up_fa(3)
+        look_up_fb(2, (0, 1), 5, 7)
+        look_up_fb(3, (0,), 6, 0)
+        look_up_fb(3, (1,), 3, 4)
+        for t in range(PACK):
+            look_up_fd(t)
+        for h in range(2):
+            interleave(nc.scalar.copy, z0_grouped[h][:], z0_rows[h][:])
+        z1_low = look_up_fc(0, None)
+        interleave(nc.scalar.copy, z1_grouped[0][:], z1_low[:])
+        quantize(t_codes[:], t_planes[:], t_grouped[:].rearrange("p d n j -> p (d n j)"))
+        z1_high = look_up_fc(1, "z0_rows1")
+        for h in range(2):
+            quantize(z0_codes[h][:], z0_planes[h][:], z0_grouped[h][:].rearrange("p v j -> p (v j)"))
+        interleave(nc.vector.tensor_copy, z1_grouped[1][:], z1_high[:])
+        finish(0, nc.scalar.copy, nc.scalar)
+        finish(1, nc.vector.tensor_copy, nc.sync)

@@ -22,7 +22,6 @@ PASSES = K // (P * PACK)
 SPARE = 16
 HALF_S = S // 2
 HALF_V = V // 2
-HALF_H = H // 2
 
 
 def tile_picked_ycin_both_p_kernel(
@@ -40,115 +39,125 @@ def tile_picked_ycin_both_p_kernel(
         def bank(b, shape, name):
             return psum.tile(shape, F32, name=name, tag=f"bank{b}")
 
+        def quantize(codes, planes, grouped):
+            nc.vector.quantize_mx(out=codes.bitcast(FP8X4), scales=planes, in_=grouped)
+
         offs_sb = lists.tile([P, S // 16], U16, name="offs_sb")
         fa_sb = lists.tile([P, S // 16], U16, name="fa_sb")
         fb_sb = lists.tile([P, S // 16], U16, name="fb_sb")
         fc_sb = lists.tile([P, V // 16], U16, name="fc_sb")
         fd_sb = lists.tile([P, V // 16], U16, name="fd_sb")
 
-        table_words = [sb([P, T], I32, f"table_words{o}") for o in range(PASSES)]
-        table_scales = sb([P, T], U8, "table_scales")
-        w_raw0 = sb([P, PACK, H], F32, "w_raw0")
-        w_raw1 = [sb([P, PACK, HALF_H], F32, f"w_raw1_{c}") for c in range(2)]
-        t_raw = [sb([P, PACK, N], F32, f"t_raw{d}") for d in range(2)]
-        m1_sb = sb([P, S], F32, "m1_sb")
-        m2_sb = sb([P, V], F32, "m2_sb")
-        unit_sb = sb([P, PACK], F32, "unit_sb")
-        y = [sb([P, S + SPARE], F32, f"y{t}") for t in range(PACK)]
-        identity = sb([P, P], F32, "identity")
+        table_words = [keep.tile([P, T], I32, name=f"table_words{o}", tag=f"table{o}", align_bytes=64) for o in range(PASSES)]
+        table_scales = keep.tile([P, T], U8, name="table_scales", align_bytes=64)
+        w_raw = [keep.tile([P, PACK, H], F32, name=f"w_raw{o}", align_bytes=64) for o in range(PASSES)]
+        t_raw = [keep.tile([P, PACK, N], F32, name=f"t_raw{d}", align_bytes=64) for d in range(2)]
+        m1_sb = keep.tile([P, S], F32, name="m1_sb", align_bytes=64)
+        m2_sb = keep.tile([P, V], F32, name="m2_sb", align_bytes=64)
+        unit_sb = keep.tile([P, PACK], F32, name="unit_sb", align_bytes=64)
+        y = [keep.tile([P, S + SPARE], F32, name=f"y{t}", align_bytes=64) for t in range(PACK)]
 
-        nc.gpsimd.memset(table_scales[:].bitcast(I32), 0)
-        make_identity(nc, identity[:])
+        nc.vector.memset(table_scales[:].bitcast(I32), 0)
         for t in range(PACK):
-            nc.gpsimd.memset(y[t][:, S:], 0.0)
+            nc.vector.memset(y[t][:, S:], 0.0)
 
         def load_words(o):
             nc.sync.dma_start(out=table_words[o][:], in_=x_words[o].rearrange("p c r -> p (c r)").bitcast(I32))
 
+        def load_w(o):
+            nc.sync.dma_start(out=w_raw[o][:], in_=w1[512 * o : 512 * (o + 1), :].rearrange("(p j) c -> p j c", j=PACK))
+
+        def load_scales(rows):
+            for r in rows:
+                for o in range(PASSES):
+                    nc.sync.dma_start(
+                        out=table_scales[4 * o + r : P : 32, :].bitcast(I32), in_=x_scales[o, r:16:4, :].bitcast(I32)
+                    )
+
         load_words(0)
         nc.sync.dma_start(offs_sb[:], offs)
-        for q in range(4):
-            nc.sync.dma_start(
-                out=table_scales[32 * q : 32 * q + 8, :].bitcast(I32), in_=x_scales[:, 4 * q : 4 * q + 4, :].bitcast(I32)
-            )
-        nc.sync.dma_start(out=w_raw0[:], in_=w1[:512, :].rearrange("(p j) c -> p j c", j=PACK))
+        load_scales((0, 1))
+        load_w(0)
+        load_scales((2, 3))
+        load_w(1)
         load_words(1)
-        for c in range(2):
-            nc.sync.dma_start(
-                out=w_raw1[c][:], in_=w1[512:, HALF_H * c : HALF_H * (c + 1)].rearrange("(p j) c -> p j c", j=PACK)
-            )
         nc.sync.dma_start(out=m1_sb[:], in_=m1)
         nc.sync.dma_start(fa_sb[:], fa)
         nc.sync.dma_start(fb_sb[:], fb)
-        for d, tm in enumerate((t1, t2)):
-            nc.sync.dma_start(out=t_raw[d][:], in_=tm.rearrange("(p j) n -> p j n", j=PACK))
         nc.sync.dma_start(out=unit_sb[:], in_=unit.rearrange("(p t) o -> p (t o)", t=PACK))
         nc.sync.dma_start(out=m2_sb[:], in_=m2)
         nc.sync.dma_start(fd_sb[:], fd)
         nc.sync.dma_start(fc_sb[:], fc)
+        for d, tm in enumerate((t1, t2)):
+            nc.sync.dma_start(out=t_raw[d][:], in_=tm.rearrange("(p j) n -> p j n", j=PACK))
 
-        x_codes = [sb([P, S], U32, f"x_codes{o}") for o in range(PASSES)]
-        x_planes = sb([P, S], U8, "x_planes")
-        w_grouped = {(o, u): sb([P, 2, P, PACK], BF16, f"w_grouped{o}_{u}") for o in range(PASSES) for u in range(2)}
+        x_codes0 = keep.tile([P, S], U32, name="x_codes0", align_bytes=64)
+        x_codes1 = keep.tile([P, S], U32, name="x_codes1", align_bytes=64)
+        x_planes = keep.tile([P, S], U8, name="x_planes", align_bytes=64)
+        w_grouped = {
+            (o, u): keep.tile([P, 2, P, PACK], BF16, name=f"w_grouped{o}_{u}", align_bytes=64)
+            for o in range(PASSES)
+            for u in range(2)
+        }
+
+        def cast_w(o):
+            src = w_raw[o][:].rearrange("p j (m t) -> p m t j", t=PACK)
+            nc.scalar.activation(out=w_grouped[o, 1][:].rearrange("p t m j -> p m t j"), in_=src[:, :, 2:4], func=COPY)
+            nc.vector.tensor_copy(out=w_grouped[o, 0][:].rearrange("p t m j -> p m t j"), in_=src[:, :, 0:2])
+
         w_mx = {}
 
-        def cast_w(o, raw, m0):
-            src = raw[:].rearrange("p j (m t) -> p m t j", t=PACK)
-            ms = slice(m0, m0 + src.shape[1])
-            nc.vector.tensor_copy(out=w_grouped[o, 0][:, :, ms].rearrange("p t m j -> p m t j"), in_=src[:, :, 0:2])
-            nc.scalar.copy(out=w_grouped[o, 1][:, :, ms].rearrange("p t m j -> p m t j"), in_=src[:, :, 2:4])
+        def quantize_w(o, u, tag):
+            codes = keep.tile([P, 2 * P], U32, name=f"w_codes{o}_{u}", tag=tag, align_bytes=64)
+            planes = keep.tile([P, 2 * P], U8, name=f"w_planes{o}_{u}", align_bytes=64)
+            nc.vector.quantize_mx(
+                out=codes[:].bitcast(FP8X4),
+                scales=planes[:],
+                in_=w_grouped[o, u][:].rearrange("p t m j -> p (t m j)"),
+            )
+            for i in range(2):
+                w_mx[o, 2 * u + i] = (codes[:, P * i : P * (i + 1)], planes[:, P * i : P * (i + 1)])
 
-        def quantize(codes, planes, grouped):
-            nc.vector.quantize_mx(out=codes.bitcast(FP8X4), scales=planes, in_=grouped)
-
-        def quantize_w(o, slots):
-            codes = sb([P, len(slots) * P], U32, f"w_codes{o}_{slots[0]}")
-            planes = sb([P, len(slots) * P], U8, f"w_planes{o}_{slots[0]}")
-            i0 = slots[0] % 2
-            grouped = w_grouped[o, slots[0] // 2][:, i0 : i0 + len(slots)]
-            quantize(codes[:], planes[:], grouped.rearrange("p t m j -> p (t m j)"))
-            for i, t in enumerate(slots):
-                w_mx[o, t] = (codes[:, P * i : P * (i + 1)], planes[:, P * i : P * (i + 1)])
-
-        pieces = [(0, slice(0, HALF_S)), (0, slice(HALF_S, S))] + [(t, slice(0, S)) for t in range(1, PACK)]
-        y_acc = [bank(b, [P, cols.stop - cols.start], f"y_acc{b}") for b, (t, cols) in enumerate(pieces)]
-
-        def products(o, slots):
-            for b, (t, cols) in enumerate(pieces):
-                if t in slots:
-                    nc.tensor.matmul_mx(
-                        out=y_acc[b][:],
-                        lhsT=w_mx[o, t][0].bitcast(FP8X4),
-                        lhsT_scale=w_mx[o, t][1],
-                        rhs=x_codes[o][:, cols].bitcast(FP8X4),
-                        rhs_scale=x_planes[4 * o : P, cols],
-                        start=(o == 0),
-                        stop=(o == PASSES - 1),
-                    )
-
-        nc.vector.tensor_copy(x_codes[0][:], table_words[0][:].bitcast(U32).indirect(offs_sb[:]))
+        nc.vector.tensor_copy(x_codes0[:], table_words[0][:].bitcast(U32).indirect(offs_sb[:]))
+        cast_w(0)
         nc.vector.tensor_copy(x_planes[:], table_scales[:].indirect(offs_sb[:]))
-        cast_w(0, w_raw0, 0)
-        quantize_w(0, (0, 1))
-        quantize_w(0, (2, 3))
-        products(0, range(PACK))
-        nc.vector.tensor_copy(x_codes[1][:], table_words[1][:].bitcast(U32).indirect(offs_sb[:]))
-        for c in range(2):
-            cast_w(1, w_raw1[c], P // 2 * c)
-        for slots in ((0,), (1,), (2, 3)):
-            quantize_w(1, slots)
-            products(1, slots)
-        for b, (t, cols) in enumerate(pieces):
-            copy = nc.vector.tensor_copy if b == 1 else nc.scalar.copy
-            copy(out=y[t][:, cols], in_=y_acc[b][:])
+        quantize_w(0, 0, "w_codes00")
+        cast_w(1)
+        quantize_w(0, 1, "w_codes01")
+        quantize_w(1, 0, "w_codes10")
+        for h in range(2):
+            nc.vector.tensor_copy(
+                x_codes1[:, HALF_S * h : HALF_S * (h + 1)], table_words[1][:].bitcast(U32).indirect(offs_sb[:, 16 * h : 16 * (h + 1)])
+            )
 
+        quantize_w(1, 1, "table1")
+        x_codes = (x_codes0, x_codes1)
+        pieces = [(t, slice(HALF_S * h, HALF_S * (h + 1))) for h in range(2) for t in (0, 1)]
+        pieces = pieces + [(t, slice(0, S)) for t in (2, 3)]
+        y_acc = [psum.tile([P, cols.stop - cols.start], F32, name=f"y_acc{b}", tag=f"bank{b}") for b, (t, cols) in enumerate(pieces)]
+        for o in range(PASSES):
+            for b, (t, cols) in enumerate(pieces):
+                nc.tensor.matmul_mx(
+                    out=y_acc[b][:],
+                    lhsT=w_mx[o, t][0].bitcast(FP8X4),
+                    lhsT_scale=w_mx[o, t][1],
+                    rhs=x_codes[o][:, cols].bitcast(FP8X4),
+                    rhs_scale=x_planes[4 * o : P, cols],
+                    start=(o == 0),
+                    stop=(o == PASSES - 1),
+                )
+        for b, (t, cols) in enumerate(pieces):
+            nc.scalar.copy(out=y[t][:, cols], in_=y_acc[b][:])
+
+        identity = keep.tile([P, P], F32, name="identity", tag="table0", align_bytes=64)
+        make_identity(nc, identity[:])
         first = [sb([P, S], F32, f"first{t}") for t in range(PACK)]
         x1 = [sb([P, V], F32, f"x1_{t}") for t in range(PACK)]
         m2u = [sb([P, V], F32, f"m2u{t}") for t in range(PACK)]
         z0_rows = [sb([P, PACK, HALF_V], BF16, f"z0_rows{h}") for h in range(2)]
         z0_grouped = [sb([P, HALF_V, PACK], BF16, f"z0_grouped{h}") for h in range(2)]
         z1_grouped = [sb([P, HALF_V, PACK], BF16, f"z1_grouped{h}") for h in range(2)]
-        t_grouped = sb([P, 2, N, PACK], BF16, "t_grouped", "w_codes1_2")
+        t_grouped = sb([P, 2, N, PACK], BF16, "t_grouped")
         t_codes = sb([P, 2 * N], U32, "t_codes")
         t_planes = sb([P, 2 * N], U8, "t_planes")
         z0_codes = [sb([P, HALF_V], U32, f"z0_codes{h}") for h in range(2)]
@@ -160,7 +169,7 @@ def tile_picked_ycin_both_p_kernel(
         p1 = {}
 
         def interleave(copy, dst, src):
-            copy(out=dst.rearrange("p (c i) j -> p c j i", i=4), in_=src.rearrange("p j (c i) -> p c j i", i=4))
+            copy(out=dst, in_=src.rearrange("p j c -> p c j"))
 
         def look_up_fa(t):
             nc.vector.tensor_tensor(first[t][:], y[t][:].indirect(fa_sb[:]), m1_sb[:], MULT)
@@ -215,7 +224,7 @@ def tile_picked_ycin_both_p_kernel(
         def finish(h, copy, queue):
             cols = slice(HALF_V * h, HALF_V * (h + 1))
             quantize(z1_codes[h][:], z1_planes[h][:], z1_grouped[h][:].rearrange("p v j -> p (v j)"))
-            acc = bank(1 + h, [P, HALF_V], f"out_acc{h}")
+            acc = bank(4 + h, [P, HALF_V], f"out_acc{h}")
             nc.tensor.matmul_mx(
                 out=acc[:],
                 lhsT=t_codes[:, :N].bitcast(FP8X4),
@@ -237,19 +246,19 @@ def tile_picked_ycin_both_p_kernel(
             copy(out=result[h][:], in_=acc[:])
             queue.dma_start(out=out[:, cols], in_=result[h][:])
 
-        for d in range(2):
-            interleave(nc.scalar.copy, t_grouped[:, d], t_raw[d][:])
         for t in range(PACK):
             nc.scalar.activation(out=m2u[t][:], in_=m2_sb[:], func=COPY, scale=unit_sb[:, t : t + 1])
+        for d in range(2):
+            interleave(nc.scalar.copy, t_grouped[:, d], t_raw[d][:])
         look_up_fa(0)
         look_up_fa(1)
-        look_up_fb(0, (0, 1), 5, 7)
+        look_up_fb(0, (0, 1), 6, 7)
         look_up_fa(2)
-        look_up_fb(1, (0, 1), 6, 0)
+        look_up_fb(1, (0, 1), 0, 1)
         look_up_fa(3)
-        look_up_fb(2, (0, 1), 5, 7)
-        look_up_fb(3, (0,), 6, 0)
-        look_up_fb(3, (1,), 3, 4)
+        look_up_fb(2, (0, 1), 6, 7)
+        look_up_fb(3, (0,), 0, 1)
+        look_up_fb(3, (1,), 2, 3)
         for t in range(PACK):
             look_up_fd(t)
         for h in range(2):

@@ -48,16 +48,16 @@ def tile_picked_ycin_both_p_kernel(
         fc_sb = lists.tile([P, V // 16], U16, name="fc_sb")
         fd_sb = lists.tile([P, V // 16], U16, name="fd_sb")
 
-        table_words = [keep.tile([P, T], I32, name=f"table_words{o}", tag=f"table{o}", align_bytes=64) for o in range(PASSES)]
+        table_words = {0: sb([P, T], I32, "table_words0", "table0")}
         table_scales = keep.tile([P, T], U8, name="table_scales", align_bytes=64)
-        w_raw = [keep.tile([P, PACK, H], F32, name=f"w_raw{o}", align_bytes=64) for o in range(PASSES)]
-        t_raw = [keep.tile([P, PACK, N], F32, name=f"t_raw{d}", align_bytes=64) for d in range(2)]
-        m1_sb = keep.tile([P, S], F32, name="m1_sb", align_bytes=64)
-        m2_sb = keep.tile([P, V], F32, name="m2_sb", align_bytes=64)
-        unit_sb = keep.tile([P, PACK], F32, name="unit_sb", align_bytes=64)
+        w_raw = [sb([P, PACK, H], F32, f"w_raw{o}") for o in range(PASSES)]
+        picked_scales = sb([P, S], U8, "picked_scales")
+        x_planes = [sb([P, S], U8, f"x_planes{o}") for o in range(PASSES)]
         y = [keep.tile([P, S + SPARE], F32, name=f"y{t}", align_bytes=64) for t in range(PACK)]
 
         nc.vector.memset(table_scales[:].bitcast(I32), 0)
+        for o in range(PASSES):
+            nc.vector.memset(x_planes[o][:].bitcast(I32), 0)
         for t in range(PACK):
             nc.vector.memset(y[t][:, S:], 0.0)
 
@@ -67,33 +67,35 @@ def tile_picked_ycin_both_p_kernel(
         def load_w(o):
             nc.sync.dma_start(out=w_raw[o][:], in_=w1[512 * o : 512 * (o + 1), :].rearrange("(p j) c -> p j c", j=PACK))
 
-        def load_scales(rows):
-            for r in rows:
-                for o in range(PASSES):
-                    nc.sync.dma_start(
-                        out=table_scales[4 * o + r : P : 32, :].bitcast(I32), in_=x_scales[o, r:16:4, :].bitcast(I32)
-                    )
+        def move_scales(o, r):
+            nc.sync.dma_start(
+                out=x_planes[o][4 * o + r : P : 32, :].bitcast(I32),
+                in_=picked_scales[64 * o + 4 * r : 64 * (o + 1) : 16, :].bitcast(I32),
+            )
 
         load_words(0)
         nc.sync.dma_start(offs_sb[:], offs)
-        load_scales((0, 1))
-        load_w(0)
-        load_scales((2, 3))
-        load_w(1)
-        load_words(1)
-        nc.sync.dma_start(out=m1_sb[:], in_=m1)
+        nc.sync.dma_start(
+            out=table_scales[0:P:4, :].bitcast(I32), in_=x_scales.rearrange("o q c -> (o q) c").bitcast(I32)
+        )
         nc.sync.dma_start(fa_sb[:], fa)
         nc.sync.dma_start(fb_sb[:], fb)
-        nc.sync.dma_start(out=unit_sb[:], in_=unit.rearrange("(p t) o -> p (t o)", t=PACK))
-        nc.sync.dma_start(out=m2_sb[:], in_=m2)
         nc.sync.dma_start(fd_sb[:], fd)
         nc.sync.dma_start(fc_sb[:], fc)
-        for d, tm in enumerate((t1, t2)):
-            nc.sync.dma_start(out=t_raw[d][:], in_=tm.rearrange("(p j) n -> p j n", j=PACK))
+        load_w(0)
+        load_w(1)
 
         x_codes0 = keep.tile([P, S], U32, name="x_codes0", align_bytes=64)
         x_codes1 = keep.tile([P, S], U32, name="x_codes1", align_bytes=64)
-        x_planes = keep.tile([P, S], U8, name="x_planes", align_bytes=64)
+        nc.vector.tensor_copy(picked_scales[:], table_scales[:].indirect(offs_sb[:]))
+        nc.vector.tensor_copy(x_codes0[:], table_words[0][:].bitcast(U32).indirect(offs_sb[:]))
+        rows = [(o, r) for o in range(PASSES) for r in range(4)]
+        for o, r in rows[:6]:
+            move_scales(o, r)
+        table_words[1] = sb([P, T], I32, "table_words1", "table_scales")
+        load_words(1)
+        for o, r in rows[6:]:
+            move_scales(o, r)
         w_grouped = {
             (o, u): keep.tile([P, 2, P, PACK], BF16, name=f"w_grouped{o}_{u}", align_bytes=64)
             for o in range(PASSES)
@@ -118,19 +120,26 @@ def tile_picked_ycin_both_p_kernel(
             for i in range(2):
                 w_mx[o, 2 * u + i] = (codes[:, P * i : P * (i + 1)], planes[:, P * i : P * (i + 1)])
 
-        nc.vector.tensor_copy(x_codes0[:], table_words[0][:].bitcast(U32).indirect(offs_sb[:]))
         cast_w(0)
-        nc.vector.tensor_copy(x_planes[:], table_scales[:].indirect(offs_sb[:]))
         quantize_w(0, 0, "w_codes00")
         cast_w(1)
         quantize_w(0, 1, "w_codes01")
         quantize_w(1, 0, "w_codes10")
+        m1_sb = sb([P, S], F32, "m1_sb", "w_raw0")
+        nc.sync.dma_start(out=m1_sb[:], in_=m1)
+        unit_sb = sb([P, PACK], F32, "unit_sb", "w_grouped0_0")
+        nc.sync.dma_start(out=unit_sb[:], in_=unit.rearrange("(p t) o -> p (t o)", t=PACK))
+        m2_sb = sb([P, V], F32, "m2_sb", "w_grouped0_1")
+        nc.sync.dma_start(out=m2_sb[:], in_=m2)
+        t_raw = [sb([P, PACK, N], F32, f"t_raw{d}", ("w_raw1", "w_grouped1_0")[d]) for d in range(2)]
+        for d, tm in enumerate((t1, t2)):
+            nc.sync.dma_start(out=t_raw[d][:], in_=tm.rearrange("(p j) n -> p j n", j=PACK))
         for h in range(2):
             nc.vector.tensor_copy(
                 x_codes1[:, HALF_S * h : HALF_S * (h + 1)], table_words[1][:].bitcast(U32).indirect(offs_sb[:, 16 * h : 16 * (h + 1)])
             )
 
-        quantize_w(1, 1, "table1")
+        quantize_w(1, 1, "table_scales")
         x_codes = (x_codes0, x_codes1)
         pieces = [(t, slice(HALF_S * h, HALF_S * (h + 1))) for h in range(2) for t in (0, 1)]
         pieces = pieces + [(t, slice(0, S)) for t in (2, 3)]
@@ -142,14 +151,14 @@ def tile_picked_ycin_both_p_kernel(
                     lhsT=w_mx[o, t][0].bitcast(FP8X4),
                     lhsT_scale=w_mx[o, t][1],
                     rhs=x_codes[o][:, cols].bitcast(FP8X4),
-                    rhs_scale=x_planes[4 * o : P, cols],
+                    rhs_scale=x_planes[o][4 * o : P, cols],
                     start=(o == 0),
                     stop=(o == PASSES - 1),
                 )
         for b, (t, cols) in enumerate(pieces):
             nc.scalar.copy(out=y[t][:, cols], in_=y_acc[b][:])
 
-        identity = keep.tile([P, P], F32, name="identity", tag="table0", align_bytes=64)
+        identity = sb([P, P], F32, "identity")
         make_identity(nc, identity[:])
         first = [sb([P, S], F32, f"first{t}") for t in range(PACK)]
         x1 = [sb([P, V], F32, f"x1_{t}") for t in range(PACK)]

@@ -39,33 +39,30 @@ def tile_picked_ycin_both_p_kernel(
         def bank(b, shape, name):
             return psum.tile(shape, F32, name=name, tag=f"bank{b}")
 
-        def quantize(codes, planes, grouped):
-            nc.vector.quantize_mx(out=codes.bitcast(FP8X4), scales=planes, in_=grouped)
-
         offs_sb = lists.tile([P, S // 16], U16, name="offs_sb")
         fa_sb = lists.tile([P, S // 16], U16, name="fa_sb")
         fb_sb = lists.tile([P, S // 16], U16, name="fb_sb")
         fc_sb = lists.tile([P, V // 16], U16, name="fc_sb")
         fd_sb = lists.tile([P, V // 16], U16, name="fd_sb")
 
-        table_words = {0: sb([P, T], I32, "table_words0", "table0")}
-        table_scales = keep.tile([P, T], U8, name="table_scales", align_bytes=64)
-        w_raw = [sb([P, PACK, H], F32, f"w_raw{o}") for o in range(PASSES)]
+        table_words = [sb([P, T], I32, f"table_words{o}") for o in range(PASSES)]
+        table_scales = sb([P, T], U8, "table_scales")
         picked_scales = sb([P, S], U8, "picked_scales")
         x_planes = [sb([P, S], U8, f"x_planes{o}") for o in range(PASSES)]
-        y = [keep.tile([P, S + SPARE], F32, name=f"y{t}", align_bytes=64) for t in range(PACK)]
+        x_codes = [sb([P, S], U32, f"x_codes{o}") for o in range(PASSES)]
+        w_raw0 = sb([P, PACK, H], F32, "w_raw0")
+        y = [sb([P, S + SPARE], F32, f"y{t}") for t in range(PACK)]
+        identity = sb([P, P], F32, "identity")
 
         nc.vector.memset(table_scales[:].bitcast(I32), 0)
         for o in range(PASSES):
             nc.vector.memset(x_planes[o][:].bitcast(I32), 0)
         for t in range(PACK):
             nc.vector.memset(y[t][:, S:], 0.0)
+        make_identity(nc, identity[:])
 
         def load_words(o):
             nc.sync.dma_start(out=table_words[o][:], in_=x_words[o].rearrange("p c r -> p (c r)").bitcast(I32))
-
-        def load_w(o):
-            nc.sync.dma_start(out=w_raw[o][:], in_=w1[512 * o : 512 * (o + 1), :].rearrange("(p j) c -> p j c", j=PACK))
 
         def move_scales(o, r):
             nc.sync.dma_start(
@@ -74,99 +71,93 @@ def tile_picked_ycin_both_p_kernel(
             )
 
         load_words(0)
-        nc.sync.dma_start(offs_sb[:], offs)
         nc.sync.dma_start(
             out=table_scales[0:P:4, :].bitcast(I32), in_=x_scales.rearrange("o q c -> (o q) c").bitcast(I32)
         )
+        nc.sync.dma_start(offs_sb[:], offs)
         nc.sync.dma_start(fa_sb[:], fa)
         nc.sync.dma_start(fb_sb[:], fb)
         nc.sync.dma_start(fd_sb[:], fd)
-        nc.sync.dma_start(fc_sb[:], fc)
-        load_w(0)
-        load_w(1)
-
-        x_codes0 = keep.tile([P, S], U32, name="x_codes0", align_bytes=64)
-        x_codes1 = keep.tile([P, S], U32, name="x_codes1", align_bytes=64)
-        nc.vector.tensor_copy(picked_scales[:], table_scales[:].indirect(offs_sb[:]))
-        nc.vector.tensor_copy(x_codes0[:], table_words[0][:].bitcast(U32).indirect(offs_sb[:]))
-        rows = [(o, r) for o in range(PASSES) for r in range(4)]
-        for o, r in rows[:6]:
-            move_scales(o, r)
-        table_words[1] = sb([P, T], I32, "table_words1", "table_scales")
+        nc.sync.dma_start(out=w_raw0[:], in_=w1[:512, :].rearrange("(p j) c -> p j c", j=PACK))
         load_words(1)
-        for o, r in rows[6:]:
+        nc.sync.dma_start(fc_sb[:], fc)
+
+        nc.vector.tensor_copy(picked_scales[:], table_scales[:].indirect(offs_sb[:]))
+        nc.vector.tensor_copy(x_codes[0][:], table_words[0][:].bitcast(U32).indirect(offs_sb[:]))
+        rows = [(o, r) for o in range(PASSES) for r in range(4)]
+        for o, r in rows[:4]:
             move_scales(o, r)
-        w_grouped = {
-            (o, u): keep.tile([P, 2, P, PACK], BF16, name=f"w_grouped{o}_{u}", align_bytes=64)
-            for o in range(PASSES)
-            for u in range(2)
-        }
+        w_raw1 = sb([P, PACK, H], F32, "w_raw1", "table_scales")
+        nc.sync.dma_start(out=w_raw1[:], in_=w1[512:, :].rearrange("(p j) c -> p j c", j=PACK))
+        for o, r in rows[4:]:
+            move_scales(o, r)
 
-        def cast_w(o):
-            src = w_raw[o][:].rearrange("p j (m t) -> p m t j", t=PACK)
-            nc.scalar.activation(out=w_grouped[o, 1][:].rearrange("p t m j -> p m t j"), in_=src[:, :, 2:4], func=COPY)
-            nc.vector.tensor_copy(out=w_grouped[o, 0][:].rearrange("p t m j -> p m t j"), in_=src[:, :, 0:2])
-
+        w_grouped = {(o, u): sb([P, 2, P, PACK], BF16, f"w_grouped{o}_{u}") for o in range(PASSES) for u in range(2)}
         w_mx = {}
 
-        def quantize_w(o, u, tag):
-            codes = keep.tile([P, 2 * P], U32, name=f"w_codes{o}_{u}", tag=tag, align_bytes=64)
-            planes = keep.tile([P, 2 * P], U8, name=f"w_planes{o}_{u}", align_bytes=64)
-            nc.vector.quantize_mx(
-                out=codes[:].bitcast(FP8X4),
-                scales=planes[:],
-                in_=w_grouped[o, u][:].rearrange("p t m j -> p (t m j)"),
-            )
-            for i in range(2):
-                w_mx[o, 2 * u + i] = (codes[:, P * i : P * (i + 1)], planes[:, P * i : P * (i + 1)])
+        def cast_w(o, raw, m0):
+            src = raw[:].rearrange("p j (m t) -> p m t j", t=PACK)
+            ms = slice(m0, m0 + src.shape[1])
+            nc.vector.tensor_copy(out=w_grouped[o, 0][:, :, ms].rearrange("p t m j -> p m t j"), in_=src[:, :, 0:2])
+            nc.scalar.copy(out=w_grouped[o, 1][:, :, ms].rearrange("p t m j -> p m t j"), in_=src[:, :, 2:4])
 
-        cast_w(0)
-        quantize_w(0, 0, "w_codes00")
-        cast_w(1)
-        quantize_w(0, 1, "w_codes01")
-        quantize_w(1, 0, "w_codes10")
+        def quantize(codes, planes, grouped):
+            nc.vector.quantize_mx(out=codes.bitcast(FP8X4), scales=planes, in_=grouped)
+
+        def quantize_w(o, slots):
+            codes = sb([P, len(slots) * P], U32, f"w_codes{o}_{slots[0]}")
+            planes = sb([P, len(slots) * P], U8, f"w_planes{o}_{slots[0]}")
+            i0 = slots[0] % 2
+            grouped = w_grouped[o, slots[0] // 2][:, i0 : i0 + len(slots)]
+            quantize(codes[:], planes[:], grouped.rearrange("p t m j -> p (t m j)"))
+            for i, t in enumerate(slots):
+                w_mx[o, t] = (codes[:, P * i : P * (i + 1)], planes[:, P * i : P * (i + 1)])
+
+        pieces = [(0, slice(0, HALF_S)), (0, slice(HALF_S, S))] + [(t, slice(0, S)) for t in range(1, PACK)]
+        y_acc = [bank(b, [P, cols.stop - cols.start], f"y_acc{b}") for b, (t, cols) in enumerate(pieces)]
+
+        def products(o, slots):
+            for b, (t, cols) in enumerate(pieces):
+                if t in slots:
+                    nc.tensor.matmul_mx(
+                        out=y_acc[b][:],
+                        lhsT=w_mx[o, t][0].bitcast(FP8X4),
+                        lhsT_scale=w_mx[o, t][1],
+                        rhs=x_codes[o][:, cols].bitcast(FP8X4),
+                        rhs_scale=x_planes[o][4 * o : P, cols],
+                        start=(o == 0),
+                        stop=(o == PASSES - 1),
+                    )
+
+        cast_w(0, w_raw0, 0)
+        quantize_w(0, (0, 1))
+        quantize_w(0, (2, 3))
+        products(0, range(PACK))
         m1_sb = sb([P, S], F32, "m1_sb", "w_raw0")
         nc.sync.dma_start(out=m1_sb[:], in_=m1)
         unit_sb = sb([P, PACK], F32, "unit_sb", "w_grouped0_0")
         nc.sync.dma_start(out=unit_sb[:], in_=unit.rearrange("(p t) o -> p (t o)", t=PACK))
         m2_sb = sb([P, V], F32, "m2_sb", "w_grouped0_1")
         nc.sync.dma_start(out=m2_sb[:], in_=m2)
-        t_raw = [sb([P, PACK, N], F32, f"t_raw{d}", ("w_raw1", "w_grouped1_0")[d]) for d in range(2)]
+        nc.vector.tensor_copy(x_codes[1][:], table_words[1][:].bitcast(U32).indirect(offs_sb[:]))
+        t_raw = [sb([P, PACK, N], F32, f"t_raw{d}", ("table_words1", "picked_scales")[d]) for d in range(2)]
         for d, tm in enumerate((t1, t2)):
             nc.sync.dma_start(out=t_raw[d][:], in_=tm.rearrange("(p j) n -> p j n", j=PACK))
-        for h in range(2):
-            nc.vector.tensor_copy(
-                x_codes1[:, HALF_S * h : HALF_S * (h + 1)], table_words[1][:].bitcast(U32).indirect(offs_sb[:, 16 * h : 16 * (h + 1)])
-            )
-
-        quantize_w(1, 1, "table_scales")
-        x_codes = (x_codes0, x_codes1)
-        pieces = [(t, slice(HALF_S * h, HALF_S * (h + 1))) for h in range(2) for t in (0, 1)]
-        pieces = pieces + [(t, slice(0, S)) for t in (2, 3)]
-        y_acc = [psum.tile([P, cols.stop - cols.start], F32, name=f"y_acc{b}", tag=f"bank{b}") for b, (t, cols) in enumerate(pieces)]
-        for o in range(PASSES):
-            for b, (t, cols) in enumerate(pieces):
-                nc.tensor.matmul_mx(
-                    out=y_acc[b][:],
-                    lhsT=w_mx[o, t][0].bitcast(FP8X4),
-                    lhsT_scale=w_mx[o, t][1],
-                    rhs=x_codes[o][:, cols].bitcast(FP8X4),
-                    rhs_scale=x_planes[o][4 * o : P, cols],
-                    start=(o == 0),
-                    stop=(o == PASSES - 1),
-                )
+        cast_w(1, w_raw1, 0)
+        for slots in ((0,), (1,), (2, 3)):
+            quantize_w(1, slots)
+            products(1, slots)
         for b, (t, cols) in enumerate(pieces):
-            nc.scalar.copy(out=y[t][:, cols], in_=y_acc[b][:])
+            copy = nc.vector.tensor_copy if b == 0 else nc.scalar.copy
+            copy(out=y[t][:, cols], in_=y_acc[b][:])
 
-        identity = sb([P, P], F32, "identity")
-        make_identity(nc, identity[:])
         first = [sb([P, S], F32, f"first{t}") for t in range(PACK)]
         x1 = [sb([P, V], F32, f"x1_{t}") for t in range(PACK)]
-        m2u = [sb([P, V], F32, f"m2u{t}") for t in range(PACK)]
+        m2u = [sb([P, V], F32, f"m2u{t}", ("w_codes1_1", "w_planes1_1", "w_planes1_2", "x_planes1")[t]) for t in range(PACK)]
         z0_rows = [sb([P, PACK, HALF_V], BF16, f"z0_rows{h}") for h in range(2)]
         z0_grouped = [sb([P, HALF_V, PACK], BF16, f"z0_grouped{h}") for h in range(2)]
         z1_grouped = [sb([P, HALF_V, PACK], BF16, f"z1_grouped{h}") for h in range(2)]
-        t_grouped = sb([P, 2, N, PACK], BF16, "t_grouped")
+        t_grouped = sb([P, 2, N, PACK], BF16, "t_grouped", "w_codes1_2")
         t_codes = sb([P, 2 * N], U32, "t_codes")
         t_planes = sb([P, 2 * N], U8, "t_planes")
         z0_codes = [sb([P, HALF_V], U32, f"z0_codes{h}") for h in range(2)]
@@ -233,7 +224,7 @@ def tile_picked_ycin_both_p_kernel(
         def finish(h, copy, queue):
             cols = slice(HALF_V * h, HALF_V * (h + 1))
             quantize(z1_codes[h][:], z1_planes[h][:], z1_grouped[h][:].rearrange("p v j -> p (v j)"))
-            acc = bank(4 + h, [P, HALF_V], f"out_acc{h}")
+            acc = bank(1 + h, [P, HALF_V], f"out_acc{h}")
             nc.tensor.matmul_mx(
                 out=acc[:],
                 lhsT=t_codes[:, :N].bitcast(FP8X4),
@@ -255,19 +246,19 @@ def tile_picked_ycin_both_p_kernel(
             copy(out=result[h][:], in_=acc[:])
             queue.dma_start(out=out[:, cols], in_=result[h][:])
 
-        for t in range(PACK):
-            nc.scalar.activation(out=m2u[t][:], in_=m2_sb[:], func=COPY, scale=unit_sb[:, t : t + 1])
         for d in range(2):
             interleave(nc.scalar.copy, t_grouped[:, d], t_raw[d][:])
+        for t in range(PACK):
+            nc.scalar.activation(out=m2u[t][:], in_=m2_sb[:], func=COPY, scale=unit_sb[:, t : t + 1])
         look_up_fa(0)
         look_up_fa(1)
-        look_up_fb(0, (0, 1), 6, 7)
+        look_up_fb(0, (0, 1), 5, 7)
         look_up_fa(2)
-        look_up_fb(1, (0, 1), 0, 1)
+        look_up_fb(1, (0, 1), 6, 0)
         look_up_fa(3)
-        look_up_fb(2, (0, 1), 6, 7)
-        look_up_fb(3, (0,), 0, 1)
-        look_up_fb(3, (1,), 2, 3)
+        look_up_fb(2, (0, 1), 5, 7)
+        look_up_fb(3, (0,), 6, 0)
+        look_up_fb(3, (1,), 3, 4)
         for t in range(PACK):
             look_up_fd(t)
         for h in range(2):

@@ -52,6 +52,7 @@ def tile_picked_ycin_both_p_kernel(
         x_codes = [sb([P, S], U32, f"x_codes{o}") for o in range(PASSES)]
         w_raw0 = sb([P, PACK, H], F32, "w_raw0")
         y = [sb([P, S + SPARE], F32, f"y{t}") for t in range(PACK)]
+        x1 = [sb([P, V + SPARE], F32, f"x1_{t}") for t in range(PACK)]
         identity = sb([P, P], F32, "identity")
 
         nc.vector.memset(table_scales[:].bitcast(I32), 0)
@@ -59,6 +60,7 @@ def tile_picked_ycin_both_p_kernel(
             nc.vector.memset(x_planes[o][:].bitcast(I32), 0)
         for t in range(PACK):
             nc.vector.memset(y[t][:, S:], 0.0)
+            nc.vector.memset(x1[t][:, V:], 0.0)
         make_identity(nc, identity[:])
 
         def load_words(o):
@@ -152,20 +154,18 @@ def tile_picked_ycin_both_p_kernel(
             copy(out=y[t][:, cols], in_=y_acc[b][:])
 
         first = [sb([P, S], F32, f"first{t}") for t in range(PACK)]
-        x1 = [sb([P, V], F32, f"x1_{t}") for t in range(PACK)]
         m2u = [sb([P, V], F32, f"m2u{t}", ("w_codes1_1", "w_planes1_1", "w_planes1_2", "x_planes1")[t]) for t in range(PACK)]
         z0_rows = [sb([P, PACK, HALF_V], BF16, f"z0_rows{h}") for h in range(2)]
         z0_grouped = [sb([P, HALF_V, PACK], BF16, f"z0_grouped{h}") for h in range(2)]
         z1_grouped = [sb([P, HALF_V, PACK], BF16, f"z1_grouped{h}") for h in range(2)]
         t_grouped = sb([P, 2, N, PACK], BF16, "t_grouped", "w_codes1_2")
-        t_codes = sb([P, 2 * N], U32, "t_codes")
         t_planes = sb([P, 2 * N], U8, "t_planes")
-        z0_codes = [sb([P, HALF_V], U32, f"z0_codes{h}") for h in range(2)]
         z0_planes = [sb([P, HALF_V], U8, f"z0_planes{h}") for h in range(2)]
         z1_codes = [sb([P, HALF_V], U32, f"z1_codes{h}") for h in range(2)]
         z1_planes = [sb([P, HALF_V], U8, f"z1_planes{h}") for h in range(2)]
         result = [sb([P, HALF_V], F32, f"result{h}") for h in range(2)]
-        second = [sb([P, V], F32, f"second{t}") for t in range(PACK)]
+        z1_rows = sb([P, PACK, V], F32, "z1_rows")
+        second = {}
         p1 = {}
 
         def interleave(copy, dst, src):
@@ -207,23 +207,27 @@ def tile_picked_ycin_both_p_kernel(
             for i, h in enumerate(halves):
                 nc.scalar.activation(out=z0_rows[h][:, t, :], in_=back[:, i, :], func=COPY, scale=unit_sb[:, t : t + 1])
 
-        def look_up_fd(t):
-            nc.vector.tensor_tensor(second[t][:], y[t][:].indirect(fd_sb[:]), m2u[t][:], MULT)
+        def look_up_fd(t, halves):
+            cols = slice(HALF_V * halves[0], HALF_V * (halves[-1] + 1))
+            second[t, halves[0]] = sb([P, cols.stop - cols.start], F32, f"second{t}_{halves[0]}")
+            nc.vector.tensor_tensor(
+                second[t, halves[0]][:],
+                y[t][:].indirect(fd_sb[:, cols.start // 16 : cols.stop // 16]),
+                m2u[t][:, cols],
+                MULT,
+            )
 
-        def look_up_fc(h, tag):
-            z1_rows = sb([P, PACK, HALF_V], F32, f"z1_rows{h}", tag)
-            for t in range(PACK):
-                nc.vector.tensor_tensor(
-                    z1_rows[:, t, :],
-                    x1[t][:].indirect(fc_sb[:, 8 * h : 8 * (h + 1)]),
-                    second[t][:, HALF_V * h : HALF_V * (h + 1)],
-                    MULT,
-                )
-            return z1_rows
+        def look_up_fc(t, halves):
+            cols = slice(HALF_V * halves[0], HALF_V * (halves[-1] + 1))
+            nc.vector.tensor_tensor(
+                z1_rows[:, t, cols],
+                x1[t][:].indirect(fc_sb[:, cols.start // 16 : cols.stop // 16]),
+                second[t, halves[0]][:],
+                MULT,
+            )
 
         def finish(h, copy, queue):
             cols = slice(HALF_V * h, HALF_V * (h + 1))
-            quantize(z1_codes[h][:], z1_planes[h][:], z1_grouped[h][:].rearrange("p v j -> p (v j)"))
             acc = bank(1 + h, [P, HALF_V], f"out_acc{h}")
             nc.tensor.matmul_mx(
                 out=acc[:],
@@ -259,16 +263,24 @@ def tile_picked_ycin_both_p_kernel(
         look_up_fb(2, (0, 1), 5, 7)
         look_up_fb(3, (0,), 6, 0)
         look_up_fb(3, (1,), 3, 4)
-        for t in range(PACK):
-            look_up_fd(t)
+        for t in range(PACK - 1):
+            look_up_fd(t, (0, 1))
+        for h in range(2):
+            look_up_fd(PACK - 1, (h,))
         for h in range(2):
             interleave(nc.scalar.copy, z0_grouped[h][:], z0_rows[h][:])
-        z1_low = look_up_fc(0, None)
-        interleave(nc.scalar.copy, z1_grouped[0][:], z1_low[:])
-        quantize(t_codes[:], t_planes[:], t_grouped[:].rearrange("p d n j -> p (d n j)"))
-        z1_high = look_up_fc(1, "z0_rows1")
+        for t in range(PACK - 1):
+            look_up_fc(t, (0, 1))
         for h in range(2):
-            quantize(z0_codes[h][:], z0_planes[h][:], z0_grouped[h][:].rearrange("p v j -> p (v j)"))
-        interleave(nc.vector.tensor_copy, z1_grouped[1][:], z1_high[:])
-        finish(0, nc.scalar.copy, nc.scalar)
+            look_up_fc(PACK - 1, (h,))
+        interleave(nc.scalar.copy, z1_grouped[0][:], z1_rows[:, :, :HALF_V])
+        t_codes = sb([P, 2 * N], U32, "t_codes", "second3_0")
+        quantize(t_codes[:], t_planes[:], t_grouped[:].rearrange("p d n j -> p (d n j)"))
+        interleave(nc.vector.tensor_copy, z1_grouped[1][:], z1_rows[:, :, HALF_V:])
+        z0_codes = [sb([P, HALF_V], U32, f"z0_codes{h}", ("second3_1", None)[h]) for h in range(2)]
+        quantize(z0_codes[0][:], z0_planes[0][:], z0_grouped[0][:].rearrange("p v j -> p (v j)"))
+        quantize(z1_codes[1][:], z1_planes[1][:], z1_grouped[1][:].rearrange("p v j -> p (v j)"))
+        quantize(z0_codes[1][:], z0_planes[1][:], z0_grouped[1][:].rearrange("p v j -> p (v j)"))
+        quantize(z1_codes[0][:], z1_planes[0][:], z1_grouped[0][:].rearrange("p v j -> p (v j)"))
         finish(1, nc.vector.tensor_copy, nc.sync)
+        finish(0, nc.scalar.copy, nc.scalar)

@@ -89,19 +89,22 @@ def tile_picked_ycin_both_p_kernel(
         rows = [(o, r) for o in range(PASSES) for r in range(4)]
         for o, r in rows[:4]:
             move_scales(o, r)
-        w_raw1 = sb([P, PACK, H], F32, "w_raw1", "table_scales")
-        nc.sync.dma_start(out=w_raw1[:], in_=w1[512:, :].rearrange("(p j) c -> p j c", j=PACK))
+        w_raw1 = [sb([P, 2, H], F32, f"w_raw1_{e}", ("table_scales", "table_words0")[e]) for e in range(2)]
+        for e in range(2):
+            nc.sync.dma_start(
+                out=w_raw1[e][:], in_=w1[512:, :].rearrange("(p j) c -> p j c", j=PACK)[:, 2 * e : 2 * e + 2, :]
+            )
         for o, r in rows[4:]:
             move_scales(o, r)
 
         w_grouped = {(o, u): sb([P, 2, P, PACK], BF16, f"w_grouped{o}_{u}") for o in range(PASSES) for u in range(2)}
         w_mx = {}
 
-        def cast_w(o, raw, m0):
+        def cast_w(o, raw, j0):
             src = raw[:].rearrange("p j (m t) -> p m t j", t=PACK)
-            ms = slice(m0, m0 + src.shape[1])
-            nc.vector.tensor_copy(out=w_grouped[o, 0][:, :, ms].rearrange("p t m j -> p m t j"), in_=src[:, :, 0:2])
-            nc.scalar.copy(out=w_grouped[o, 1][:, :, ms].rearrange("p t m j -> p m t j"), in_=src[:, :, 2:4])
+            js = slice(j0, j0 + src.shape[3])
+            nc.vector.tensor_copy(out=w_grouped[o, 0][:, :, :, js].rearrange("p t m j -> p m t j"), in_=src[:, :, 0:2])
+            nc.scalar.copy(out=w_grouped[o, 1][:, :, :, js].rearrange("p t m j -> p m t j"), in_=src[:, :, 2:4])
 
         def quantize(codes, planes, grouped):
             nc.vector.quantize_mx(out=codes.bitcast(FP8X4), scales=planes, in_=grouped)
@@ -145,7 +148,8 @@ def tile_picked_ycin_both_p_kernel(
         t_raw = [sb([P, PACK, N], F32, f"t_raw{d}", ("table_words1", "picked_scales")[d]) for d in range(2)]
         for d, tm in enumerate((t1, t2)):
             nc.sync.dma_start(out=t_raw[d][:], in_=tm.rearrange("(p j) n -> p j n", j=PACK))
-        cast_w(1, w_raw1, 0)
+        for e in range(2):
+            cast_w(1, w_raw1[e], 2 * e)
         for slots in ((0,), (1,), (2, 3)):
             quantize_w(1, slots)
             products(1, slots)
@@ -282,5 +286,5 @@ def tile_picked_ycin_both_p_kernel(
         quantize(z1_codes[1][:], z1_planes[1][:], z1_grouped[1][:].rearrange("p v j -> p (v j)"))
         quantize(z0_codes[1][:], z0_planes[1][:], z0_grouped[1][:].rearrange("p v j -> p (v j)"))
         quantize(z1_codes[0][:], z1_planes[0][:], z1_grouped[0][:].rearrange("p v j -> p (v j)"))
-        finish(1, nc.vector.tensor_copy, nc.sync)
-        finish(0, nc.scalar.copy, nc.scalar)
+        finish(1, nc.scalar.copy, nc.scalar)
+        finish(0, nc.vector.tensor_copy, nc.sync)

@@ -22,6 +22,7 @@ PASSES = K // (P * PACK)
 SPARE = 16
 HALF_S = S // 2
 HALF_V = V // 2
+HALF_H = H // 2
 
 
 def tile_picked_ycin_both_p_kernel(
@@ -50,17 +51,18 @@ def tile_picked_ycin_both_p_kernel(
         picked_scales = sb([P, S], U8, "picked_scales")
         x_planes = [sb([P, S], U8, f"x_planes{o}") for o in range(PASSES)]
         x_codes = [sb([P, S], U32, f"x_codes{o}") for o in range(PASSES)]
-        w_raw0 = sb([P, PACK, H], F32, "w_raw0")
-        y = [sb([P, S + SPARE], F32, f"y{t}") for t in range(PACK)]
-        x1 = [sb([P, V + SPARE], F32, f"x1_{t}") for t in range(PACK)]
+        y = {t: sb([P, S + SPARE], F32, f"y{t}") for t in (0, 1)}
+        y_slot = [sb([P, S], F32, f"y_slot{s}") for s in range(PACK)]
+        x1 = [sb([P, V + SPARE], F32, f"x1_{s}") for s in range(PACK)]
         identity = sb([P, P], F32, "identity")
 
         nc.vector.memset(table_scales[:].bitcast(I32), 0)
         for o in range(PASSES):
             nc.vector.memset(x_planes[o][:].bitcast(I32), 0)
-        for t in range(PACK):
+        for t in (0, 1):
             nc.vector.memset(y[t][:, S:], 0.0)
-            nc.vector.memset(x1[t][:, V:], 0.0)
+        for s in range(PACK):
+            nc.vector.memset(x1[s][:, V:], 0.0)
         make_identity(nc, identity[:])
 
         def load_words(o):
@@ -68,171 +70,219 @@ def tile_picked_ycin_both_p_kernel(
 
         def move_scales(o, r):
             nc.sync.dma_start(
-                out=x_planes[o][4 * o + r : P : 32, :].bitcast(I32),
+                out=x_planes[o][r:P:32, :].bitcast(I32),
                 in_=picked_scales[64 * o + 4 * r : 64 * (o + 1) : 16, :].bitcast(I32),
             )
 
-        load_words(0)
+        w_raw = {}
+
+        def load_w(o, half, tag=None):
+            w_raw[o, half] = sb([P, PACK, HALF_H], F32, f"w_raw{o}_{half}", tag)
+            rows = w1[512 * o : 512 * (o + 1), HALF_H * half : HALF_H * (half + 1)]
+            nc.sync.dma_start(out=w_raw[o, half][:], in_=rows.rearrange("(p j) c -> p j c", j=PACK))
+
+        load_w(0, 0)
         nc.sync.dma_start(
             out=table_scales[0:P:4, :].bitcast(I32), in_=x_scales.rearrange("o q c -> (o q) c").bitcast(I32)
         )
         nc.sync.dma_start(offs_sb[:], offs)
-        nc.sync.dma_start(fa_sb[:], fa)
-        nc.sync.dma_start(fb_sb[:], fb)
-        nc.sync.dma_start(fd_sb[:], fd)
-        nc.sync.dma_start(out=w_raw0[:], in_=w1[:512, :].rearrange("(p j) c -> p j c", j=PACK))
+        load_words(0)
         load_words(1)
-        nc.sync.dma_start(fc_sb[:], fc)
 
         nc.vector.tensor_copy(picked_scales[:], table_scales[:].indirect(offs_sb[:]))
         nc.vector.tensor_copy(x_codes[0][:], table_words[0][:].bitcast(U32).indirect(offs_sb[:]))
-        rows = [(o, r) for o in range(PASSES) for r in range(4)]
-        for o, r in rows[:4]:
-            move_scales(o, r)
-        w_raw1 = [sb([P, 2, H], F32, f"w_raw1_{e}", ("table_scales", "table_words0")[e]) for e in range(2)]
-        for e in range(2):
-            nc.sync.dma_start(
-                out=w_raw1[e][:], in_=w1[512:, :].rearrange("(p j) c -> p j c", j=PACK)[:, 2 * e : 2 * e + 2, :]
-            )
-        for o, r in rows[4:]:
-            move_scales(o, r)
+        for r in range(4):
+            move_scales(0, r)
+        load_w(1, 0)
+        load_w(0, 1)
+        for r in range(4):
+            move_scales(1, r)
+        nc.sync.dma_start(fa_sb[:], fa)
+        m1_sb = sb([P, S], F32, "m1_sb")
+        nc.sync.dma_start(out=m1_sb[:], in_=m1)
 
-        w_grouped = {(o, u): sb([P, 2, P, PACK], BF16, f"w_grouped{o}_{u}") for o in range(PASSES) for u in range(2)}
+        w_grouped = {}
         w_mx = {}
 
-        def cast_w(o, raw, j0):
-            src = raw[:].rearrange("p j (m t) -> p m t j", t=PACK)
-            js = slice(j0, j0 + src.shape[3])
-            nc.vector.tensor_copy(out=w_grouped[o, 0][:, :, :, js].rearrange("p t m j -> p m t j"), in_=src[:, :, 0:2])
-            nc.scalar.copy(out=w_grouped[o, 1][:, :, :, js].rearrange("p t m j -> p m t j"), in_=src[:, :, 2:4])
+        def cast_w(o, tiles, copy):
+            t0, n = tiles[0], len(tiles)
+            w_grouped[o, t0] = sb([P, 2 * n, P // 2, PACK], BF16, f"w_grouped{o}_{t0}")
+            src = w_raw[o, t0 // 2][:].rearrange("p j (m s) -> p m s j", s=PACK)
+            s0 = 2 * (t0 % 2)
+            copy(out=w_grouped[o, t0][:].rearrange("p s m j -> p m s j"), in_=src[:, :, s0 : s0 + 2 * n])
+
+        def interleave(copy, dst, src):
+            copy(out=dst, in_=src.rearrange("p j c -> p c j"))
 
         def quantize(codes, planes, grouped):
             nc.vector.quantize_mx(out=codes.bitcast(FP8X4), scales=planes, in_=grouped)
 
-        def quantize_w(o, slots):
-            codes = sb([P, len(slots) * P], U32, f"w_codes{o}_{slots[0]}")
-            planes = sb([P, len(slots) * P], U8, f"w_planes{o}_{slots[0]}")
-            i0 = slots[0] % 2
-            grouped = w_grouped[o, slots[0] // 2][:, i0 : i0 + len(slots)]
-            quantize(codes[:], planes[:], grouped.rearrange("p t m j -> p (t m j)"))
-            for i, t in enumerate(slots):
+        def quantize_w(o, tiles, tag=None):
+            t0, n = tiles[0], len(tiles)
+            codes = sb([P, n * P], U32, f"w_codes{o}_{t0}", tag)
+            planes = sb([P, n * P], U8, f"w_planes{o}_{t0}")
+            quantize(codes[:], planes[:], w_grouped[o, t0][:].rearrange("p s m j -> p (s m j)"))
+            for i, t in enumerate(tiles):
                 w_mx[o, t] = (codes[:, P * i : P * (i + 1)], planes[:, P * i : P * (i + 1)])
 
-        pieces = [(0, slice(0, HALF_S)), (0, slice(HALF_S, S))] + [(t, slice(0, S)) for t in range(1, PACK)]
-        y_acc = [bank(b, [P, cols.stop - cols.start], f"y_acc{b}") for b, (t, cols) in enumerate(pieces)]
+        low, high, whole = slice(0, HALF_S), slice(HALF_S, S), slice(0, S)
+        pieces = [(0, low), (0, high), (1, whole), (2, low), (3, whole), (2, high)]
+        y_acc = {}
 
-        def products(o, slots):
+        def products(passes, tile):
             for b, (t, cols) in enumerate(pieces):
-                if t in slots:
+                for o in passes if t == tile else ():
+                    if o == 0:
+                        y_acc[b] = bank((0, 1, 2, 0, 2, 1)[b], [P, cols.stop - cols.start], f"y_acc{b}")
                     nc.tensor.matmul_mx(
                         out=y_acc[b][:],
                         lhsT=w_mx[o, t][0].bitcast(FP8X4),
                         lhsT_scale=w_mx[o, t][1],
                         rhs=x_codes[o][:, cols].bitcast(FP8X4),
-                        rhs_scale=x_planes[o][4 * o : P, cols],
+                        rhs_scale=x_planes[o][:, cols],
                         start=(o == 0),
                         stop=(o == PASSES - 1),
                     )
 
-        cast_w(0, w_raw0, 0)
-        quantize_w(0, (0, 1))
-        quantize_w(0, (2, 3))
-        products(0, range(PACK))
-        m1_sb = sb([P, S], F32, "m1_sb", "w_raw0")
-        nc.sync.dma_start(out=m1_sb[:], in_=m1)
-        unit_sb = sb([P, PACK], F32, "unit_sb", "w_grouped0_0")
+        def empty_y(tile):
+            for b, (t, cols) in enumerate(pieces):
+                if t == tile:
+                    copy = nc.vector.tensor_copy if b == 0 else nc.scalar.copy
+                    copy(out=y[t][:, cols], in_=y_acc[b][:])
+
+        cast_w(0, (0,), nc.scalar.copy)
+        cast_w(0, (1,), nc.scalar.copy)
+        for t in (0, 1):
+            quantize_w(0, (t,), ("table_scales", None)[t])
+            products((0,), t)
+        load_w(1, 1, "table_words0")
+        nc.sync.dma_start(fb_sb[:], fb)
+        nc.sync.dma_start(fc_sb[:], fc)
+        nc.sync.dma_start(fd_sb[:], fd)
+        unit_sb = sb([P, PACK], F32, "unit_sb", "w_raw0_0")
         nc.sync.dma_start(out=unit_sb[:], in_=unit.rearrange("(p t) o -> p (t o)", t=PACK))
-        m2_sb = sb([P, V], F32, "m2_sb", "w_grouped0_1")
-        nc.sync.dma_start(out=m2_sb[:], in_=m2)
         nc.vector.tensor_copy(x_codes[1][:], table_words[1][:].bitcast(U32).indirect(offs_sb[:]))
-        t_raw = [sb([P, PACK, N], F32, f"t_raw{d}", ("table_words1", "picked_scales")[d]) for d in range(2)]
+        m2_sb = sb([P, V], F32, "m2_sb", "table_words1")
+        nc.sync.dma_start(out=m2_sb[:], in_=m2)
+        cast_w(1, (0,), nc.vector.tensor_copy)
+        cast_w(1, (1,), nc.scalar.copy)
+        t_raw = [sb([P, PACK, N], F32, f"t_raw{d}", ("w_raw1_0", "picked_scales")[d]) for d in range(2)]
         for d, tm in enumerate((t1, t2)):
             nc.sync.dma_start(out=t_raw[d][:], in_=tm.rearrange("(p j) n -> p j n", j=PACK))
-        for e in range(2):
-            cast_w(1, w_raw1[e], 2 * e)
-        for slots in ((0,), (1,), (2, 3)):
-            quantize_w(1, slots)
-            products(1, slots)
-        for b, (t, cols) in enumerate(pieces):
-            copy = nc.vector.tensor_copy if b == 0 else nc.scalar.copy
-            copy(out=y[t][:, cols], in_=y_acc[b][:])
+        for t in (0, 1):
+            quantize_w(1, (t,))
+            products((1,), t)
+        for t in (0, 1):
+            empty_y(t)
+        cast_w(0, (2, 3), nc.vector.tensor_copy)
+        quantize_w(0, (2, 3), "w_codes1_0")
+        for t in (2, 3):
+            products((0,), t)
+        for t in (2, 3):
+            cast_w(1, (t,), nc.scalar.copy)
+            quantize_w(1, (t,))
+            products((1,), t)
+        m2u = {}
+        for s, halves in [(s, (0, 1)) for s in range(PACK - 1)] + [(PACK - 1, (h,)) for h in range(2)]:
+            cols = slice(HALF_V * halves[0], HALF_V * (halves[-1] + 1))
+            m2u[s, halves[0]] = sb([P, cols.stop - cols.start], F32, f"m2u{s}_{halves[0]}")
+            nc.scalar.activation(out=m2u[s, halves[0]][:], in_=m2_sb[:, cols], func=COPY, scale=unit_sb[:, s : s + 1])
+        t_grouped = sb([P, 2, N, PACK], BF16, "t_grouped")
+        y[2] = sb([P, S], F32, "y2", "table_words1")
+        empty_y(2)
+        interleave(nc.scalar.copy, t_grouped[:, 0], t_raw[0][:])
+        y[3] = sb([P, S], F32, "y3", "w_raw1_0")
 
-        first = [sb([P, S], F32, f"first{t}") for t in range(PACK)]
-        m2u = [sb([P, V], F32, f"m2u{t}", ("w_codes1_1", "w_planes1_1", "w_planes1_2", "x_planes1")[t]) for t in range(PACK)]
-        z0_rows = [sb([P, PACK, HALF_V], BF16, f"z0_rows{h}") for h in range(2)]
-        z0_grouped = [sb([P, HALF_V, PACK], BF16, f"z0_grouped{h}") for h in range(2)]
-        z1_grouped = [sb([P, HALF_V, PACK], BF16, f"z1_grouped{h}") for h in range(2)]
-        t_grouped = sb([P, 2, N, PACK], BF16, "t_grouped", "w_codes1_2")
+        def deal_y(t):
+            for u in range(2):
+                nc.sync.dma_start(
+                    out=y_slot[2 * (t % 2) + u][64 * (t // 2) : 64 * (t // 2 + 1), :], in_=y[t][64 * u : 64 * (u + 1), :S]
+                )
+
+        for t in range(PACK - 1):
+            deal_y(t)
+
+        first = [sb([P, S], F32, f"first{t}", ("w_raw0_1", "w_grouped0_2", None, None)[t]) for t in range(PACK)]
+        z0_pairs = sb([P, 2, V, 2], BF16, "z0_pairs")
+        z0_grouped = sb([P, V, PACK], BF16, "z0_grouped")
         t_planes = sb([P, 2 * N], U8, "t_planes")
         z0_planes = [sb([P, HALF_V], U8, f"z0_planes{h}") for h in range(2)]
         z1_codes = [sb([P, HALF_V], U32, f"z1_codes{h}") for h in range(2)]
         z1_planes = [sb([P, HALF_V], U8, f"z1_planes{h}") for h in range(2)]
         result = [sb([P, HALF_V], F32, f"result{h}") for h in range(2)]
-        z1_rows = sb([P, PACK, V], F32, "z1_rows")
+        x1_turned = [sb([P, 2, 2, 2, P // 2], F32, f"x1_turned{g}") for g in range(2)]
+        back = {}
         second = {}
         p1 = {}
 
-        def interleave(copy, dst, src):
-            copy(out=dst, in_=src.rearrange("p j c -> p c j"))
-
-        def look_up_fa(t):
-            nc.vector.tensor_tensor(first[t][:], y[t][:].indirect(fa_sb[:]), m1_sb[:], MULT)
-
-        def look_up_fb(t, halves, turn_bank, back_bank):
-            n = len(halves)
+        def look_up_fa(t, halves):
             cols = slice(HALF_S * halves[0], HALF_S * (halves[-1] + 1))
-            vs = slice(cols.start // 2, cols.stop // 2)
-            name = f"{t}_{halves[0]}"
-            p1[name] = sb([P, n, HALF_S], F32, f"p1_{name}")
             nc.vector.tensor_tensor(
-                p1[name][:].rearrange("p h s -> p (h s)"),
+                first[t][:, cols], y[t][:].indirect(fa_sb[:, cols.start // 16 : cols.stop // 16]), m1_sb[:, cols], MULT
+            )
+
+        def look_up_fb(t, halves, tag=None):
+            cols = slice(HALF_S * halves[0], HALF_S * (halves[-1] + 1))
+            product = sb([P, len(halves), HALF_S], F32, f"p1_{t}_{halves[0]}", tag)
+            nc.vector.tensor_tensor(
+                product[:].rearrange("p h s -> p (h s)"),
                 y[t][:].indirect(fb_sb[:, cols.start // 16 : cols.stop // 16]),
                 first[t][:, cols],
                 MULT,
             )
-            turned = bank(turn_bank, [P, n, P], f"turned{name}")
-            for h in range(n):
+            for i, h in enumerate(halves):
+                p1[t, h] = product[:, i, :]
+
+        def sum_pairs(t, halves, turn_bank):
+            n, h0 = len(halves), halves[0]
+            turned = bank(turn_bank, [P, n, P], f"turned{t}_{h0}")
+            for i, h in enumerate(halves):
                 for d in range(2):
                     nc.tensor.matmul(
-                        out=turned[:, h, :],
-                        lhsT=p1[name][:, h, d::2],
+                        out=turned[:, i, :],
+                        lhsT=p1[t, h][:, d::2],
                         rhs=identity[:],
                         is_transpose=True,
                         start=(d == 0),
                         stop=(d == 1),
                     )
-            x1_turned = sb([P, n, P], F32, f"x1_turned{name}")
-            nc.scalar.copy(out=x1_turned[:], in_=turned[:])
-            back = bank(back_bank, [P, n, P], f"back{name}")
-            for h in range(n):
-                nc.tensor.transpose(back[:, h, :], x1_turned[:, h, :], identity[:])
-            back_v = back[:].rearrange("p h v -> p (h v)")
-            nc.scalar.copy(out=x1[t][:, vs], in_=back_v)
-            for i, h in enumerate(halves):
-                nc.scalar.activation(out=z0_rows[h][:, t, :], in_=back[:, i, :], func=COPY, scale=unit_sb[:, t : t + 1])
+            nc.scalar.copy(
+                out=x1_turned[t % 2][:, h0 : h0 + n, :, t // 2, :], in_=turned[:].rearrange("p h (u m) -> p h u m", u=2)
+            )
 
-        def look_up_fd(t, halves):
+        def turn_back(s, back_bank):
+            back[s] = bank(back_bank, [P, 2, P], f"back{s}")
+            for h in range(2):
+                nc.tensor.transpose(back[s][:, h, :], x1_turned[s // 2][:, h, s % 2].rearrange("p a m -> p (a m)"), identity[:])
+
+        def keep_x1(s):
+            nc.scalar.copy(out=x1[s][:, :V], in_=back[s][:].rearrange("p h v -> p (h v)"))
+
+        def scale_z0(s, src):
+            nc.scalar.activation(out=z0_pairs[:, s // 2, :, s % 2], in_=src, func=COPY, scale=unit_sb[:, s : s + 1])
+
+        def look_up_fd(s, halves):
             cols = slice(HALF_V * halves[0], HALF_V * (halves[-1] + 1))
-            second[t, halves[0]] = sb([P, cols.stop - cols.start], F32, f"second{t}_{halves[0]}")
+            second[s, halves[0]] = sb([P, cols.stop - cols.start], F32, f"second{s}_{halves[0]}")
             nc.vector.tensor_tensor(
-                second[t, halves[0]][:],
-                y[t][:].indirect(fd_sb[:, cols.start // 16 : cols.stop // 16]),
-                m2u[t][:, cols],
+                second[s, halves[0]][:],
+                y_slot[s][:].indirect(fd_sb[:, cols.start // 16 : cols.stop // 16]),
+                m2u[s, halves[0]][:],
                 MULT,
             )
 
-        def look_up_fc(t, halves):
+        def look_up_fc(s, halves):
             cols = slice(HALF_V * halves[0], HALF_V * (halves[-1] + 1))
             nc.vector.tensor_tensor(
-                z1_rows[:, t, cols],
-                x1[t][:].indirect(fc_sb[:, cols.start // 16 : cols.stop // 16]),
-                second[t, halves[0]][:],
+                z1_rows[:, s, cols],
+                x1[s][:].indirect(fc_sb[:, cols.start // 16 : cols.stop // 16]),
+                second[s, halves[0]][:],
                 MULT,
             )
 
         def finish(h, copy, queue):
             cols = slice(HALF_V * h, HALF_V * (h + 1))
-            acc = bank(1 + h, [P, HALF_V], f"out_acc{h}")
+            acc = bank(3 + h, [P, HALF_V], f"out_acc{h}")
             nc.tensor.matmul_mx(
                 out=acc[:],
                 lhsT=t_codes[:, :N].bitcast(FP8X4),
@@ -254,25 +304,47 @@ def tile_picked_ycin_both_p_kernel(
             copy(out=result[h][:], in_=acc[:])
             queue.dma_start(out=out[:, cols], in_=result[h][:])
 
-        for d in range(2):
-            interleave(nc.scalar.copy, t_grouped[:, d], t_raw[d][:])
-        for t in range(PACK):
-            nc.scalar.activation(out=m2u[t][:], in_=m2_sb[:], func=COPY, scale=unit_sb[:, t : t + 1])
-        look_up_fa(0)
-        look_up_fa(1)
-        look_up_fb(0, (0, 1), 5, 7)
-        look_up_fa(2)
-        look_up_fb(1, (0, 1), 6, 0)
-        look_up_fa(3)
-        look_up_fb(2, (0, 1), 5, 7)
-        look_up_fb(3, (0,), 6, 0)
-        look_up_fb(3, (1,), 3, 4)
+        look_up_fa(0, (0, 1))
+        look_up_fa(1, (0, 1))
+        look_up_fb(0, (0,))
+        sum_pairs(0, (0,), 0)
+        look_up_fb(0, (1,), "table_words0")
+        sum_pairs(0, (1,), 1)
+        empty_y(3)
+        deal_y(3)
+        look_up_fb(1, (0, 1), "w_grouped1_3")
+        sum_pairs(1, (0, 1), 2)
+        interleave(nc.scalar.copy, t_grouped[:, 1], t_raw[1][:])
+        for h in range(2):
+            look_up_fa(2, (h,))
+        for h in range(2):
+            look_up_fb(2, (h,))
+            sum_pairs(2, (h,), 3 + h)
+        for h in range(2):
+            look_up_fa(3, (h,))
+        for s in (0, 1):
+            turn_back(s, 5 + s)
+            keep_x1(s)
+        for s in (0, 1):
+            scale_z0(s, x1[s][:, :V])
+        for h in range(2):
+            look_up_fb(3, (h,))
+        sum_pairs(3, (0, 1), 5)
+        for s in (2, 3):
+            turn_back(s, (7, 0)[s - 2])
+        keep_x1(2)
+        for s in (2, 3):
+            scale_z0(s, back[s][:].rearrange("p h v -> p (h v)"))
+        keep_x1(3)
         for t in range(PACK - 1):
             look_up_fd(t, (0, 1))
         for h in range(2):
             look_up_fd(PACK - 1, (h,))
-        for h in range(2):
-            interleave(nc.scalar.copy, z0_grouped[h][:], z0_rows[h][:])
+        pairs = z0_pairs[:].rearrange("p g v u -> p g (v u)").bitcast(U32)
+        words = z0_grouped[:].rearrange("p v j -> p (v j)").bitcast(U32).rearrange("p (v g) -> p v g", g=2)
+        interleave(nc.scalar.copy, words, pairs)
+        z1_grouped = [sb([P, HALF_V, PACK], BF16, f"z1_grouped{h}", ("z0_pairs", None)[h]) for h in range(2)]
+        z1_rows = sb([P, PACK, V], F32, "z1_rows", "m2u3_0")
         for t in range(PACK - 1):
             look_up_fc(t, (0, 1))
         for h in range(2):
@@ -282,9 +354,9 @@ def tile_picked_ycin_both_p_kernel(
         quantize(t_codes[:], t_planes[:], t_grouped[:].rearrange("p d n j -> p (d n j)"))
         interleave(nc.vector.tensor_copy, z1_grouped[1][:], z1_rows[:, :, HALF_V:])
         z0_codes = [sb([P, HALF_V], U32, f"z0_codes{h}", ("second3_1", None)[h]) for h in range(2)]
-        quantize(z0_codes[0][:], z0_planes[0][:], z0_grouped[0][:].rearrange("p v j -> p (v j)"))
+        quantize(z0_codes[0][:], z0_planes[0][:], z0_grouped[:, :HALF_V].rearrange("p v j -> p (v j)"))
         quantize(z1_codes[1][:], z1_planes[1][:], z1_grouped[1][:].rearrange("p v j -> p (v j)"))
-        quantize(z0_codes[1][:], z0_planes[1][:], z0_grouped[1][:].rearrange("p v j -> p (v j)"))
+        quantize(z0_codes[1][:], z0_planes[1][:], z0_grouped[:, HALF_V:].rearrange("p v j -> p (v j)"))
         quantize(z1_codes[0][:], z1_planes[0][:], z1_grouped[0][:].rearrange("p v j -> p (v j)"))
         finish(1, nc.scalar.copy, nc.scalar)
         finish(0, nc.vector.tensor_copy, nc.sync)

@@ -349,10 +349,11 @@ def tile_picked_ycin_both_p_kernel(
             look_up_fc(t, (0, 1))
         for h in range(2):
             look_up_fc(PACK - 1, (h,))
+        interleave(nc.scalar.copy, z1_grouped[1][:, :, :2], z1_rows[:, :2, HALF_V:])
         interleave(nc.scalar.copy, z1_grouped[0][:], z1_rows[:, :, :HALF_V])
         t_codes = sb([P, 2 * N], U32, "t_codes", "second3_0")
         quantize(t_codes[:], t_planes[:], t_grouped[:].rearrange("p d n j -> p (d n j)"))
-        interleave(nc.vector.tensor_copy, z1_grouped[1][:], z1_rows[:, :, HALF_V:])
+        interleave(nc.vector.tensor_copy, z1_grouped[1][:, :, 2:], z1_rows[:, 2:, HALF_V:])
         z0_codes = [sb([P, HALF_V], U32, f"z0_codes{h}", ("second3_1", None)[h]) for h in range(2)]
         quantize(z0_codes[0][:], z0_planes[0][:], z0_grouped[:, :HALF_V].rearrange("p v j -> p (v j)"))
         quantize(z1_codes[1][:], z1_planes[1][:], z1_grouped[1][:].rearrange("p v j -> p (v j)"))

@@ -14,6 +14,7 @@ U16 = mybir.dt.uint16
 U8 = mybir.dt.uint8
 FP8X4 = mybir.dt.float8_e4m3fn_x4
 MULT = mybir.AluOpType.mult
+ADD = mybir.AluOpType.add
 COPY = mybir.ActivationFunctionType.Copy
 
 P = 128
@@ -51,7 +52,7 @@ def tile_picked_ycin_both_p_kernel(
         picked_scales = sb([P, S], U8, "picked_scales")
         x_planes = [sb([P, S], U8, f"x_planes{o}") for o in range(PASSES)]
         x_codes = [sb([P, S], U32, f"x_codes{o}") for o in range(PASSES)]
-        y = {t: sb([P, S + SPARE], F32, f"y{t}") for t in (0, 1)}
+        y = [sb([P, S + SPARE], F32, f"y{t}") for t in range(PACK)]
         y_slot = [sb([P, S], F32, f"y_slot{s}") for s in range(PACK)]
         x1 = [sb([P, V + SPARE], F32, f"x1_{s}") for s in range(PACK)]
         identity = sb([P, P], F32, "identity")
@@ -59,11 +60,10 @@ def tile_picked_ycin_both_p_kernel(
         nc.vector.memset(table_scales[:].bitcast(I32), 0)
         for o in range(PASSES):
             nc.vector.memset(x_planes[o][:].bitcast(I32), 0)
-        for t in (0, 1):
-            nc.vector.memset(y[t][:, S:], 0.0)
-        for s in range(PACK):
-            nc.vector.memset(x1[s][:, V:], 0.0)
         make_identity(nc, identity[:])
+        for s in range(PACK):
+            nc.gpsimd.memset(y[s][:, S:], 0.0)
+            nc.gpsimd.memset(x1[s][:, V:], 0.0)
 
         def load_words(o):
             nc.sync.dma_start(out=table_words[o][:], in_=x_words[o].rearrange("p c r -> p (c r)").bitcast(I32))
@@ -86,8 +86,17 @@ def tile_picked_ycin_both_p_kernel(
             out=table_scales[0:P:4, :].bitcast(I32), in_=x_scales.rearrange("o q c -> (o q) c").bitcast(I32)
         )
         nc.sync.dma_start(offs_sb[:], offs)
+        m1_cols = sb([P, 2, 2], F32, "m1_cols")
+        nc.sync.dma_start(out=m1_cols[:], in_=m1[0].rearrange("(h p d) -> p h d", h=2, d=2))
         load_words(0)
         load_words(1)
+
+        m1_spread = bank(3, [P, 2, 2, P], "m1_spread")
+        for h in range(2):
+            for d in range(2):
+                nc.tensor.transpose(m1_spread[:, h, d, :], m1_cols[:, h, d : d + 1].to_broadcast([P, P]), identity[:])
+        m1_sb = sb([P, S], F32, "m1_sb")
+        nc.scalar.copy(out=m1_sb[:].rearrange("p (h v d) -> p h v d", h=2, d=2), in_=m1_spread[:].rearrange("p h d v -> p h v d"))
 
         nc.vector.tensor_copy(picked_scales[:], table_scales[:].indirect(offs_sb[:]))
         nc.vector.tensor_copy(x_codes[0][:], table_words[0][:].bitcast(U32).indirect(offs_sb[:]))
@@ -98,8 +107,6 @@ def tile_picked_ycin_both_p_kernel(
         for r in range(4):
             move_scales(1, r)
         nc.sync.dma_start(fa_sb[:], fa)
-        m1_sb = sb([P, S], F32, "m1_sb")
-        nc.sync.dma_start(out=m1_sb[:], in_=m1)
 
         w_grouped = {}
         w_mx = {}
@@ -126,14 +133,14 @@ def tile_picked_ycin_both_p_kernel(
                 w_mx[o, t] = (codes[:, P * i : P * (i + 1)], planes[:, P * i : P * (i + 1)])
 
         low, high, whole = slice(0, HALF_S), slice(HALF_S, S), slice(0, S)
-        pieces = [(0, low), (0, high), (1, whole), (2, low), (3, whole), (2, high)]
+        pieces = [(0, low), (0, high), (1, whole), (2, low), (2, high), (3, whole)]
         y_acc = {}
 
         def products(passes, tile):
             for b, (t, cols) in enumerate(pieces):
                 for o in passes if t == tile else ():
                     if o == 0:
-                        y_acc[b] = bank((0, 1, 2, 0, 2, 1)[b], [P, cols.stop - cols.start], f"y_acc{b}")
+                        y_acc[b] = bank(b % 3, [P, cols.stop - cols.start], f"y_acc{b}")
                     nc.tensor.matmul_mx(
                         out=y_acc[b][:],
                         lhsT=w_mx[o, t][0].bitcast(FP8X4),
@@ -172,26 +179,30 @@ def tile_picked_ycin_both_p_kernel(
         for t in (0, 1):
             quantize_w(1, (t,))
             products((1,), t)
+        first = {}
+
+        def look_up_fa(t, tag=None):
+            first[t] = sb([P, S], F32, f"first{t}", tag)
+            if t % 2 == 0:
+                nc.vector.tensor_tensor(first[t][:], y[t][:].indirect(fa_sb[:]), m1_sb[:], MULT)
+            else:
+                nc.scalar.activation(out=first[t][:], in_=y[t][:].indirect(fa_sb[:]), func=COPY)
+
         for t in (0, 1):
             empty_y(t)
         cast_w(0, (2, 3), nc.vector.tensor_copy)
         quantize_w(0, (2, 3), "w_codes1_0")
         for t in (2, 3):
             products((0,), t)
+        look_up_fa(0, "w_raw0_1")
         for t in (2, 3):
             cast_w(1, (t,), nc.scalar.copy)
-            quantize_w(1, (t,))
-            products((1,), t)
-        m2u = {}
-        for s, halves in [(s, (0, 1)) for s in range(PACK - 1)] + [(PACK - 1, (h,)) for h in range(2)]:
-            cols = slice(HALF_V * halves[0], HALF_V * (halves[-1] + 1))
-            m2u[s, halves[0]] = sb([P, cols.stop - cols.start], F32, f"m2u{s}_{halves[0]}")
-            nc.scalar.activation(out=m2u[s, halves[0]][:], in_=m2_sb[:, cols], func=COPY, scale=unit_sb[:, s : s + 1])
+        look_up_fa(1, "table_words0")
         t_grouped = sb([P, 2, N, PACK], BF16, "t_grouped")
-        y[2] = sb([P, S], F32, "y2", "table_words1")
-        empty_y(2)
-        interleave(nc.scalar.copy, t_grouped[:, 0], t_raw[0][:])
-        y[3] = sb([P, S], F32, "y3", "w_raw1_0")
+        for d in range(2):
+            nc.gpsimd.tensor_scalar(
+                out=t_grouped[:, d], in0=t_raw[d][:].rearrange("p j c -> p c j"), scalar1=1.0, scalar2=0.0, op0=MULT, op1=ADD
+            )
 
         def deal_y(t):
             for u in range(2):
@@ -199,165 +210,170 @@ def tile_picked_ycin_both_p_kernel(
                     out=y_slot[2 * (t % 2) + u][64 * (t // 2) : 64 * (t // 2 + 1), :], in_=y[t][64 * u : 64 * (u + 1), :S]
                 )
 
-        for t in range(PACK - 1):
-            deal_y(t)
-
-        first = [sb([P, S], F32, f"first{t}", ("w_raw0_1", "w_grouped0_2", None, None)[t]) for t in range(PACK)]
         z0_pairs = sb([P, 2, V, 2], BF16, "z0_pairs")
-        z0_grouped = sb([P, V, PACK], BF16, "z0_grouped")
+        z0_grouped = [sb([P, HALF_V, PACK], BF16, f"z0_grouped{h}") for h in range(2)]
+        z1_grouped = [sb([P, HALF_V, PACK], BF16, f"z1_grouped{h}") for h in range(2)]
         t_planes = sb([P, 2 * N], U8, "t_planes")
-        z0_planes = [sb([P, HALF_V], U8, f"z0_planes{h}") for h in range(2)]
-        z1_codes = [sb([P, HALF_V], U32, f"z1_codes{h}") for h in range(2)]
-        z1_planes = [sb([P, HALF_V], U8, f"z1_planes{h}") for h in range(2)]
+        z_codes = {}
+        z_planes = [[sb([P, HALF_V], U8, f"z{d}_planes{h}") for h in range(2)] for d in range(2)]
         result = [sb([P, HALF_V], F32, f"result{h}") for h in range(2)]
-        x1_turned = [sb([P, 2, 2, 2, P // 2], F32, f"x1_turned{g}") for g in range(2)]
+        summed = sb([P, 2, 2, 2, P // 2], F32, "summed")
+        weighted = sb([P, 2, 2, 2, 2, P // 2], F32, "weighted")
+        p1 = {}
+        turned = {}
         back = {}
         second = {}
-        p1 = {}
 
-        def look_up_fa(t, halves):
-            cols = slice(HALF_S * halves[0], HALF_S * (halves[-1] + 1))
-            nc.vector.tensor_tensor(
-                first[t][:, cols], y[t][:].indirect(fa_sb[:, cols.start // 16 : cols.stop // 16]), m1_sb[:, cols], MULT
-            )
+        def look_up_fb(t, tag=None):
+            p1[t] = sb([P, S], F32, f"p1_{t}", tag)
+            nc.vector.tensor_tensor(p1[t][:], y[t][:].indirect(fb_sb[:]), first[t][:], MULT)
 
-        def look_up_fb(t, halves, tag=None):
-            cols = slice(HALF_S * halves[0], HALF_S * (halves[-1] + 1))
-            product = sb([P, len(halves), HALF_S], F32, f"p1_{t}_{halves[0]}", tag)
-            nc.vector.tensor_tensor(
-                product[:].rearrange("p h s -> p (h s)"),
-                y[t][:].indirect(fb_sb[:, cols.start // 16 : cols.stop // 16]),
-                first[t][:, cols],
-                MULT,
-            )
-            for i, h in enumerate(halves):
-                p1[t, h] = product[:, i, :]
+        def turn(t, turn_bank):
+            turned[t] = bank(turn_bank, [P, 2, 2, P], f"turned{t}")
+            for h in range(2):
+                for d in range(2):
+                    nc.tensor.transpose(turned[t][:, h, d, :], p1[t][:, 2 * P * h + d : 2 * P * (h + 1) : 2], identity[:])
 
-        def sum_pairs(t, halves, turn_bank):
-            n, h0 = len(halves), halves[0]
-            turned = bank(turn_bank, [P, n, P], f"turned{t}_{h0}")
-            for i, h in enumerate(halves):
+        def weigh(t):
+            for h in range(2):
+                for d in range(2):
+                    nc.scalar.activation(
+                        out=weighted[:, h, d, :, t // 2, :],
+                        in_=turned[t][:, h, d, :].rearrange("p (u m) -> p u m", u=2),
+                        func=COPY,
+                        scale=m1_cols[:, h, d : d + 1],
+                    )
+
+        def sum_pairs(t, turn_bank):
+            turned[t] = bank(turn_bank, [P, 2, P], f"turned{t}")
+            for h in range(2):
                 for d in range(2):
                     nc.tensor.matmul(
-                        out=turned[:, i, :],
-                        lhsT=p1[t, h][:, d::2],
+                        out=turned[t][:, h, :],
+                        lhsT=p1[t][:, 2 * P * h + d : 2 * P * (h + 1) : 2],
                         rhs=identity[:],
                         is_transpose=True,
                         start=(d == 0),
                         stop=(d == 1),
                     )
-            nc.scalar.copy(
-                out=x1_turned[t % 2][:, h0 : h0 + n, :, t // 2, :], in_=turned[:].rearrange("p h (u m) -> p h u m", u=2)
-            )
+
+        def keep_sums(t):
+            nc.scalar.copy(out=summed[:, :, :, t // 2, :], in_=turned[t][:].rearrange("p h (u m) -> p h u m", u=2))
 
         def turn_back(s, back_bank):
             back[s] = bank(back_bank, [P, 2, P], f"back{s}")
             for h in range(2):
-                nc.tensor.transpose(back[s][:, h, :], x1_turned[s // 2][:, h, s % 2].rearrange("p a m -> p (a m)"), identity[:])
+                terms = [summed[:, h, s]] if s < 2 else [weighted[:, h, d, s % 2] for d in range(2)]
+                for i, term in enumerate(terms):
+                    nc.tensor.matmul(
+                        out=back[s][:, h, :],
+                        lhsT=term.rearrange("p a m -> p (a m)"),
+                        rhs=identity[:],
+                        is_transpose=True,
+                        start=(i == 0),
+                        stop=(i == len(terms) - 1),
+                    )
 
         def keep_x1(s):
             nc.scalar.copy(out=x1[s][:, :V], in_=back[s][:].rearrange("p h v -> p (h v)"))
 
-        def scale_z0(s, src):
-            nc.scalar.activation(out=z0_pairs[:, s // 2, :, s % 2], in_=src, func=COPY, scale=unit_sb[:, s : s + 1])
-
-        def look_up_fd(s, halves):
-            cols = slice(HALF_V * halves[0], HALF_V * (halves[-1] + 1))
-            second[s, halves[0]] = sb([P, cols.stop - cols.start], F32, f"second{s}_{halves[0]}")
-            nc.vector.tensor_tensor(
-                second[s, halves[0]][:],
-                y_slot[s][:].indirect(fd_sb[:, cols.start // 16 : cols.stop // 16]),
-                m2u[s, halves[0]][:],
-                MULT,
+        def scale_z0(s):
+            nc.scalar.activation(
+                out=z0_pairs[:, s // 2, :, s % 2],
+                in_=back[s][:].rearrange("p h v -> p (h v)"),
+                func=COPY,
+                scale=unit_sb[:, s : s + 1],
             )
+
+        def weave_z0(h):
+            pairs = z0_pairs[:].rearrange("p g v u -> p g (v u)").bitcast(U32)[:, :, HALF_V * h : HALF_V * (h + 1)]
+            words = z0_grouped[h][:].rearrange("p v j -> p (v j)").bitcast(U32).rearrange("p (v g) -> p v g", g=2)
+            interleave(nc.scalar.copy, words, pairs)
+
+        def look_up_fd(s, tag=None):
+            second[s] = sb([P, V], F32, f"second{s}", tag)
+            nc.vector.tensor_tensor(second[s][:], y_slot[s][:].indirect(fd_sb[:]), m2u[s // 2][:, s % 2, :], MULT)
 
         def look_up_fc(s, halves):
             cols = slice(HALF_V * halves[0], HALF_V * (halves[-1] + 1))
             nc.vector.tensor_tensor(
-                z1_rows[:, s, cols],
-                x1[s][:].indirect(fc_sb[:, cols.start // 16 : cols.stop // 16]),
-                second[s, halves[0]][:],
-                MULT,
+                z1_rows[:, s, cols], x1[s][:].indirect(fc_sb[:, cols.start // 16 : cols.stop // 16]), second[s][:, cols], MULT
             )
+
+        def quantize_z(d, h):
+            grouped = (z0_grouped, z1_grouped)[d][h]
+            z_codes[d, h] = sb([P, HALF_V], U32, f"z{d}_codes{h}", f"second{2 + h}" if d == 0 else None)
+            quantize(z_codes[d, h][:], z_planes[d][h][:], grouped[:].rearrange("p v j -> p (v j)"))
 
         def finish(h, copy, queue):
             cols = slice(HALF_V * h, HALF_V * (h + 1))
             acc = bank(3 + h, [P, HALF_V], f"out_acc{h}")
-            nc.tensor.matmul_mx(
-                out=acc[:],
-                lhsT=t_codes[:, :N].bitcast(FP8X4),
-                lhsT_scale=t_planes[:, :N],
-                rhs=z0_codes[h][:].bitcast(FP8X4),
-                rhs_scale=z0_planes[h][:],
-                start=True,
-                stop=False,
-            )
-            nc.tensor.matmul_mx(
-                out=acc[:],
-                lhsT=t_codes[:, N:].bitcast(FP8X4),
-                lhsT_scale=t_planes[:, N:],
-                rhs=z1_codes[h][:].bitcast(FP8X4),
-                rhs_scale=z1_planes[h][:],
-                start=False,
-                stop=True,
-            )
+            for d in range(2):
+                nc.tensor.matmul_mx(
+                    out=acc[:],
+                    lhsT=t_codes[:, N * d : N * (d + 1)].bitcast(FP8X4),
+                    lhsT_scale=t_planes[:, N * d : N * (d + 1)],
+                    rhs=z_codes[d, h][:].bitcast(FP8X4),
+                    rhs_scale=z_planes[d][h][:],
+                    start=(d == 0),
+                    stop=(d == 1),
+                )
             copy(out=result[h][:], in_=acc[:])
             queue.dma_start(out=out[:, cols], in_=result[h][:])
 
-        look_up_fa(0, (0, 1))
-        look_up_fa(1, (0, 1))
-        look_up_fb(0, (0,))
-        sum_pairs(0, (0,), 0)
-        look_up_fb(0, (1,), "table_words0")
-        sum_pairs(0, (1,), 1)
+        m2u = {}
+
+        def scale_m2(g, tag):
+            m2u[g] = sb([P, 2, V], F32, f"m2u{g}", tag)
+            for u in range(2):
+                s = 2 * g + u
+                nc.scalar.activation(out=m2u[g][:, u, :], in_=m2_sb[:], func=COPY, scale=unit_sb[:, s : s + 1])
+
+        quantize_w(1, (2,))
+        products((1,), 2)
+        look_up_fb(0, "w_grouped1_2")
+        quantize_w(1, (3,))
+        products((1,), 3)
+        empty_y(2)
+        scale_m2(0, "w_grouped1_3")
         empty_y(3)
-        deal_y(3)
-        look_up_fb(1, (0, 1), "w_grouped1_3")
-        sum_pairs(1, (0, 1), 2)
-        interleave(nc.scalar.copy, t_grouped[:, 1], t_raw[1][:])
-        for h in range(2):
-            look_up_fa(2, (h,))
-        for h in range(2):
-            look_up_fb(2, (h,))
-            sum_pairs(2, (h,), 3 + h)
-        for h in range(2):
-            look_up_fa(3, (h,))
-        for s in (0, 1):
-            turn_back(s, 5 + s)
+        look_up_fa(3)
+        for t in range(PACK):
+            deal_y(t)
+        look_up_fb(1)
+        sum_pairs(0, 3)
+        turn(1, 2)
+        look_up_fa(2)
+        look_up_fb(2)
+        sum_pairs(2, 5)
+        look_up_fb(3)
+        turn(3, 6)
+        keep_sums(0)
+        scale_m2(1, "p1_1")
+        weigh(1)
+        keep_sums(2)
+        weigh(3)
+        for s in range(PACK):
+            turn_back(s, (0, 1, 4, 7)[s])
             keep_x1(s)
-        for s in (0, 1):
-            scale_z0(s, x1[s][:, :V])
-        for h in range(2):
-            look_up_fb(3, (h,))
-        sum_pairs(3, (0, 1), 5)
-        for s in (2, 3):
-            turn_back(s, (7, 0)[s - 2])
-        keep_x1(2)
-        for s in (2, 3):
-            scale_z0(s, back[s][:].rearrange("p h v -> p (h v)"))
-        keep_x1(3)
-        for t in range(PACK - 1):
-            look_up_fd(t, (0, 1))
-        for h in range(2):
-            look_up_fd(PACK - 1, (h,))
-        pairs = z0_pairs[:].rearrange("p g v u -> p g (v u)").bitcast(U32)
-        words = z0_grouped[:].rearrange("p v j -> p (v j)").bitcast(U32).rearrange("p (v g) -> p v g", g=2)
-        interleave(nc.scalar.copy, words, pairs)
-        z1_grouped = [sb([P, HALF_V, PACK], BF16, f"z1_grouped{h}", ("z0_pairs", None)[h]) for h in range(2)]
-        z1_rows = sb([P, PACK, V], F32, "z1_rows", "m2u3_0")
-        for t in range(PACK - 1):
-            look_up_fc(t, (0, 1))
+        for s in range(PACK):
+            scale_z0(s)
+        for s in range(PACK):
+            look_up_fd(s)
+        t_codes = sb([P, 2 * N], U32, "t_codes", "first3")
+        quantize(t_codes[:], t_planes[:], t_grouped[:].rearrange("p d n j -> p (d n j)"))
+        z1_rows = sb([P, PACK, V], F32, "z1_rows", "p1_1")
+        for s in range(PACK - 1):
+            look_up_fc(s, (0, 1))
         for h in range(2):
             look_up_fc(PACK - 1, (h,))
-        interleave(nc.scalar.copy, z1_grouped[1][:, :, :2], z1_rows[:, :2, HALF_V:])
+        for h in range(2):
+            weave_z0(h)
         interleave(nc.scalar.copy, z1_grouped[0][:], z1_rows[:, :, :HALF_V])
-        t_codes = sb([P, 2 * N], U32, "t_codes", "second3_0")
-        quantize(t_codes[:], t_planes[:], t_grouped[:].rearrange("p d n j -> p (d n j)"))
-        interleave(nc.vector.tensor_copy, z1_grouped[1][:, :, 2:], z1_rows[:, 2:, HALF_V:])
-        z0_codes = [sb([P, HALF_V], U32, f"z0_codes{h}", ("second3_1", None)[h]) for h in range(2)]
-        quantize(z0_codes[0][:], z0_planes[0][:], z0_grouped[:, :HALF_V].rearrange("p v j -> p (v j)"))
-        quantize(z1_codes[1][:], z1_planes[1][:], z1_grouped[1][:].rearrange("p v j -> p (v j)"))
-        quantize(z0_codes[1][:], z0_planes[1][:], z0_grouped[:, HALF_V:].rearrange("p v j -> p (v j)"))
-        quantize(z1_codes[0][:], z1_planes[0][:], z1_grouped[0][:].rearrange("p v j -> p (v j)"))
+        interleave(nc.vector.tensor_copy, z1_grouped[1][:], z1_rows[:, :, HALF_V:])
+        quantize_z(0, 1)
+        quantize_z(1, 1)
+        quantize_z(0, 0)
+        quantize_z(1, 0)
         finish(1, nc.scalar.copy, nc.scalar)
         finish(0, nc.vector.tensor_copy, nc.sync)

@@ -14,7 +14,6 @@ U16 = mybir.dt.uint16
 U8 = mybir.dt.uint8
 FP8X4 = mybir.dt.float8_e4m3fn_x4
 MULT = mybir.AluOpType.mult
-ADD = mybir.AluOpType.add
 COPY = mybir.ActivationFunctionType.Copy
 
 P = 128
@@ -60,6 +59,8 @@ def tile_picked_ycin_both_p_kernel(
         nc.vector.memset(table_scales[:].bitcast(I32), 0)
         for o in range(PASSES):
             nc.vector.memset(x_planes[o][:].bitcast(I32), 0)
+        rows = sb([P, H], F32, "rows")
+        nc.gpsimd.memset(rows[:], 0.0)
         make_identity(nc, identity[:])
         for s in range(PACK):
             nc.gpsimd.memset(y[s][:, S:], 0.0)
@@ -78,25 +79,47 @@ def tile_picked_ycin_both_p_kernel(
 
         def load_w(o, half, tag=None):
             w_raw[o, half] = sb([P, PACK, HALF_H], F32, f"w_raw{o}_{half}", tag)
-            rows = w1[512 * o : 512 * (o + 1), HALF_H * half : HALF_H * (half + 1)]
-            nc.sync.dma_start(out=w_raw[o, half][:], in_=rows.rearrange("(p j) c -> p j c", j=PACK))
+            part = w1[512 * o : 512 * (o + 1), HALF_H * half : HALF_H * (half + 1)]
+            nc.sync.dma_start(out=w_raw[o, half][:], in_=part.rearrange("(p j) c -> p j c", j=PACK))
 
         load_w(0, 0)
         nc.sync.dma_start(
             out=table_scales[0:P:4, :].bitcast(I32), in_=x_scales.rearrange("o q c -> (o q) c").bitcast(I32)
         )
         nc.sync.dma_start(offs_sb[:], offs)
-        m1_cols = sb([P, 2, 2], F32, "m1_cols")
-        nc.sync.dma_start(out=m1_cols[:], in_=m1[0].rearrange("(h p d) -> p h d", h=2, d=2))
+        nc.sync.dma_start(out=rows[0:2, :HALF_S], in_=m1[0].rearrange("(h c) -> h c", h=2))
+        nc.sync.dma_start(out=rows[2:3, :V], in_=m2[0:1, :])
+        nc.sync.dma_start(out=rows[3:4, :], in_=unit.rearrange("i o -> o i"))
         load_words(0)
         load_words(1)
 
+        m_turned = bank(4, [P, 2, P], "m_turned")
+        for d in range(2):
+            nc.tensor.transpose(m_turned[:, d, :], rows[:, d:HALF_S:2], identity[:])
+        m_cols = sb([P, 3, 2], F32, "m_cols")
+        nc.scalar.copy(out=m_cols[:], in_=m_turned[:, :, 0:3].rearrange("p d h -> p h d"))
+        unit_turned = bank(5, [P, PACK, P], "unit_turned")
+        for s in range(PACK):
+            nc.tensor.transpose(unit_turned[:, s, :], rows[:, s::PACK], identity[:])
+        unit_sb = sb([P, PACK], F32, "unit_sb")
+        nc.scalar.copy(out=unit_sb[:], in_=unit_turned[:, :, 3])
         m1_spread = bank(3, [P, 2, 2, P], "m1_spread")
         for h in range(2):
             for d in range(2):
-                nc.tensor.transpose(m1_spread[:, h, d, :], m1_cols[:, h, d : d + 1].to_broadcast([P, P]), identity[:])
+                nc.tensor.transpose(m1_spread[:, h, d, :], m_cols[:, h, d : d + 1].to_broadcast([P, P]), identity[:])
         m1_sb = sb([P, S], F32, "m1_sb")
         nc.scalar.copy(out=m1_sb[:].rearrange("p (h v d) -> p h v d", h=2, d=2), in_=m1_spread[:].rearrange("p h d v -> p h v d"))
+        m2_spread = bank(6, [P, 2, P], "m2_spread")
+        for d in range(2):
+            nc.tensor.transpose(m2_spread[:, d, :], m_cols[:, 2, d : d + 1].to_broadcast([P, P]), identity[:])
+        m2u = [sb([P, V], F32, f"m2u{s}") for s in range(PACK)]
+        for s in range(PACK):
+            nc.scalar.activation(
+                out=m2u[s][:].rearrange("p (v d) -> p v d", d=2),
+                in_=m2_spread[:].rearrange("p d v -> p v d"),
+                func=COPY,
+                scale=unit_sb[:, s : s + 1],
+            )
 
         nc.vector.tensor_copy(picked_scales[:], table_scales[:].indirect(offs_sb[:]))
         nc.vector.tensor_copy(x_codes[0][:], table_words[0][:].bitcast(U32).indirect(offs_sb[:]))
@@ -166,11 +189,7 @@ def tile_picked_ycin_both_p_kernel(
         nc.sync.dma_start(fb_sb[:], fb)
         nc.sync.dma_start(fc_sb[:], fc)
         nc.sync.dma_start(fd_sb[:], fd)
-        unit_sb = sb([P, PACK], F32, "unit_sb", "w_raw0_0")
-        nc.sync.dma_start(out=unit_sb[:], in_=unit.rearrange("(p t) o -> p (t o)", t=PACK))
         nc.vector.tensor_copy(x_codes[1][:], table_words[1][:].bitcast(U32).indirect(offs_sb[:]))
-        m2_sb = sb([P, V], F32, "m2_sb", "table_words1")
-        nc.sync.dma_start(out=m2_sb[:], in_=m2)
         cast_w(1, (0,), nc.vector.tensor_copy)
         cast_w(1, (1,), nc.scalar.copy)
         t_raw = [sb([P, PACK, N], F32, f"t_raw{d}", ("w_raw1_0", "picked_scales")[d]) for d in range(2)]
@@ -198,11 +217,6 @@ def tile_picked_ycin_both_p_kernel(
         for t in (2, 3):
             cast_w(1, (t,), nc.scalar.copy)
         look_up_fa(1, "table_words0")
-        t_grouped = sb([P, 2, N, PACK], BF16, "t_grouped")
-        for d in range(2):
-            nc.gpsimd.tensor_scalar(
-                out=t_grouped[:, d], in0=t_raw[d][:].rearrange("p j c -> p c j"), scalar1=1.0, scalar2=0.0, op0=MULT, op1=ADD
-            )
 
         def deal_y(t):
             for u in range(2):
@@ -224,24 +238,33 @@ def tile_picked_ycin_both_p_kernel(
         back = {}
         second = {}
 
-        def look_up_fb(t, tag=None):
-            p1[t] = sb([P, S], F32, f"p1_{t}", tag)
-            nc.vector.tensor_tensor(p1[t][:], y[t][:].indirect(fb_sb[:]), first[t][:], MULT)
+        def look_up_fb(t, halves=(0, 1), tag=None):
+            cols = slice(HALF_S * halves[0], HALF_S * (halves[-1] + 1))
+            product = sb([P, len(halves), HALF_S], F32, f"p1_{t}_{halves[0]}", tag)
+            nc.vector.tensor_tensor(
+                product[:].rearrange("p h j -> p (h j)"),
+                y[t][:].indirect(fb_sb[:, cols.start // 16 : cols.stop // 16]),
+                first[t][:, cols],
+                MULT,
+            )
+            for i, h in enumerate(halves):
+                p1[t, h] = product[:, i, :]
 
-        def turn(t, turn_bank):
-            turned[t] = bank(turn_bank, [P, 2, 2, P], f"turned{t}")
-            for h in range(2):
+        def turn(t, halves, turn_bank):
+            tile = bank(turn_bank, [P, len(halves), 2, P], f"turned{t}_{halves[0]}")
+            for i, h in enumerate(halves):
+                turned[t, h] = tile[:, i]
                 for d in range(2):
-                    nc.tensor.transpose(turned[t][:, h, d, :], p1[t][:, 2 * P * h + d : 2 * P * (h + 1) : 2], identity[:])
+                    nc.tensor.transpose(turned[t, h][:, d, :], p1[t, h][:, d::2], identity[:])
 
         def weigh(t):
             for h in range(2):
                 for d in range(2):
                     nc.scalar.activation(
                         out=weighted[:, h, d, :, t // 2, :],
-                        in_=turned[t][:, h, d, :].rearrange("p (u m) -> p u m", u=2),
+                        in_=turned[t, h][:, d, :].rearrange("p (u m) -> p u m", u=2),
                         func=COPY,
-                        scale=m1_cols[:, h, d : d + 1],
+                        scale=m_cols[:, h, d : d + 1],
                     )
 
         def sum_pairs(t, turn_bank):
@@ -250,7 +273,7 @@ def tile_picked_ycin_both_p_kernel(
                 for d in range(2):
                     nc.tensor.matmul(
                         out=turned[t][:, h, :],
-                        lhsT=p1[t][:, 2 * P * h + d : 2 * P * (h + 1) : 2],
+                        lhsT=p1[t, h][:, d::2],
                         rhs=identity[:],
                         is_transpose=True,
                         start=(d == 0),
@@ -292,7 +315,7 @@ def tile_picked_ycin_both_p_kernel(
 
         def look_up_fd(s, tag=None):
             second[s] = sb([P, V], F32, f"second{s}", tag)
-            nc.vector.tensor_tensor(second[s][:], y_slot[s][:].indirect(fd_sb[:]), m2u[s // 2][:, s % 2, :], MULT)
+            nc.vector.tensor_tensor(second[s][:], y_slot[s][:].indirect(fd_sb[:]), m2u[s][:], MULT)
 
         def look_up_fc(s, halves):
             cols = slice(HALF_V * halves[0], HALF_V * (halves[-1] + 1))
@@ -321,36 +344,30 @@ def tile_picked_ycin_both_p_kernel(
             copy(out=result[h][:], in_=acc[:])
             queue.dma_start(out=out[:, cols], in_=result[h][:])
 
-        m2u = {}
-
-        def scale_m2(g, tag):
-            m2u[g] = sb([P, 2, V], F32, f"m2u{g}", tag)
-            for u in range(2):
-                s = 2 * g + u
-                nc.scalar.activation(out=m2u[g][:, u, :], in_=m2_sb[:], func=COPY, scale=unit_sb[:, s : s + 1])
-
         quantize_w(1, (2,))
         products((1,), 2)
-        look_up_fb(0, "w_grouped1_2")
+        look_up_fb(0, tag="w_grouped1_2")
         quantize_w(1, (3,))
         products((1,), 3)
         empty_y(2)
-        scale_m2(0, "w_grouped1_3")
         empty_y(3)
         look_up_fa(3)
         for t in range(PACK):
             deal_y(t)
         look_up_fb(1)
         sum_pairs(0, 3)
-        turn(1, 2)
+        turn(1, (0, 1), 2)
         look_up_fa(2)
         look_up_fb(2)
         sum_pairs(2, 5)
-        look_up_fb(3)
-        turn(3, 6)
         keep_sums(0)
-        scale_m2(1, "p1_1")
+        for h in range(2):
+            look_up_fb(3, (h,))
+            turn(3, (h,), (6, 3)[h])
         weigh(1)
+        t_grouped = sb([P, 2, N, PACK], BF16, "t_grouped", "first2")
+        for d in range(2):
+            interleave(nc.scalar.copy, t_grouped[:, d], t_raw[d][:])
         keep_sums(2)
         weigh(3)
         for s in range(PACK):
@@ -360,9 +377,7 @@ def tile_picked_ycin_both_p_kernel(
             scale_z0(s)
         for s in range(PACK):
             look_up_fd(s)
-        t_codes = sb([P, 2 * N], U32, "t_codes", "first3")
-        quantize(t_codes[:], t_planes[:], t_grouped[:].rearrange("p d n j -> p (d n j)"))
-        z1_rows = sb([P, PACK, V], F32, "z1_rows", "p1_1")
+        z1_rows = sb([P, PACK, V], F32, "z1_rows", "m2u3")
         for s in range(PACK - 1):
             look_up_fc(s, (0, 1))
         for h in range(2):
@@ -371,6 +386,8 @@ def tile_picked_ycin_both_p_kernel(
             weave_z0(h)
         interleave(nc.scalar.copy, z1_grouped[0][:], z1_rows[:, :, :HALF_V])
         interleave(nc.vector.tensor_copy, z1_grouped[1][:], z1_rows[:, :, HALF_V:])
+        t_codes = sb([P, 2 * N], U32, "t_codes", "second1")
+        quantize(t_codes[:], t_planes[:], t_grouped[:].rearrange("p d n j -> p (d n j)"))
         quantize_z(0, 1)
         quantize_z(1, 1)
         quantize_z(0, 0)

@@ -56,15 +56,15 @@ def tile_picked_ycin_both_p_kernel(
         x1 = [sb([P, V + SPARE], F32, f"x1_{s}") for s in range(PACK)]
         identity = sb([P, P], F32, "identity")
 
+        rows = sb([P, H], F32, "rows")
         nc.vector.memset(table_scales[:].bitcast(I32), 0)
+        nc.vector.memset(rows[:], 0.0)
         for o in range(PASSES):
             nc.vector.memset(x_planes[o][:].bitcast(I32), 0)
-        rows = sb([P, H], F32, "rows")
-        nc.gpsimd.memset(rows[:], 0.0)
         make_identity(nc, identity[:])
         for s in range(PACK):
-            nc.gpsimd.memset(y[s][:, S:], 0.0)
-            nc.gpsimd.memset(x1[s][:, V:], 0.0)
+            nc.vector.memset(y[s][:, S:], 0.0)
+            nc.vector.memset(x1[s][:, V:], 0.0)
 
         def load_words(o):
             nc.sync.dma_start(out=table_words[o][:], in_=x_words[o].rearrange("p c r -> p (c r)").bitcast(I32))
@@ -87,10 +87,10 @@ def tile_picked_ycin_both_p_kernel(
             out=table_scales[0:P:4, :].bitcast(I32), in_=x_scales.rearrange("o q c -> (o q) c").bitcast(I32)
         )
         nc.sync.dma_start(offs_sb[:], offs)
+        load_words(0)
         nc.sync.dma_start(out=rows[0:2, :HALF_S], in_=m1[0].rearrange("(h c) -> h c", h=2))
         nc.sync.dma_start(out=rows[2:3, :V], in_=m2[0:1, :])
         nc.sync.dma_start(out=rows[3:4, :], in_=unit.rearrange("i o -> o i"))
-        load_words(0)
         load_words(1)
 
         m_turned = bank(4, [P, 2, P], "m_turned")

@@ -1,7 +1,6 @@
 from contextlib import ExitStack
 
 import concourse.mybir as mybir
-from concourse.masks import make_identity
 
 K, T, S, H, N, V = 1024, 2048, 512, 512, 128, 256
 FLOPS = 2 * K * H * S + 2 * 2 * H * N * V
@@ -14,6 +13,7 @@ U16 = mybir.dt.uint16
 U8 = mybir.dt.uint8
 FP8X4 = mybir.dt.float8_e4m3fn_x4
 MULT = mybir.AluOpType.mult
+ADD = mybir.AluOpType.add
 COPY = mybir.ActivationFunctionType.Copy
 
 P = 128
@@ -22,7 +22,7 @@ PASSES = K // (P * PACK)
 SPARE = 16
 HALF_S = S // 2
 HALF_V = V // 2
-HALF_H = H // 2
+VECTOR_ROWS = 80
 
 
 def tile_picked_ycin_both_p_kernel(
@@ -32,6 +32,7 @@ def tile_picked_ycin_both_p_kernel(
     with ExitStack() as ctx:
         lists = ctx.enter_context(tc.tile_pool(name="lists", bufs=1))
         keep = ctx.enter_context(tc.tile_pool(name="keep", bufs=1))
+        shared = ctx.enter_context(tc.tile_pool(name="shared", bufs=1))
         psum = ctx.enter_context(tc.psum_pool(name="psum", bufs=1))
 
         def sb(shape, dtype, name, tag=None):
@@ -47,350 +48,222 @@ def tile_picked_ycin_both_p_kernel(
         fd_sb = lists.tile([P, V // 16], U16, name="fd_sb")
 
         table_words = [sb([P, T], I32, f"table_words{o}") for o in range(PASSES)]
-        table_scales = sb([P, T], U8, "table_scales")
-        picked_scales = sb([P, S], U8, "picked_scales")
-        x_planes = [sb([P, S], U8, f"x_planes{o}") for o in range(PASSES)]
+        table_scales = sb([P, PASSES, T], U8, "table_scales")
+        picked_scales = sb([P, PASSES, S], U8, "picked_scales")
+        x_planes = sb([P, PASSES, S], U8, "x_planes")
         x_codes = [sb([P, S], U32, f"x_codes{o}") for o in range(PASSES)]
-        y = [sb([P, S + SPARE], F32, f"y{t}") for t in range(PACK)]
-        y_slot = [sb([P, S], F32, f"y_slot{s}") for s in range(PACK)]
+        w_raw = [sb([P, PACK, H], F32, f"w_raw{o}") for o in range(PASSES)]
+        y = {0: sb([P, S + SPARE], F32, "y0")}
         x1 = [sb([P, V + SPARE], F32, f"x1_{s}") for s in range(PACK)]
-        identity = sb([P, P], F32, "identity")
 
-        rows = sb([P, H], F32, "rows")
-        nc.vector.memset(table_scales[:].bitcast(I32), 0)
-        nc.vector.memset(rows[:], 0.0)
-        for o in range(PASSES):
-            nc.vector.memset(x_planes[o][:].bitcast(I32), 0)
-        make_identity(nc, identity[:])
+        nc.vector.memset(table_scales[: P - 16].rearrange("p o c -> p (o c)").bitcast(I32), 0)
+        nc.vector.memset(x_planes[:].rearrange("p o c -> p (o c)").bitcast(I32), 0)
+        nc.vector.memset(y[0][:, S:], 0.0)
         for s in range(PACK):
-            nc.vector.memset(y[s][:, S:], 0.0)
-            nc.vector.memset(x1[s][:, V:], 0.0)
+            nc.scalar.activation(out=x1[s][:, V:], in_=y[0][:, S:], func=COPY)
 
         def load_words(o):
             nc.sync.dma_start(out=table_words[o][:], in_=x_words[o].rearrange("p c r -> p (c r)").bitcast(I32))
 
-        def move_scales(o, r):
-            nc.sync.dma_start(
-                out=x_planes[o][r:P:32, :].bitcast(I32),
-                in_=picked_scales[64 * o + 4 * r : 64 * (o + 1) : 16, :].bitcast(I32),
-            )
+        def load_w(o, rows):
+            part = w1[512 * o : 512 * (o + 1), :].rearrange("(p j) c -> p j c", j=PACK)
+            nc.sync.dma_start(out=w_raw[o][:, rows, :], in_=part[:, rows, :])
 
-        w_raw = {}
-
-        def load_w(o, half, tag=None):
-            w_raw[o, half] = sb([P, PACK, HALF_H], F32, f"w_raw{o}_{half}", tag)
-            part = w1[512 * o : 512 * (o + 1), HALF_H * half : HALF_H * (half + 1)]
-            nc.sync.dma_start(out=w_raw[o, half][:], in_=part.rearrange("(p j) c -> p j c", j=PACK))
-
-        load_w(0, 0)
         nc.sync.dma_start(
-            out=table_scales[0:P:4, :].bitcast(I32), in_=x_scales.rearrange("o q c -> (o q) c").bitcast(I32)
+            out=table_scales[P - 16 :].bitcast(I32), in_=x_scales.rearrange("o q c -> q o c").bitcast(I32)
         )
         nc.sync.dma_start(offs_sb[:], offs)
-        load_words(0)
-        nc.sync.dma_start(out=rows[0:2, :HALF_S], in_=m1[0].rearrange("(h c) -> h c", h=2))
-        nc.sync.dma_start(out=rows[2:3, :V], in_=m2[0:1, :])
-        nc.sync.dma_start(out=rows[3:4, :], in_=unit.rearrange("i o -> o i"))
-        load_words(1)
-
-        m_turned = bank(4, [P, 2, P], "m_turned")
-        for d in range(2):
-            nc.tensor.transpose(m_turned[:, d, :], rows[:, d:HALF_S:2], identity[:])
-        m_cols = sb([P, 3, 2], F32, "m_cols")
-        nc.scalar.copy(out=m_cols[:], in_=m_turned[:, :, 0:3].rearrange("p d h -> p h d"))
-        unit_turned = bank(5, [P, PACK, P], "unit_turned")
-        for s in range(PACK):
-            nc.tensor.transpose(unit_turned[:, s, :], rows[:, s::PACK], identity[:])
-        unit_sb = sb([P, PACK], F32, "unit_sb")
-        nc.scalar.copy(out=unit_sb[:], in_=unit_turned[:, :, 3])
-        m1_spread = bank(3, [P, 2, 2, P], "m1_spread")
-        for h in range(2):
-            for d in range(2):
-                nc.tensor.transpose(m1_spread[:, h, d, :], m_cols[:, h, d : d + 1].to_broadcast([P, P]), identity[:])
-        m1_sb = sb([P, S], F32, "m1_sb")
-        nc.scalar.copy(out=m1_sb[:].rearrange("p (h v d) -> p h v d", h=2, d=2), in_=m1_spread[:].rearrange("p h d v -> p h v d"))
-        m2_spread = bank(6, [P, 2, P], "m2_spread")
-        for d in range(2):
-            nc.tensor.transpose(m2_spread[:, d, :], m_cols[:, 2, d : d + 1].to_broadcast([P, P]), identity[:])
-        m2u = [sb([P, V], F32, f"m2u{s}") for s in range(PACK)]
-        for s in range(PACK):
-            nc.scalar.activation(
-                out=m2u[s][:].rearrange("p (v d) -> p v d", d=2),
-                in_=m2_spread[:].rearrange("p d v -> p v d"),
-                func=COPY,
-                scale=unit_sb[:, s : s + 1],
-            )
-
-        nc.vector.tensor_copy(picked_scales[:], table_scales[:].indirect(offs_sb[:]))
-        nc.vector.tensor_copy(x_codes[0][:], table_words[0][:].bitcast(U32).indirect(offs_sb[:]))
-        for r in range(4):
-            move_scales(0, r)
-        load_w(1, 0)
-        load_w(0, 1)
-        for r in range(4):
-            move_scales(1, r)
+        load_w(0, slice(0, 4))
         nc.sync.dma_start(fa_sb[:], fa)
-
-        w_grouped = {}
-        w_mx = {}
-
-        def cast_w(o, tiles, copy):
-            t0, n = tiles[0], len(tiles)
-            w_grouped[o, t0] = sb([P, 2 * n, P // 2, PACK], BF16, f"w_grouped{o}_{t0}")
-            src = w_raw[o, t0 // 2][:].rearrange("p j (m s) -> p m s j", s=PACK)
-            s0 = 2 * (t0 % 2)
-            copy(out=w_grouped[o, t0][:].rearrange("p s m j -> p m s j"), in_=src[:, :, s0 : s0 + 2 * n])
-
-        def interleave(copy, dst, src):
-            copy(out=dst, in_=src.rearrange("p j c -> p c j"))
+        load_words(0)
+        load_w(1, slice(0, 4))
+        for o in range(PASSES):
+            nc.vector.tensor_copy(picked_scales[:, o, :], table_scales[:, o, :].indirect(offs_sb[:]))
+        for r in range(4):
+            nc.sync.dma_start(
+                out=x_planes[r:P:32].rearrange("p o c -> p (o c)").bitcast(I32),
+                in_=picked_scales[P - 16 + r : P : 4].rearrange("p o c -> p (o c)").bitcast(I32),
+            )
+        load_words(1)
+        t_raw = shared.tile([P, 2, PACK, N], F32, name="t_raw", offset=1024)
+        for d, tm in enumerate((t1, t2)):
+            nc.sync.dma_start(out=t_raw[:, d], in_=tm.rearrange("(p j) n -> p j n", j=PACK))
+        m1_sb = sb([P, S], F32, "m1_sb")
+        m2_sb = sb([P, V], F32, "m2_sb")
+        unit_sb = sb([P, PACK], F32, "unit_sb")
+        nc.sync.dma_start(out=m1_sb[:], in_=m1)
+        nc.sync.dma_start(fb_sb[:], fb)
+        nc.sync.dma_start(fd_sb[:], fd)
+        nc.sync.dma_start(out=m2_sb[:], in_=m2)
+        nc.sync.dma_start(out=unit_sb[:], in_=unit.rearrange("(p s) o -> p (s o)", s=PACK))
+        nc.sync.dma_start(fc_sb[:], fc)
 
         def quantize(codes, planes, grouped):
             nc.vector.quantize_mx(out=codes.bitcast(FP8X4), scales=planes, in_=grouped)
 
-        def quantize_w(o, tiles, tag=None):
-            t0, n = tiles[0], len(tiles)
-            codes = sb([P, n * P], U32, f"w_codes{o}_{t0}", tag)
-            planes = sb([P, n * P], U8, f"w_planes{o}_{t0}")
-            quantize(codes[:], planes[:], w_grouped[o, t0][:].rearrange("p s m j -> p (s m j)"))
-            for i, t in enumerate(tiles):
-                w_mx[o, t] = (codes[:, P * i : P * (i + 1)], planes[:, P * i : P * (i + 1)])
+        w_grouped = [sb([P, PACK, P, PACK], BF16, f"w_grouped{o}") for o in range(PASSES)]
+        w_codes = [sb([P, H], U32, f"w_codes{o}") for o in range(PASSES)]
+        w_planes = [sb([P, H], U8, f"w_planes{o}") for o in range(PASSES)]
+
+        def cast_w(o, rows, copy):
+            src = w_raw[o][:].rearrange("p j (m s) -> p m s j", s=PACK)
+            copy(out=w_grouped[o][:].rearrange("p s m j -> p m s j")[:, rows], in_=src[:, rows])
+
+        def quantize_w(o):
+            quantize(w_codes[o][:], w_planes[o][:], w_grouped[o][:].rearrange("p s m j -> p (s m j)"))
 
         low, high, whole = slice(0, HALF_S), slice(HALF_S, S), slice(0, S)
-        pieces = [(0, low), (0, high), (1, whole), (2, low), (2, high), (3, whole)]
-        y_acc = {}
+        pieces = [(0, low), (0, high), (1, whole), (2, whole), (3, whole)]
+        y_acc = [bank(b, [P, cols.stop - cols.start], f"y_acc{b}") for b, (s, cols) in enumerate(pieces)]
 
-        def products(passes, tile):
-            for b, (t, cols) in enumerate(pieces):
-                for o in passes if t == tile else ():
-                    if o == 0:
-                        y_acc[b] = bank(b % 3, [P, cols.stop - cols.start], f"y_acc{b}")
-                    nc.tensor.matmul_mx(
-                        out=y_acc[b][:],
-                        lhsT=w_mx[o, t][0].bitcast(FP8X4),
-                        lhsT_scale=w_mx[o, t][1],
-                        rhs=x_codes[o][:, cols].bitcast(FP8X4),
-                        rhs_scale=x_planes[o][:, cols],
-                        start=(o == 0),
-                        stop=(o == PASSES - 1),
-                    )
-
-        def empty_y(tile):
-            for b, (t, cols) in enumerate(pieces):
-                if t == tile:
-                    copy = nc.vector.tensor_copy if b == 0 else nc.scalar.copy
-                    copy(out=y[t][:, cols], in_=y_acc[b][:])
-
-        cast_w(0, (0,), nc.scalar.copy)
-        cast_w(0, (1,), nc.scalar.copy)
-        for t in (0, 1):
-            quantize_w(0, (t,), ("table_scales", None)[t])
-            products((0,), t)
-        load_w(1, 1, "table_words0")
-        nc.sync.dma_start(fb_sb[:], fb)
-        nc.sync.dma_start(fc_sb[:], fc)
-        nc.sync.dma_start(fd_sb[:], fd)
-        nc.vector.tensor_copy(x_codes[1][:], table_words[1][:].bitcast(U32).indirect(offs_sb[:]))
-        cast_w(1, (0,), nc.vector.tensor_copy)
-        cast_w(1, (1,), nc.scalar.copy)
-        t_raw = [sb([P, PACK, N], F32, f"t_raw{d}", ("w_raw1_0", "picked_scales")[d]) for d in range(2)]
-        for d, tm in enumerate((t1, t2)):
-            nc.sync.dma_start(out=t_raw[d][:], in_=tm.rearrange("(p j) n -> p j n", j=PACK))
-        for t in (0, 1):
-            quantize_w(1, (t,))
-            products((1,), t)
-        first = {}
-
-        def look_up_fa(t, tag=None):
-            first[t] = sb([P, S], F32, f"first{t}", tag)
-            if t % 2 == 0:
-                nc.vector.tensor_tensor(first[t][:], y[t][:].indirect(fa_sb[:]), m1_sb[:], MULT)
-            else:
-                nc.scalar.activation(out=first[t][:], in_=y[t][:].indirect(fa_sb[:]), func=COPY)
-
-        for t in (0, 1):
-            empty_y(t)
-        cast_w(0, (2, 3), nc.vector.tensor_copy)
-        quantize_w(0, (2, 3), "w_codes1_0")
-        for t in (2, 3):
-            products((0,), t)
-        look_up_fa(0, "w_raw0_1")
-        for t in (2, 3):
-            cast_w(1, (t,), nc.scalar.copy)
-        look_up_fa(1, "table_words0")
-
-        def deal_y(t):
-            for u in range(2):
-                nc.sync.dma_start(
-                    out=y_slot[2 * (t % 2) + u][64 * (t // 2) : 64 * (t // 2 + 1), :], in_=y[t][64 * u : 64 * (u + 1), :S]
+        def products(o):
+            for b, (s, cols) in enumerate(pieces):
+                nc.tensor.matmul_mx(
+                    out=y_acc[b][:],
+                    lhsT=w_codes[o][:, P * s : P * (s + 1)].bitcast(FP8X4),
+                    lhsT_scale=w_planes[o][:, P * s : P * (s + 1)],
+                    rhs=x_codes[o][:, cols].bitcast(FP8X4),
+                    rhs_scale=x_planes[:, o, cols],
+                    start=(o == 0),
+                    stop=(o == PASSES - 1),
                 )
 
-        z0_pairs = sb([P, 2, V, 2], BF16, "z0_pairs")
-        z0_grouped = [sb([P, HALF_V, PACK], BF16, f"z0_grouped{h}") for h in range(2)]
-        z1_grouped = [sb([P, HALF_V, PACK], BF16, f"z1_grouped{h}") for h in range(2)]
+        cast_w(0, slice(0, P), nc.scalar.copy)
+        nc.vector.tensor_copy(x_codes[0][:], table_words[0][:].bitcast(U32).indirect(offs_sb[:]))
+        quantize_w(0)
+        products(0)
+        cast_w(1, slice(0, VECTOR_ROWS), nc.vector.tensor_copy)
+        cast_w(1, slice(VECTOR_ROWS, P), nc.scalar.copy)
+        quantize_w(1)
+        for cols in (low, high):
+            nc.vector.tensor_copy(
+                x_codes[1][:, cols], table_words[1][:].bitcast(U32).indirect(offs_sb[:, cols.start // 16 : cols.stop // 16])
+            )
+        products(1)
+
+        def empty_y(b, copy):
+            s, cols = pieces[b]
+            copy(out=y[s][:, cols], in_=y_acc[b][:])
+
+        t_grouped = sb([P, 2, N, PACK], BF16, "t_grouped")
+        t_codes = sb([P, 2 * N], U32, "t_codes")
         t_planes = sb([P, 2 * N], U8, "t_planes")
-        z_codes = {}
+        for d in range(2):
+            nc.scalar.copy(out=t_grouped[:, d], in_=t_raw[:, d].rearrange("p j c -> p c j"))
+        empty_y(0, nc.vector.tensor_copy)
+        empty_y(1, nc.vector.tensor_copy)
+        for s in range(1, PACK):
+            y[s] = shared.tile([P, S + SPARE], F32, name=f"y{s}", offset=4 * (S + SPARE) * (s - 1))
+            nc.scalar.activation(out=y[s][:, S:], in_=y[0][:, S:], func=COPY)
+
+        first = {}
+        weighted = {}
+        p1 = {}
+        x1_fc = sb([P, PACK, V], F32, "x1_fc")
+        second = sb([P, PACK, V], F32, "second")
+        z0_pairs = sb([P, 2, V, 2], BF16, "z0_pairs")
+        z_grouped = [[sb([P, HALF_V, PACK], BF16, f"z{d}_grouped{h}") for h in range(2)] for d in range(2)]
+        z_codes = [[sb([P, HALF_V], U32, f"z{d}_codes{h}") for h in range(2)] for d in range(2)]
         z_planes = [[sb([P, HALF_V], U8, f"z{d}_planes{h}") for h in range(2)] for d in range(2)]
         result = [sb([P, HALF_V], F32, f"result{h}") for h in range(2)]
-        summed = sb([P, 2, 2, 2, P // 2], F32, "summed")
-        weighted = sb([P, 2, 2, 2, 2, P // 2], F32, "weighted")
-        p1 = {}
-        turned = {}
-        back = {}
-        second = {}
 
-        def look_up_fb(t, halves=(0, 1), tag=None):
-            cols = slice(HALF_S * halves[0], HALF_S * (halves[-1] + 1))
-            product = sb([P, len(halves), HALF_S], F32, f"p1_{t}_{halves[0]}", tag)
-            nc.vector.tensor_tensor(
-                product[:].rearrange("p h j -> p (h j)"),
-                y[t][:].indirect(fb_sb[:, cols.start // 16 : cols.stop // 16]),
-                first[t][:, cols],
-                MULT,
+        def look_up_fa(s):
+            first[s] = sb([P, S], F32, f"first{s}")
+            nc.scalar.activation(out=first[s][:], in_=y[s][:].indirect(fa_sb[:]), func=COPY)
+
+        def weigh(s):
+            weighted[s] = sb([P, S], F32, f"weighted{s}")
+            if s == 0:
+                nc.vector.tensor_tensor(weighted[s][:], y[s][:].indirect(fa_sb[:]), m1_sb[:], MULT)
+            else:
+                nc.vector.tensor_tensor(weighted[s][:], first[s][:], m1_sb[:], MULT)
+
+        def look_up_fb(s):
+            p1[s] = sb([P, V, 2], F32, f"p1_{s}")
+            nc.vector.tensor_tensor(p1[s][:].rearrange("p v d -> p (v d)"), y[s][:].indirect(fb_sb[:]), weighted[s][:], MULT)
+
+        def sum_pairs(s):
+            nc.vector.tensor_tensor(x1[s][:, :V], p1[s][:, :, 0], p1[s][:, :, 1], ADD)
+
+        def look_up_fd(s):
+            nc.scalar.activation(out=y_fd[:, s, :], in_=y[s][:].indirect(fd_sb[:]), func=COPY)
+
+        def look_up_fc(s):
+            nc.scalar.activation(out=x1_fc[:, s, :], in_=x1[s][:].indirect(fc_sb[:]), func=COPY)
+
+        def weigh_second(s):
+            nc.vector.scalar_tensor_tensor(
+                out=second[:, s, :], in0=y_fd[:, s, :], scalar=unit_sb[:, s : s + 1], in1=m2_sb[:], op0=MULT, op1=MULT
             )
-            for i, h in enumerate(halves):
-                p1[t, h] = product[:, i, :]
-
-        def turn(t, halves, turn_bank):
-            tile = bank(turn_bank, [P, len(halves), 2, P], f"turned{t}_{halves[0]}")
-            for i, h in enumerate(halves):
-                turned[t, h] = tile[:, i]
-                for d in range(2):
-                    nc.tensor.transpose(turned[t, h][:, d, :], p1[t, h][:, d::2], identity[:])
-
-        def weigh(t):
-            for h in range(2):
-                for d in range(2):
-                    nc.scalar.activation(
-                        out=weighted[:, h, d, :, t // 2, :],
-                        in_=turned[t, h][:, d, :].rearrange("p (u m) -> p u m", u=2),
-                        func=COPY,
-                        scale=m_cols[:, h, d : d + 1],
-                    )
-
-        def sum_pairs(t, turn_bank):
-            turned[t] = bank(turn_bank, [P, 2, P], f"turned{t}")
-            for h in range(2):
-                for d in range(2):
-                    nc.tensor.matmul(
-                        out=turned[t][:, h, :],
-                        lhsT=p1[t, h][:, d::2],
-                        rhs=identity[:],
-                        is_transpose=True,
-                        start=(d == 0),
-                        stop=(d == 1),
-                    )
-
-        def keep_sums(t):
-            nc.scalar.copy(out=summed[:, :, :, t // 2, :], in_=turned[t][:].rearrange("p h (u m) -> p h u m", u=2))
-
-        def turn_back(s, back_bank):
-            back[s] = bank(back_bank, [P, 2, P], f"back{s}")
-            for h in range(2):
-                terms = [summed[:, h, s]] if s < 2 else [weighted[:, h, d, s % 2] for d in range(2)]
-                for i, term in enumerate(terms):
-                    nc.tensor.matmul(
-                        out=back[s][:, h, :],
-                        lhsT=term.rearrange("p a m -> p (a m)"),
-                        rhs=identity[:],
-                        is_transpose=True,
-                        start=(i == 0),
-                        stop=(i == len(terms) - 1),
-                    )
-
-        def keep_x1(s):
-            nc.scalar.copy(out=x1[s][:, :V], in_=back[s][:].rearrange("p h v -> p (h v)"))
 
         def scale_z0(s):
-            nc.scalar.activation(
-                out=z0_pairs[:, s // 2, :, s % 2],
-                in_=back[s][:].rearrange("p h v -> p (h v)"),
-                func=COPY,
-                scale=unit_sb[:, s : s + 1],
-            )
+            nc.scalar.activation(out=z0_pairs[:, s // 2, :, s % 2], in_=x1[s][:, :V], func=COPY, scale=unit_sb[:, s : s + 1])
 
         def weave_z0(h):
             pairs = z0_pairs[:].rearrange("p g v u -> p g (v u)").bitcast(U32)[:, :, HALF_V * h : HALF_V * (h + 1)]
-            words = z0_grouped[h][:].rearrange("p v j -> p (v j)").bitcast(U32).rearrange("p (v g) -> p v g", g=2)
-            interleave(nc.scalar.copy, words, pairs)
+            words = z_grouped[0][h][:].rearrange("p v j -> p (v j)").bitcast(U32).rearrange("p (v g) -> p v g", g=2)
+            nc.scalar.copy(out=words, in_=pairs.rearrange("p g v -> p v g"))
 
-        def look_up_fd(s, tag=None):
-            second[s] = sb([P, V], F32, f"second{s}", tag)
-            nc.vector.tensor_tensor(second[s][:], y_slot[s][:].indirect(fd_sb[:]), m2u[s][:], MULT)
-
-        def look_up_fc(s, halves):
-            cols = slice(HALF_V * halves[0], HALF_V * (halves[-1] + 1))
+        def weave_z1(h):
+            cols = slice(HALF_V * h, HALF_V * (h + 1))
             nc.vector.tensor_tensor(
-                z1_rows[:, s, cols], x1[s][:].indirect(fc_sb[:, cols.start // 16 : cols.stop // 16]), second[s][:, cols], MULT
+                z_grouped[1][h][:].rearrange("p (c i) s -> p c s i", i=4),
+                x1_fc[:, :, cols].rearrange("p s (c i) -> p c s i", i=4),
+                second[:, :, cols].rearrange("p s (c i) -> p c s i", i=4),
+                MULT,
             )
 
         def quantize_z(d, h):
-            grouped = (z0_grouped, z1_grouped)[d][h]
-            z_codes[d, h] = sb([P, HALF_V], U32, f"z{d}_codes{h}", f"second{2 + h}" if d == 0 else None)
-            quantize(z_codes[d, h][:], z_planes[d][h][:], grouped[:].rearrange("p v j -> p (v j)"))
+            quantize(z_codes[d][h][:], z_planes[d][h][:], z_grouped[d][h][:].rearrange("p v j -> p (v j)"))
 
         def finish(h, copy, queue):
             cols = slice(HALF_V * h, HALF_V * (h + 1))
-            acc = bank(3 + h, [P, HALF_V], f"out_acc{h}")
-            for d in range(2):
+            acc = bank(5 + h, [P, HALF_V], f"out_acc{h}")
+            for d in (1, 0):
                 nc.tensor.matmul_mx(
                     out=acc[:],
                     lhsT=t_codes[:, N * d : N * (d + 1)].bitcast(FP8X4),
                     lhsT_scale=t_planes[:, N * d : N * (d + 1)],
-                    rhs=z_codes[d, h][:].bitcast(FP8X4),
+                    rhs=z_codes[d][h][:].bitcast(FP8X4),
                     rhs_scale=z_planes[d][h][:],
-                    start=(d == 0),
-                    stop=(d == 1),
+                    start=(d == 1),
+                    stop=(d == 0),
                 )
             copy(out=result[h][:], in_=acc[:])
             queue.dma_start(out=out[:, cols], in_=result[h][:])
 
-        quantize_w(1, (2,))
-        products((1,), 2)
-        look_up_fb(0, tag="w_grouped1_2")
-        quantize_w(1, (3,))
-        products((1,), 3)
-        empty_y(2)
-        empty_y(3)
-        look_up_fa(3)
-        for t in range(PACK):
-            deal_y(t)
-        look_up_fb(1)
-        sum_pairs(0, 3)
-        turn(1, (0, 1), 2)
+        empty_y(2, nc.scalar.copy)
+        empty_y(3, nc.scalar.copy)
+        look_up_fa(1)
+        empty_y(4, nc.scalar.copy)
         look_up_fa(2)
-        look_up_fb(2)
-        sum_pairs(2, 5)
-        keep_sums(0)
-        for h in range(2):
-            look_up_fb(3, (h,))
-            turn(3, (h,), (6, 3)[h])
-        weigh(1)
-        t_grouped = sb([P, 2, N, PACK], BF16, "t_grouped", "first2")
-        for d in range(2):
-            interleave(nc.scalar.copy, t_grouped[:, d], t_raw[d][:])
-        keep_sums(2)
-        weigh(3)
+        look_up_fa(3)
+        weigh(0)
+        quantize(t_codes[:], t_planes[:], t_grouped[:].rearrange("p d n j -> p (d n j)"))
         for s in range(PACK):
-            turn_back(s, (0, 1, 4, 7)[s])
-            keep_x1(s)
-        for s in range(PACK):
-            scale_z0(s)
+            look_up_fb(s)
+            if s + 1 < PACK:
+                weigh(s + 1)
+                sum_pairs(s)
+        y_fd = sb([P, PACK, V], F32, "y_fd", "first1")
         for s in range(PACK):
             look_up_fd(s)
-        z1_rows = sb([P, PACK, V], F32, "z1_rows", "m2u3")
+        weigh_second(0)
+        sum_pairs(PACK - 1)
+        for s in range(1, PACK):
+            weigh_second(s)
         for s in range(PACK - 1):
-            look_up_fc(s, (0, 1))
+            look_up_fc(s)
+        scale_z0(0)
+        look_up_fc(PACK - 1)
+        for s in range(1, PACK):
+            scale_z0(s)
         for h in range(2):
-            look_up_fc(PACK - 1, (h,))
+            weave_z1(h)
         for h in range(2):
             weave_z0(h)
-        interleave(nc.scalar.copy, z1_grouped[0][:], z1_rows[:, :, :HALF_V])
-        interleave(nc.vector.tensor_copy, z1_grouped[1][:], z1_rows[:, :, HALF_V:])
-        t_codes = sb([P, 2 * N], U32, "t_codes", "second1")
-        quantize(t_codes[:], t_planes[:], t_grouped[:].rearrange("p d n j -> p (d n j)"))
-        quantize_z(0, 1)
-        quantize_z(1, 1)
-        quantize_z(0, 0)
-        quantize_z(1, 0)
-        finish(1, nc.scalar.copy, nc.scalar)
-        finish(0, nc.vector.tensor_copy, nc.sync)
+        for d in (1, 0):
+            for h in range(2):
+                quantize_z(d, h)
+        finish(0, nc.scalar.copy, nc.scalar)
+        finish(1, nc.vector.tensor_copy, nc.sync)

@@ -23,6 +23,9 @@ SPARE = 16
 HALF_S = S // 2
 HALF_V = V // 2
 VECTOR_ROWS = 80
+LAST = 0
+EARLY = (1, 2, 3)
+ORDER = EARLY + (LAST,)
 
 
 def tile_picked_ycin_both_p_kernel(
@@ -53,30 +56,35 @@ def tile_picked_ycin_both_p_kernel(
         x_planes = sb([P, PASSES, S], U8, "x_planes")
         x_codes = [sb([P, S], U32, f"x_codes{o}") for o in range(PASSES)]
         w_raw = [sb([P, PACK, H], F32, f"w_raw{o}") for o in range(PASSES)]
-        y = {0: sb([P, S + SPARE], F32, "y0")}
-        x1 = [sb([P, V + SPARE], F32, f"x1_{s}") for s in range(PACK)]
+        first_slot = ORDER[0]
+        y = {first_slot: sb([P, S + SPARE], F32, "y_first")}
+        zeros = y[first_slot][:, S:]
+        x1 = {s: sb([P, V + SPARE], F32, f"x1_{s}") for s in EARLY}
+        x1_all = sb([P, PACK * V], F32, "x1_all")
 
         nc.vector.memset(table_scales[: P - 16].rearrange("p o c -> p (o c)").bitcast(I32), 0)
         nc.vector.memset(x_planes[:].rearrange("p o c -> p (o c)").bitcast(I32), 0)
-        nc.vector.memset(y[0][:, S:], 0.0)
-        for s in range(PACK):
-            nc.scalar.activation(out=x1[s][:, V:], in_=y[0][:, S:], func=COPY)
+        nc.vector.memset(zeros, 0.0)
+        y_floor = shared.tile([P, PACK - 1, S + SPARE], F32, name="y_floor", offset=0)
+        nc.vector.memset(y_floor[:, :, S:], 0.0)
+        for s in EARLY:
+            nc.scalar.activation(out=x1[s][:, V:], in_=zeros, func=COPY)
 
         def load_words(o):
             nc.sync.dma_start(out=table_words[o][:], in_=x_words[o].rearrange("p c r -> p (c r)").bitcast(I32))
 
-        def load_w(o, rows):
+        def load_w(o):
             part = w1[512 * o : 512 * (o + 1), :].rearrange("(p j) c -> p j c", j=PACK)
-            nc.sync.dma_start(out=w_raw[o][:, rows, :], in_=part[:, rows, :])
+            nc.sync.dma_start(out=w_raw[o][:], in_=part)
 
         nc.sync.dma_start(
             out=table_scales[P - 16 :].bitcast(I32), in_=x_scales.rearrange("o q c -> q o c").bitcast(I32)
         )
         nc.sync.dma_start(offs_sb[:], offs)
-        load_w(0, slice(0, 4))
+        load_w(0)
         nc.sync.dma_start(fa_sb[:], fa)
         load_words(0)
-        load_w(1, slice(0, 4))
+        load_w(1)
         for o in range(PASSES):
             nc.vector.tensor_copy(picked_scales[:, o, :], table_scales[:, o, :].indirect(offs_sb[:]))
         for r in range(4):
@@ -85,17 +93,17 @@ def tile_picked_ycin_both_p_kernel(
                 in_=picked_scales[P - 16 + r : P : 4].rearrange("p o c -> p (o c)").bitcast(I32),
             )
         load_words(1)
-        t_raw = shared.tile([P, 2, PACK, N], F32, name="t_raw", offset=1024)
-        for d, tm in enumerate((t1, t2)):
-            nc.sync.dma_start(out=t_raw[:, d], in_=tm.rearrange("(p j) n -> p j n", j=PACK))
+        t_raw = shared.tile([P, 2, 2, PACK, N], F32, name="t_raw", offset=0)
         m1_sb = sb([P, S], F32, "m1_sb")
         m2_sb = sb([P, V], F32, "m2_sb")
         unit_sb = sb([P, PACK], F32, "unit_sb")
-        nc.sync.dma_start(out=m1_sb[:], in_=m1)
         nc.sync.dma_start(fb_sb[:], fb)
+        for d, tm in enumerate((t1, t2)):
+            nc.sync.dma_start(out=t_raw[:, d, 0], in_=tm.rearrange("(p j) n -> p j n", j=PACK))
+        nc.sync.dma_start(out=m1_sb[:], in_=m1)
+        nc.sync.dma_start(out=unit_sb[:], in_=unit.rearrange("(p s) o -> p (s o)", s=PACK))
         nc.sync.dma_start(fd_sb[:], fd)
         nc.sync.dma_start(out=m2_sb[:], in_=m2)
-        nc.sync.dma_start(out=unit_sb[:], in_=unit.rearrange("(p s) o -> p (s o)", s=PACK))
         nc.sync.dma_start(fc_sb[:], fc)
 
         def quantize(codes, planes, grouped):
@@ -113,25 +121,26 @@ def tile_picked_ycin_both_p_kernel(
             quantize(w_codes[o][:], w_planes[o][:], w_grouped[o][:].rearrange("p s m j -> p (s m j)"))
 
         low, high, whole = slice(0, HALF_S), slice(HALF_S, S), slice(0, S)
-        pieces = [(0, low), (0, high), (1, whole), (2, whole), (3, whole)]
+        pieces = [(first_slot, low), (first_slot, high)] + [(s, whole) for s in ORDER[1:]]
         y_acc = [bank(b, [P, cols.stop - cols.start], f"y_acc{b}") for b, (s, cols) in enumerate(pieces)]
 
-        def products(o):
-            for b, (s, cols) in enumerate(pieces):
-                nc.tensor.matmul_mx(
-                    out=y_acc[b][:],
-                    lhsT=w_codes[o][:, P * s : P * (s + 1)].bitcast(FP8X4),
-                    lhsT_scale=w_planes[o][:, P * s : P * (s + 1)],
-                    rhs=x_codes[o][:, cols].bitcast(FP8X4),
-                    rhs_scale=x_planes[:, o, cols],
-                    start=(o == 0),
-                    stop=(o == PASSES - 1),
-                )
+        def product(o, b, cols, stop):
+            s, held = pieces[b]
+            nc.tensor.matmul_mx(
+                out=y_acc[b][:, cols.start - held.start : cols.stop - held.start],
+                lhsT=w_codes[o][:, P * s : P * (s + 1)].bitcast(FP8X4),
+                lhsT_scale=w_planes[o][:, P * s : P * (s + 1)],
+                rhs=x_codes[o][:, cols].bitcast(FP8X4),
+                rhs_scale=x_planes[:, o, cols],
+                start=(o == 0),
+                stop=stop,
+            )
 
         cast_w(0, slice(0, P), nc.scalar.copy)
         nc.vector.tensor_copy(x_codes[0][:], table_words[0][:].bitcast(U32).indirect(offs_sb[:]))
         quantize_w(0)
-        products(0)
+        for b, (s, cols) in enumerate(pieces):
+            product(0, b, cols, False)
         cast_w(1, slice(0, VECTOR_ROWS), nc.vector.tensor_copy)
         cast_w(1, slice(VECTOR_ROWS, P), nc.scalar.copy)
         quantize_w(1)
@@ -139,7 +148,12 @@ def tile_picked_ycin_both_p_kernel(
             nc.vector.tensor_copy(
                 x_codes[1][:, cols], table_words[1][:].bitcast(U32).indirect(offs_sb[:, cols.start // 16 : cols.stop // 16])
             )
-        products(1)
+        product(1, 0, low, True)
+        product(1, 2, low, False)
+        product(1, 1, high, True)
+        product(1, 2, high, True)
+        product(1, 3, whole, True)
+        product(1, 4, whole, True)
 
         def empty_y(b, copy):
             s, cols = pieces[b]
@@ -149,69 +163,77 @@ def tile_picked_ycin_both_p_kernel(
         t_codes = sb([P, 2 * N], U32, "t_codes")
         t_planes = sb([P, 2 * N], U8, "t_planes")
         for d in range(2):
-            nc.scalar.copy(out=t_grouped[:, d], in_=t_raw[:, d].rearrange("p j c -> p c j"))
+            nc.scalar.copy(out=t_grouped[:, d], in_=t_raw[:, d, 0].rearrange("p j c -> p c j"))
         empty_y(0, nc.vector.tensor_copy)
         empty_y(1, nc.vector.tensor_copy)
-        for s in range(1, PACK):
-            y[s] = shared.tile([P, S + SPARE], F32, name=f"y{s}", offset=4 * (S + SPARE) * (s - 1))
-            nc.scalar.activation(out=y[s][:, S:], in_=y[0][:, S:], func=COPY)
+        for n, s in enumerate(ORDER[1:]):
+            y[s] = shared.tile([P, S + SPARE], F32, name=f"y{s}", offset=4 * (S + SPARE) * n)
 
-        first = {}
-        weighted = {}
-        p1 = {}
+        y_fa = {s: sb([P, S], F32, f"y_fa{s}") for s in ORDER[1:]}
+        y_fa[first_slot] = shared.tile([P, S], F32, name="y_fa_first", offset=4 * (S + SPARE) * 3)
+        y_fb = {s: sb([P, S], F32, f"y_fb{s}") for s in ORDER}
+        p1 = {s: sb([P, V, 2], F32, f"p1_{s}") for s in ORDER}
         x1_fc = sb([P, PACK, V], F32, "x1_fc")
         second = sb([P, PACK, V], F32, "second")
-        z0_pairs = sb([P, 2, V, 2], BF16, "z0_pairs")
         z_grouped = [[sb([P, HALF_V, PACK], BF16, f"z{d}_grouped{h}") for h in range(2)] for d in range(2)]
         z_codes = [[sb([P, HALF_V], U32, f"z{d}_codes{h}") for h in range(2)] for d in range(2)]
         z_planes = [[sb([P, HALF_V], U8, f"z{d}_planes{h}") for h in range(2)] for d in range(2)]
         result = [sb([P, HALF_V], F32, f"result{h}") for h in range(2)]
 
         def look_up_fa(s):
-            first[s] = sb([P, S], F32, f"first{s}")
-            nc.scalar.activation(out=first[s][:], in_=y[s][:].indirect(fa_sb[:]), func=COPY)
-
-        def weigh(s):
-            weighted[s] = sb([P, S], F32, f"weighted{s}")
-            if s == 0:
-                nc.vector.tensor_tensor(weighted[s][:], y[s][:].indirect(fa_sb[:]), m1_sb[:], MULT)
-            else:
-                nc.vector.tensor_tensor(weighted[s][:], first[s][:], m1_sb[:], MULT)
+            nc.scalar.activation(out=y_fa[s][:], in_=y[s][:].indirect(fa_sb[:]), func=COPY)
 
         def look_up_fb(s):
-            p1[s] = sb([P, V, 2], F32, f"p1_{s}")
-            nc.vector.tensor_tensor(p1[s][:].rearrange("p v d -> p (v d)"), y[s][:].indirect(fb_sb[:]), weighted[s][:], MULT)
+            nc.vector.tensor_tensor(y_fb[s][:], y[s][:].indirect(fb_sb[:]), m1_sb[:], MULT)
+
+        def multiply(s):
+            nc.vector.scalar_tensor_tensor(
+                out=p1[s][:].rearrange("p v d -> p (v d)"),
+                in0=y_fa[s][:],
+                scalar=unit_sb[:, s : s + 1],
+                in1=y_fb[s][:],
+                op0=MULT,
+                op1=MULT,
+            )
 
         def sum_pairs(s):
-            nc.vector.tensor_tensor(x1[s][:, :V], p1[s][:, :, 0], p1[s][:, :, 1], ADD)
+            rows = x1_all[:, V * s : V * (s + 1)]
+            if s == LAST:
+                nc.vector.tensor_tensor(rows, p1[s][:, :, 0], p1[s][:, :, 1], ADD)
+            else:
+                nc.vector.tensor_tensor(x1[s][:, :V], p1[s][:, :, 0], p1[s][:, :, 1], ADD)
+                nc.sync.dma_start(out=rows, in_=x1[s][:, :V])
 
         def look_up_fd(s):
             nc.scalar.activation(out=y_fd[:, s, :], in_=y[s][:].indirect(fd_sb[:]), func=COPY)
 
+        def look_up_fd_weighed(s):
+            nc.vector.tensor_tensor(second[:, s, :], y[s][:].indirect(fd_sb[:]), m2_sb[:], MULT)
+
+        def weigh_second(s):
+            nc.vector.tensor_tensor(second[:, s, :], y_fd[:, s, :], m2_sb[:], MULT)
+
         def look_up_fc(s):
             nc.scalar.activation(out=x1_fc[:, s, :], in_=x1[s][:].indirect(fc_sb[:]), func=COPY)
 
-        def weigh_second(s):
-            nc.vector.scalar_tensor_tensor(
-                out=second[:, s, :], in0=y_fd[:, s, :], scalar=unit_sb[:, s : s + 1], in1=m2_sb[:], op0=MULT, op1=MULT
+        def look_up_fc_last(h):
+            nc.scalar.activation(
+                out=x1_fc[:, LAST, HALF_V * h : HALF_V * (h + 1)],
+                in_=x1_all[:].indirect(fc_sb[:, HALF_V // 16 * h : HALF_V // 16 * (h + 1)]),
+                func=COPY,
             )
 
-        def scale_z0(s):
-            nc.scalar.activation(out=z0_pairs[:, s // 2, :, s % 2], in_=x1[s][:, :V], func=COPY, scale=unit_sb[:, s : s + 1])
+        def woven(rows, h):
+            return rows[:, :, HALF_V * h : HALF_V * (h + 1)].rearrange("p s (c i) -> p c s i", i=4)
+
+        def grouped(d, h):
+            return z_grouped[d][h][:].rearrange("p (c i) s -> p c s i", i=4)
 
         def weave_z0(h):
-            pairs = z0_pairs[:].rearrange("p g v u -> p g (v u)").bitcast(U32)[:, :, HALF_V * h : HALF_V * (h + 1)]
-            words = z_grouped[0][h][:].rearrange("p v j -> p (v j)").bitcast(U32).rearrange("p (v g) -> p v g", g=2)
-            nc.scalar.copy(out=words, in_=pairs.rearrange("p g v -> p v g"))
+            nc.scalar.copy(out=grouped(0, h), in_=woven(x1_all[:].rearrange("p (s v) -> p s v", s=PACK), h))
 
         def weave_z1(h):
-            cols = slice(HALF_V * h, HALF_V * (h + 1))
-            nc.vector.tensor_tensor(
-                z_grouped[1][h][:].rearrange("p (c i) s -> p c s i", i=4),
-                x1_fc[:, :, cols].rearrange("p s (c i) -> p c s i", i=4),
-                second[:, :, cols].rearrange("p s (c i) -> p c s i", i=4),
-                MULT,
-            )
+            nc.vector.tensor_tensor(grouped(1, h), woven(x1_fc[:], h), woven(second[:], h), MULT)
 
         def quantize_z(d, h):
             quantize(z_codes[d][h][:], z_planes[d][h][:], z_grouped[d][h][:].rearrange("p v j -> p (v j)"))
@@ -232,38 +254,44 @@ def tile_picked_ycin_both_p_kernel(
             copy(out=result[h][:], in_=acc[:])
             queue.dma_start(out=out[:, cols], in_=result[h][:])
 
+        a, b, c, e = ORDER
         empty_y(2, nc.scalar.copy)
+        look_up_fa(a)
+        look_up_fa(b)
         empty_y(3, nc.scalar.copy)
-        look_up_fa(1)
+        look_up_fa(c)
         empty_y(4, nc.scalar.copy)
-        look_up_fa(2)
-        look_up_fa(3)
-        weigh(0)
+        look_up_fa(e)
+        look_up_fb(a)
+        look_up_fb(b)
+        multiply(a)
+        multiply(b)
+        look_up_fb(c)
+        sum_pairs(a)
+        sum_pairs(b)
+        multiply(c)
+        look_up_fd_weighed(a)
+        sum_pairs(c)
+        look_up_fb(e)
         quantize(t_codes[:], t_planes[:], t_grouped[:].rearrange("p d n j -> p (d n j)"))
-        for s in range(PACK):
-            look_up_fb(s)
-            if s + 1 < PACK:
-                weigh(s + 1)
-                sum_pairs(s)
-        y_fd = sb([P, PACK, V], F32, "y_fd", "first1")
-        for s in range(PACK):
+        multiply(e)
+        y_fd = sb([P, PACK, V], F32, "y_fd", f"y_fa{c}")
+        for s in (b, c, e):
             look_up_fd(s)
-        weigh_second(0)
-        sum_pairs(PACK - 1)
-        for s in range(1, PACK):
-            weigh_second(s)
-        for s in range(PACK - 1):
+        for s in EARLY:
             look_up_fc(s)
-        scale_z0(0)
-        look_up_fc(PACK - 1)
-        for s in range(1, PACK):
-            scale_z0(s)
+        weigh_second(b)
+        sum_pairs(e)
+        weigh_second(c)
+        weigh_second(e)
+        for h in range(2):
+            look_up_fc_last(h)
         for h in range(2):
             weave_z1(h)
         for h in range(2):
             weave_z0(h)
-        for d in (1, 0):
-            for h in range(2):
+        for h in range(2):
+            for d in (1, 0):
                 quantize_z(d, h)
         finish(0, nc.scalar.copy, nc.scalar)
         finish(1, nc.vector.tensor_copy, nc.sync)

@@ -24,7 +24,7 @@ HALF_S = S // 2
 HALF_V = V // 2
 VECTOR_ROWS = 80
 LAST = 0
-EARLY = (1, 2, 3)
+EARLY = (3, 2, 1)
 ORDER = EARLY + (LAST,)
 
 
@@ -97,9 +97,9 @@ def tile_picked_ycin_both_p_kernel(
         m1_sb = sb([P, S], F32, "m1_sb")
         m2_sb = sb([P, V], F32, "m2_sb")
         unit_sb = sb([P, PACK], F32, "unit_sb")
-        nc.sync.dma_start(fb_sb[:], fb)
         for d, tm in enumerate((t1, t2)):
             nc.sync.dma_start(out=t_raw[:, d, 0], in_=tm.rearrange("(p j) n -> p j n", j=PACK))
+        nc.sync.dma_start(fb_sb[:], fb)
         nc.sync.dma_start(out=m1_sb[:], in_=m1)
         nc.sync.dma_start(out=unit_sb[:], in_=unit.rearrange("(p s) o -> p (s o)", s=PACK))
         nc.sync.dma_start(fd_sb[:], fd)
@@ -121,7 +121,9 @@ def tile_picked_ycin_both_p_kernel(
             quantize(w_codes[o][:], w_planes[o][:], w_grouped[o][:].rearrange("p s m j -> p (s m j)"))
 
         low, high, whole = slice(0, HALF_S), slice(HALF_S, S), slice(0, S)
-        pieces = [(first_slot, low), (first_slot, high)] + [(s, whole) for s in ORDER[1:]]
+        third, fourth = slice(HALF_S, HALF_S + S // 4), slice(S - S // 4, S)
+        pieces = [(first_slot, low), (first_slot, third), (first_slot, fourth)]
+        pieces = pieces + [(ORDER[1], low), (ORDER[1], high)] + [(s, whole) for s in ORDER[2:]]
         y_acc = [bank(b, [P, cols.stop - cols.start], f"y_acc{b}") for b, (s, cols) in enumerate(pieces)]
 
         def product(o, b, cols, stop):
@@ -144,40 +146,48 @@ def tile_picked_ycin_both_p_kernel(
         cast_w(1, slice(0, VECTOR_ROWS), nc.vector.tensor_copy)
         cast_w(1, slice(VECTOR_ROWS, P), nc.scalar.copy)
         quantize_w(1)
-        for cols in (low, high):
+        for cols in (low, third, fourth):
             nc.vector.tensor_copy(
                 x_codes[1][:, cols], table_words[1][:].bitcast(U32).indirect(offs_sb[:, cols.start // 16 : cols.stop // 16])
             )
         product(1, 0, low, True)
-        product(1, 2, low, False)
-        product(1, 1, high, True)
-        product(1, 2, high, True)
-        product(1, 3, whole, True)
-        product(1, 4, whole, True)
+        product(1, 3, low, True)
+        product(1, 1, third, True)
+        product(1, 2, fourth, True)
+        product(1, 4, high, True)
+        product(1, 5, whole, True)
+        product(1, 6, whole, True)
 
         def empty_y(b, copy):
             s, cols = pieces[b]
             copy(out=y[s][:, cols], in_=y_acc[b][:])
 
-        t_grouped = sb([P, 2, N, PACK], BF16, "t_grouped")
-        t_codes = sb([P, 2 * N], U32, "t_codes")
-        t_planes = sb([P, 2 * N], U8, "t_planes")
+        t_grouped = [sb([P, N, PACK], BF16, f"t_grouped{d}") for d in range(2)]
+        t_planes = [sb([P, N], U8, f"t_planes{d}") for d in range(2)]
+        t_codes = {}
+
+        def quantize_t(d, tag=None):
+            t_codes[d] = sb([P, N], U32, f"t_codes{d}", tag)
+            quantize(t_codes[d][:], t_planes[d][:], t_grouped[d][:].rearrange("p n j -> p (n j)"))
+
         for d in range(2):
-            nc.scalar.copy(out=t_grouped[:, d], in_=t_raw[:, d, 0].rearrange("p j c -> p c j"))
+            nc.scalar.copy(out=t_grouped[d][:], in_=t_raw[:, d, 0].rearrange("p j c -> p c j"))
         empty_y(0, nc.vector.tensor_copy)
         empty_y(1, nc.vector.tensor_copy)
+        empty_y(2, nc.vector.tensor_copy)
+        quantize_t(0)
         for n, s in enumerate(ORDER[1:]):
             y[s] = shared.tile([P, S + SPARE], F32, name=f"y{s}", offset=4 * (S + SPARE) * n)
 
         y_fa = {s: sb([P, S], F32, f"y_fa{s}") for s in ORDER[1:]}
         y_fa[first_slot] = shared.tile([P, S], F32, name="y_fa_first", offset=4 * (S + SPARE) * 3)
-        y_fb = {s: sb([P, S], F32, f"y_fb{s}") for s in ORDER}
+        y_fb = {s: sb([P, S], F32, f"y_fb{s}") for s in ORDER[1:3]}
+        y_fb[first_slot] = sb([P, S], F32, "y_fb_first", "t_grouped0")
         p1 = {s: sb([P, V, 2], F32, f"p1_{s}") for s in ORDER}
         x1_fc = sb([P, PACK, V], F32, "x1_fc")
-        second = sb([P, PACK, V], F32, "second")
-        z_grouped = [[sb([P, HALF_V, PACK], BF16, f"z{d}_grouped{h}") for h in range(2)] for d in range(2)]
-        z_codes = [[sb([P, HALF_V], U32, f"z{d}_codes{h}") for h in range(2)] for d in range(2)]
-        z_planes = [[sb([P, HALF_V], U8, f"z{d}_planes{h}") for h in range(2)] for d in range(2)]
+        z_grouped = [sb([P, 2, HALF_V, PACK], BF16, f"z_grouped{h}") for h in range(2)]
+        z_codes = [sb([P, 2, HALF_V], U32, f"z_codes{h}") for h in range(2)]
+        z_planes = [sb([P, 2, HALF_V], U8, f"z_planes{h}") for h in range(2)]
         result = [sb([P, HALF_V], F32, f"result{h}") for h in range(2)]
 
         def look_up_fa(s):
@@ -186,23 +196,23 @@ def tile_picked_ycin_both_p_kernel(
         def look_up_fb(s):
             nc.vector.tensor_tensor(y_fb[s][:], y[s][:].indirect(fb_sb[:]), m1_sb[:], MULT)
 
-        def multiply(s):
+        def multiply(s, cols=whole):
             nc.vector.scalar_tensor_tensor(
-                out=p1[s][:].rearrange("p v d -> p (v d)"),
-                in0=y_fa[s][:],
+                out=p1[s][:].rearrange("p v d -> p (v d)")[:, cols],
+                in0=y_fa[s][:, cols],
                 scalar=unit_sb[:, s : s + 1],
-                in1=y_fb[s][:],
+                in1=y_fb[s][:, cols],
                 op0=MULT,
                 op1=MULT,
             )
 
         def sum_pairs(s):
-            rows = x1_all[:, V * s : V * (s + 1)]
-            if s == LAST:
-                nc.vector.tensor_tensor(rows, p1[s][:, :, 0], p1[s][:, :, 1], ADD)
-            else:
-                nc.vector.tensor_tensor(x1[s][:, :V], p1[s][:, :, 0], p1[s][:, :, 1], ADD)
-                nc.sync.dma_start(out=rows, in_=x1[s][:, :V])
+            nc.vector.tensor_tensor(x1[s][:, :V], p1[s][:, :, 0], p1[s][:, :, 1], ADD)
+            nc.sync.dma_start(out=x1_all[:, V * s : V * (s + 1)], in_=x1[s][:, :V])
+
+        def sum_pairs_last(h):
+            cols = slice(HALF_V * h, HALF_V * (h + 1))
+            nc.vector.tensor_tensor(x1_all[:, cols], p1[LAST][:, cols, 0], p1[LAST][:, cols, 1], ADD)
 
         def look_up_fd(s):
             nc.scalar.activation(out=y_fd[:, s, :], in_=y[s][:].indirect(fd_sb[:]), func=COPY)
@@ -210,8 +220,10 @@ def tile_picked_ycin_both_p_kernel(
         def look_up_fd_weighed(s):
             nc.vector.tensor_tensor(second[:, s, :], y[s][:].indirect(fd_sb[:]), m2_sb[:], MULT)
 
-        def weigh_second(s):
-            nc.vector.tensor_tensor(second[:, s, :], y_fd[:, s, :], m2_sb[:], MULT)
+        def weigh_second(h):
+            cols = slice(HALF_V * h, HALF_V * (h + 1))
+            spread = m2_sb[:, cols].unsqueeze(1).to_broadcast([P, PACK - 1, HALF_V])
+            nc.vector.tensor_tensor(second[:, : PACK - 1, cols], y_fd[:, :, cols], spread, MULT)
 
         def look_up_fc(s):
             nc.scalar.activation(out=x1_fc[:, s, :], in_=x1[s][:].indirect(fc_sb[:]), func=COPY)
@@ -227,7 +239,7 @@ def tile_picked_ycin_both_p_kernel(
             return rows[:, :, HALF_V * h : HALF_V * (h + 1)].rearrange("p s (c i) -> p c s i", i=4)
 
         def grouped(d, h):
-            return z_grouped[d][h][:].rearrange("p (c i) s -> p c s i", i=4)
+            return z_grouped[h][:, d].rearrange("p (c i) s -> p c s i", i=4)
 
         def weave_z0(h):
             nc.scalar.copy(out=grouped(0, h), in_=woven(x1_all[:].rearrange("p (s v) -> p s v", s=PACK), h))
@@ -235,19 +247,23 @@ def tile_picked_ycin_both_p_kernel(
         def weave_z1(h):
             nc.vector.tensor_tensor(grouped(1, h), woven(x1_fc[:], h), woven(second[:], h), MULT)
 
-        def quantize_z(d, h):
-            quantize(z_codes[d][h][:], z_planes[d][h][:], z_grouped[d][h][:].rearrange("p v j -> p (v j)"))
+        def quantize_z(h, depths):
+            quantize(
+                z_codes[h][:, depths].rearrange("p d v -> p (d v)"),
+                z_planes[h][:, depths].rearrange("p d v -> p (d v)"),
+                z_grouped[h][:, depths].rearrange("p d v j -> p (d v j)"),
+            )
 
         def finish(h, copy, queue):
             cols = slice(HALF_V * h, HALF_V * (h + 1))
-            acc = bank(5 + h, [P, HALF_V], f"out_acc{h}")
+            acc = bank(h, [P, HALF_V], f"out_acc{h}")
             for d in (1, 0):
                 nc.tensor.matmul_mx(
                     out=acc[:],
-                    lhsT=t_codes[:, N * d : N * (d + 1)].bitcast(FP8X4),
-                    lhsT_scale=t_planes[:, N * d : N * (d + 1)],
-                    rhs=z_codes[d][h][:].bitcast(FP8X4),
-                    rhs_scale=z_planes[d][h][:],
+                    lhsT=t_codes[d][:].bitcast(FP8X4),
+                    lhsT_scale=t_planes[d][:],
+                    rhs=z_codes[h][:, d].bitcast(FP8X4),
+                    rhs_scale=z_planes[h][:, d],
                     start=(d == 1),
                     stop=(d == 0),
                 )
@@ -255,43 +271,47 @@ def tile_picked_ycin_both_p_kernel(
             queue.dma_start(out=out[:, cols], in_=result[h][:])
 
         a, b, c, e = ORDER
-        empty_y(2, nc.scalar.copy)
-        look_up_fa(a)
-        look_up_fa(b)
         empty_y(3, nc.scalar.copy)
-        look_up_fa(c)
         empty_y(4, nc.scalar.copy)
+        look_up_fa(a)
+        empty_y(5, nc.scalar.copy)
+        look_up_fa(b)
+        empty_y(6, nc.scalar.copy)
+        look_up_fa(c)
         look_up_fa(e)
         look_up_fb(a)
         look_up_fb(b)
         multiply(a)
-        multiply(b)
         look_up_fb(c)
+        multiply(b)
         sum_pairs(a)
-        sum_pairs(b)
         multiply(c)
-        look_up_fd_weighed(a)
+        sum_pairs(b)
         sum_pairs(c)
+        y_fb[e] = sb([P, S], F32, "y_fb_last", f"p1_{b}")
         look_up_fb(e)
-        quantize(t_codes[:], t_planes[:], t_grouped[:].rearrange("p d n j -> p (d n j)"))
-        multiply(e)
-        y_fd = sb([P, PACK, V], F32, "y_fd", f"y_fa{c}")
+        quantize_t(1, f"p1_{c}")
+        multiply(e, low)
+        multiply(e, high)
+        for h in range(2):
+            sum_pairs_last(h)
+        y_fd = sb([P, PACK - 1, V], F32, "y_fd", f"y_fa{c}")
+        second = sb([P, PACK, V], F32, "second", f"y_fa{e}")
         for s in (b, c, e):
             look_up_fd(s)
         for s in EARLY:
             look_up_fc(s)
-        weigh_second(b)
-        sum_pairs(e)
-        weigh_second(c)
-        weigh_second(e)
+        look_up_fd_weighed(a)
+        for h in range(2):
+            weigh_second(h)
         for h in range(2):
             look_up_fc_last(h)
         for h in range(2):
             weave_z1(h)
         for h in range(2):
             weave_z0(h)
-        for h in range(2):
-            for d in (1, 0):
-                quantize_z(d, h)
+        quantize_z(0, slice(0, 2))
+        quantize_z(1, slice(1, 2))
+        quantize_z(1, slice(0, 1))
         finish(0, nc.scalar.copy, nc.scalar)
         finish(1, nc.vector.tensor_copy, nc.sync)

@@ -57,16 +57,17 @@ def tile_picked_ycin_both_p_kernel(
         x_codes = [sb([P, S], U32, f"x_codes{o}") for o in range(PASSES)]
         w_raw = [sb([P, PACK, H], F32, f"w_raw{o}") for o in range(PASSES)]
         first_slot = ORDER[0]
-        y = {first_slot: sb([P, S + SPARE], F32, "y_first")}
+        y = {s: sb([P, S + SPARE], F32, f"y{s}") for s in ORDER if s != ORDER[2]}
+        y_floor = shared.tile([P, SPARE], F32, name="y_floor", offset=4 * S)
         zeros = y[first_slot][:, S:]
         x1 = {s: sb([P, V + SPARE], F32, f"x1_{s}") for s in EARLY}
         x1_all = sb([P, PACK * V], F32, "x1_all")
 
         nc.vector.memset(table_scales[: P - 16].rearrange("p o c -> p (o c)").bitcast(I32), 0)
         nc.vector.memset(x_planes[:].rearrange("p o c -> p (o c)").bitcast(I32), 0)
-        nc.vector.memset(zeros, 0.0)
-        y_floor = shared.tile([P, PACK - 1, S + SPARE], F32, name="y_floor", offset=0)
-        nc.vector.memset(y_floor[:, :, S:], 0.0)
+        for s in y:
+            nc.vector.memset(y[s][:, S:], 0.0)
+        nc.vector.memset(y_floor[:], 0.0)
         for s in EARLY:
             nc.scalar.activation(out=x1[s][:, V:], in_=zeros, func=COPY)
 
@@ -77,7 +78,7 @@ def tile_picked_ycin_both_p_kernel(
             part = w1[512 * o : 512 * (o + 1), :].rearrange("(p j) c -> p j c", j=PACK)
             nc.sync.dma_start(out=w_raw[o][:], in_=part)
 
-        nc.sync.dma_start(
+        nc.scalar.dma_start(
             out=table_scales[P - 16 :].bitcast(I32), in_=x_scales.rearrange("o q c -> q o c").bitcast(I32)
         )
         nc.sync.dma_start(offs_sb[:], offs)
@@ -93,12 +94,12 @@ def tile_picked_ycin_both_p_kernel(
                 in_=picked_scales[P - 16 + r : P : 4].rearrange("p o c -> p (o c)").bitcast(I32),
             )
         load_words(1)
-        t_raw = shared.tile([P, 2, 2, PACK, N], F32, name="t_raw", offset=0)
+        t_raw = [sb([P, PACK, N], F32, f"t_raw{d}") for d in range(2)]
         m1_sb = sb([P, S], F32, "m1_sb")
         m2_sb = sb([P, V], F32, "m2_sb")
         unit_sb = sb([P, PACK], F32, "unit_sb")
         for d, tm in enumerate((t1, t2)):
-            nc.sync.dma_start(out=t_raw[:, d, 0], in_=tm.rearrange("(p j) n -> p j n", j=PACK))
+            nc.sync.dma_start(out=t_raw[d][:], in_=tm.rearrange("(p j) n -> p j n", j=PACK))
         nc.sync.dma_start(fb_sb[:], fb)
         nc.sync.dma_start(out=m1_sb[:], in_=m1)
         nc.sync.dma_start(out=unit_sb[:], in_=unit.rearrange("(p s) o -> p (s o)", s=PACK))
@@ -110,7 +111,7 @@ def tile_picked_ycin_both_p_kernel(
             nc.vector.quantize_mx(out=codes.bitcast(FP8X4), scales=planes, in_=grouped)
 
         w_grouped = [sb([P, PACK, P, PACK], BF16, f"w_grouped{o}") for o in range(PASSES)]
-        w_codes = [sb([P, H], U32, f"w_codes{o}") for o in range(PASSES)]
+        w_codes = [sb([P, H], U32, "w_codes0"), shared.tile([P, H], U32, name="w_codes1", offset=0, align_bytes=64)]
         w_planes = [sb([P, H], U8, f"w_planes{o}") for o in range(PASSES)]
 
         def cast_w(o, rows, copy):
@@ -162,27 +163,18 @@ def tile_picked_ycin_both_p_kernel(
             s, cols = pieces[b]
             copy(out=y[s][:, cols], in_=y_acc[b][:])
 
-        t_grouped = [sb([P, N, PACK], BF16, f"t_grouped{d}") for d in range(2)]
-        t_planes = [sb([P, N], U8, f"t_planes{d}") for d in range(2)]
-        t_codes = {}
-
-        def quantize_t(d, tag=None):
-            t_codes[d] = sb([P, N], U32, f"t_codes{d}", tag)
-            quantize(t_codes[d][:], t_planes[d][:], t_grouped[d][:].rearrange("p n j -> p (n j)"))
+        t_grouped = sb([P, 2, N, PACK], BF16, "t_grouped")
+        t_planes = sb([P, 2, N], U8, "t_planes")
 
         for d in range(2):
-            nc.scalar.copy(out=t_grouped[d][:], in_=t_raw[:, d, 0].rearrange("p j c -> p c j"))
+            nc.gpsimd.tensor_scalar(t_grouped[:, d], t_raw[d][:].rearrange("p j c -> p c j"), 1.0, 0.0, MULT, ADD)
         empty_y(0, nc.vector.tensor_copy)
         empty_y(1, nc.vector.tensor_copy)
         empty_y(2, nc.vector.tensor_copy)
-        quantize_t(0)
-        for n, s in enumerate(ORDER[1:]):
-            y[s] = shared.tile([P, S + SPARE], F32, name=f"y{s}", offset=4 * (S + SPARE) * n)
 
-        y_fa = {s: sb([P, S], F32, f"y_fa{s}") for s in ORDER[1:]}
-        y_fa[first_slot] = shared.tile([P, S], F32, name="y_fa_first", offset=4 * (S + SPARE) * 3)
-        y_fb = {s: sb([P, S], F32, f"y_fb{s}") for s in ORDER[1:3]}
-        y_fb[first_slot] = sb([P, S], F32, "y_fb_first", "t_grouped0")
+        y[ORDER[2]] = shared.tile([P, S + SPARE], F32, name="y_third", offset=0)
+        y_fa = {s: sb([P, S], F32, f"y_fa{s}") for s in ORDER}
+        y_fb = {s: sb([P, S], F32, f"y_fb{s}") for s in ORDER[:3]}
         p1 = {s: sb([P, V, 2], F32, f"p1_{s}") for s in ORDER}
         x1_fc = sb([P, PACK, V], F32, "x1_fc")
         z_grouped = [sb([P, 2, HALF_V, PACK], BF16, f"z_grouped{h}") for h in range(2)]
@@ -260,8 +252,8 @@ def tile_picked_ycin_both_p_kernel(
             for d in (1, 0):
                 nc.tensor.matmul_mx(
                     out=acc[:],
-                    lhsT=t_codes[d][:].bitcast(FP8X4),
-                    lhsT_scale=t_planes[d][:],
+                    lhsT=t_codes[:, d].bitcast(FP8X4),
+                    lhsT_scale=t_planes[:, d],
                     rhs=z_codes[h][:, d].bitcast(FP8X4),
                     rhs_scale=z_planes[h][:, d],
                     start=(d == 1),
@@ -290,7 +282,12 @@ def tile_picked_ycin_both_p_kernel(
         sum_pairs(c)
         y_fb[e] = sb([P, S], F32, "y_fb_last", f"p1_{b}")
         look_up_fb(e)
-        quantize_t(1, f"p1_{c}")
+        t_codes = sb([P, 2, N], U32, "t_codes", f"p1_{c}")
+        quantize(
+            t_codes[:].rearrange("p d n -> p (d n)"),
+            t_planes[:].rearrange("p d n -> p (d n)"),
+            t_grouped[:].rearrange("p d n j -> p (d n j)"),
+        )
         multiply(e, low)
         multiply(e, high)
         for h in range(2):

@@ -83,7 +83,6 @@ def tile_picked_ycin_both_p_kernel(
         )
         nc.sync.dma_start(offs_sb[:], offs)
         load_w(0)
-        nc.sync.dma_start(fa_sb[:], fa)
         load_words(0)
         load_w(1)
         for o in range(PASSES):
@@ -94,6 +93,7 @@ def tile_picked_ycin_both_p_kernel(
                 in_=picked_scales[P - 16 + r : P : 4].rearrange("p o c -> p (o c)").bitcast(I32),
             )
         load_words(1)
+        nc.sync.dma_start(fa_sb[:], fa)
         t_raw = [sb([P, PACK, N], F32, f"t_raw{d}") for d in range(2)]
         m1_sb = sb([P, S], F32, "m1_sb")
         m2_sb = sb([P, V], F32, "m2_sb")
@@ -170,7 +170,6 @@ def tile_picked_ycin_both_p_kernel(
             nc.gpsimd.tensor_scalar(t_grouped[:, d], t_raw[d][:].rearrange("p j c -> p c j"), 1.0, 0.0, MULT, ADD)
         empty_y(0, nc.vector.tensor_copy)
         empty_y(1, nc.vector.tensor_copy)
-        empty_y(2, nc.vector.tensor_copy)
 
         y[ORDER[2]] = shared.tile([P, S + SPARE], F32, name="y_third", offset=0)
         y_fa = {s: sb([P, S], F32, f"y_fa{s}") for s in ORDER}
@@ -264,6 +263,7 @@ def tile_picked_ycin_both_p_kernel(
 
         a, b, c, e = ORDER
         empty_y(3, nc.scalar.copy)
+        empty_y(2, nc.scalar.copy)
         empty_y(4, nc.scalar.copy)
         look_up_fa(a)
         empty_y(5, nc.scalar.copy)

@@ -22,7 +22,7 @@ PASSES = K // (P * PACK)
 SPARE = 16
 HALF_S = S // 2
 HALF_V = V // 2
-VECTOR_ROWS = 80
+VECTOR_ROWS = 72
 LAST = 0
 EARLY = (3, 2, 1)
 ORDER = EARLY + (LAST,)

from contextlib import ExitStack

import concourse.mybir as mybir

K, T, S, H, N, V = 1024, 2048, 512, 512, 128, 256
FLOPS = 2 * K * H * S + 2 * 2 * H * N * V

F32 = mybir.dt.float32
BF16 = mybir.dt.bfloat16
I32 = mybir.dt.int32
U32 = mybir.dt.uint32
U16 = mybir.dt.uint16
U8 = mybir.dt.uint8
FP8X4 = mybir.dt.float8_e4m3fn_x4
MULT = mybir.AluOpType.mult
ADD = mybir.AluOpType.add
COPY = mybir.ActivationFunctionType.Copy

P = 128
PACK = 4
PASSES = K // (P * PACK)
SPARE = 16
HALF_S = S // 2
HALF_V = V // 2
VECTOR_ROWS = 72
LAST = 0
EARLY = (3, 2, 1)
ORDER = EARLY + (LAST,)


def tile_picked_ycin_both_p_kernel(
    tc, x_words, x_scales, w1, m1, m2, unit, t1, t2, offs, fa, fb, fc, fd, out
):
    nc = tc.nc
    with ExitStack() as ctx:
        lists = ctx.enter_context(tc.tile_pool(name="lists", bufs=1))
        keep = ctx.enter_context(tc.tile_pool(name="keep", bufs=1))
        shared = ctx.enter_context(tc.tile_pool(name="shared", bufs=1))
        psum = ctx.enter_context(tc.psum_pool(name="psum", bufs=1))

        def sb(shape, dtype, name, tag=None):
            return keep.tile(shape, dtype, name=name, tag=tag or name, align_bytes=64)

        def bank(b, shape, name):
            return psum.tile(shape, F32, name=name, tag=f"bank{b}")

        offs_sb = lists.tile([P, S // 16], U16, name="offs_sb")
        fa_sb = lists.tile([P, S // 16], U16, name="fa_sb")
        fb_sb = lists.tile([P, S // 16], U16, name="fb_sb")
        fc_sb = lists.tile([P, V // 16], U16, name="fc_sb")
        fd_sb = lists.tile([P, V // 16], U16, name="fd_sb")

        table_words = [sb([P, T], I32, f"table_words{o}") for o in range(PASSES)]
        table_scales = sb([P, PASSES, T], U8, "table_scales")
        picked_scales = sb([P, PASSES, S], U8, "picked_scales")
        x_planes = sb([P, PASSES, S], U8, "x_planes")
        x_codes = [sb([P, S], U32, f"x_codes{o}") for o in range(PASSES)]
        w_raw = [sb([P, PACK, H], F32, f"w_raw{o}") for o in range(PASSES)]
        first_slot = ORDER[0]
        y = {s: sb([P, S + SPARE], F32, f"y{s}") for s in ORDER if s != ORDER[2]}
        y_floor = shared.tile([P, SPARE], F32, name="y_floor", offset=4 * S)
        zeros = y[first_slot][:, S:]
        x1 = {s: sb([P, V + SPARE], F32, f"x1_{s}") for s in EARLY}
        x1_all = sb([P, PACK * V], F32, "x1_all")

        nc.vector.memset(table_scales[: P - 16].rearrange("p o c -> p (o c)").bitcast(I32), 0)
        nc.vector.memset(x_planes[:].rearrange("p o c -> p (o c)").bitcast(I32), 0)
        for s in y:
            nc.vector.memset(y[s][:, S:], 0.0)
        nc.vector.memset(y_floor[:], 0.0)
        for s in EARLY:
            nc.scalar.activation(out=x1[s][:, V:], in_=zeros, func=COPY)

        def load_words(o):
            nc.sync.dma_start(out=table_words[o][:], in_=x_words[o].rearrange("p c r -> p (c r)").bitcast(I32))

        def load_w(o):
            part = w1[512 * o : 512 * (o + 1), :].rearrange("(p j) c -> p j c", j=PACK)
            nc.sync.dma_start(out=w_raw[o][:], in_=part)

        nc.scalar.dma_start(
            out=table_scales[P - 16 :].bitcast(I32), in_=x_scales.rearrange("o q c -> q o c").bitcast(I32)
        )
        nc.sync.dma_start(offs_sb[:], offs)
        load_w(0)
        load_words(0)
        load_w(1)
        for o in range(PASSES):
            nc.vector.tensor_copy(picked_scales[:, o, :], table_scales[:, o, :].indirect(offs_sb[:]))
        for r in range(4):
            nc.sync.dma_start(
                out=x_planes[r:P:32].rearrange("p o c -> p (o c)").bitcast(I32),
                in_=picked_scales[P - 16 + r : P : 4].rearrange("p o c -> p (o c)").bitcast(I32),
            )
        load_words(1)
        nc.sync.dma_start(fa_sb[:], fa)
        t_raw = [sb([P, PACK, N], F32, f"t_raw{d}") for d in range(2)]
        m1_sb = sb([P, S], F32, "m1_sb")
        m2_sb = sb([P, V], F32, "m2_sb")
        unit_sb = sb([P, PACK], F32, "unit_sb")
        for d, tm in enumerate((t1, t2)):
            nc.sync.dma_start(out=t_raw[d][:], in_=tm.rearrange("(p j) n -> p j n", j=PACK))
        nc.sync.dma_start(fb_sb[:], fb)
        nc.sync.dma_start(out=m1_sb[:], in_=m1)
        nc.sync.dma_start(out=unit_sb[:], in_=unit.rearrange("(p s) o -> p (s o)", s=PACK))
        nc.sync.dma_start(fd_sb[:], fd)
        nc.sync.dma_start(out=m2_sb[:], in_=m2)
        nc.sync.dma_start(fc_sb[:], fc)

        def quantize(codes, planes, grouped):
            nc.vector.quantize_mx(out=codes.bitcast(FP8X4), scales=planes, in_=grouped)

        w_grouped = [sb([P, PACK, P, PACK], BF16, f"w_grouped{o}") for o in range(PASSES)]
        w_codes = [sb([P, H], U32, "w_codes0"), shared.tile([P, H], U32, name="w_codes1", offset=0, align_bytes=64)]
        w_planes = [sb([P, H], U8, f"w_planes{o}") for o in range(PASSES)]

        def cast_w(o, rows, copy):
            src = w_raw[o][:].rearrange("p j (m s) -> p m s j", s=PACK)
            copy(out=w_grouped[o][:].rearrange("p s m j -> p m s j")[:, rows], in_=src[:, rows])

        def quantize_w(o):
            quantize(w_codes[o][:], w_planes[o][:], w_grouped[o][:].rearrange("p s m j -> p (s m j)"))

        low, high, whole = slice(0, HALF_S), slice(HALF_S, S), slice(0, S)
        third, fourth = slice(HALF_S, HALF_S + S // 4), slice(S - S // 4, S)
        pieces = [(first_slot, low), (first_slot, third), (first_slot, fourth)]
        pieces = pieces + [(ORDER[1], low), (ORDER[1], high)] + [(s, whole) for s in ORDER[2:]]
        y_acc = [bank(b, [P, cols.stop - cols.start], f"y_acc{b}") for b, (s, cols) in enumerate(pieces)]

        def product(o, b, cols, stop):
            s, held = pieces[b]
            nc.tensor.matmul_mx(
                out=y_acc[b][:, cols.start - held.start : cols.stop - held.start],
                lhsT=w_codes[o][:, P * s : P * (s + 1)].bitcast(FP8X4),
                lhsT_scale=w_planes[o][:, P * s : P * (s + 1)],
                rhs=x_codes[o][:, cols].bitcast(FP8X4),
                rhs_scale=x_planes[:, o, cols],
                start=(o == 0),
                stop=stop,
            )

        cast_w(0, slice(0, P), nc.scalar.copy)
        nc.vector.tensor_copy(x_codes[0][:], table_words[0][:].bitcast(U32).indirect(offs_sb[:]))
        quantize_w(0)
        for b, (s, cols) in enumerate(pieces):
            product(0, b, cols, False)
        cast_w(1, slice(0, VECTOR_ROWS), nc.vector.tensor_copy)
        cast_w(1, slice(VECTOR_ROWS, P), nc.scalar.copy)
        quantize_w(1)
        for cols in (low, third, fourth):
            nc.vector.tensor_copy(
                x_codes[1][:, cols], table_words[1][:].bitcast(U32).indirect(offs_sb[:, cols.start // 16 : cols.stop // 16])
            )
        product(1, 0, low, True)
        product(1, 3, low, True)
        product(1, 1, third, True)
        product(1, 2, fourth, True)
        product(1, 4, high, True)
        product(1, 5, whole, True)
        product(1, 6, whole, True)

        def empty_y(b, copy):
            s, cols = pieces[b]
            copy(out=y[s][:, cols], in_=y_acc[b][:])

        t_grouped = sb([P, 2, N, PACK], BF16, "t_grouped")
        t_planes = sb([P, 2, N], U8, "t_planes")

        for d in range(2):
            nc.gpsimd.tensor_scalar(t_grouped[:, d], t_raw[d][:].rearrange("p j c -> p c j"), 1.0, 0.0, MULT, ADD)
        empty_y(0, nc.vector.tensor_copy)
        empty_y(1, nc.vector.tensor_copy)

        y[ORDER[2]] = shared.tile([P, S + SPARE], F32, name="y_third", offset=0)
        y_fa = {s: sb([P, S], F32, f"y_fa{s}") for s in ORDER}
        y_fb = {s: sb([P, S], F32, f"y_fb{s}") for s in ORDER[:3]}
        p1 = {s: sb([P, V, 2], F32, f"p1_{s}") for s in ORDER}
        x1_fc = sb([P, PACK, V], F32, "x1_fc")
        z_grouped = [sb([P, 2, HALF_V, PACK], BF16, f"z_grouped{h}") for h in range(2)]
        z_codes = [sb([P, 2, HALF_V], U32, f"z_codes{h}") for h in range(2)]
        z_planes = [sb([P, 2, HALF_V], U8, f"z_planes{h}") for h in range(2)]
        result = [sb([P, HALF_V], F32, f"result{h}") for h in range(2)]

        def look_up_fa(s):
            nc.scalar.activation(out=y_fa[s][:], in_=y[s][:].indirect(fa_sb[:]), func=COPY)

        def look_up_fb(s):
            nc.vector.tensor_tensor(y_fb[s][:], y[s][:].indirect(fb_sb[:]), m1_sb[:], MULT)

        def multiply(s, cols=whole):
            nc.vector.scalar_tensor_tensor(
                out=p1[s][:].rearrange("p v d -> p (v d)")[:, cols],
                in0=y_fa[s][:, cols],
                scalar=unit_sb[:, s : s + 1],
                in1=y_fb[s][:, cols],
                op0=MULT,
                op1=MULT,
            )

        def sum_pairs(s):
            nc.vector.tensor_tensor(x1[s][:, :V], p1[s][:, :, 0], p1[s][:, :, 1], ADD)
            nc.sync.dma_start(out=x1_all[:, V * s : V * (s + 1)], in_=x1[s][:, :V])

        def sum_pairs_last(h):
            cols = slice(HALF_V * h, HALF_V * (h + 1))
            nc.vector.tensor_tensor(x1_all[:, cols], p1[LAST][:, cols, 0], p1[LAST][:, cols, 1], ADD)

        def look_up_fd(s):
            nc.scalar.activation(out=y_fd[:, s, :], in_=y[s][:].indirect(fd_sb[:]), func=COPY)

        def look_up_fd_weighed(s):
            nc.vector.tensor_tensor(second[:, s, :], y[s][:].indirect(fd_sb[:]), m2_sb[:], MULT)

        def weigh_second(h):
            cols = slice(HALF_V * h, HALF_V * (h + 1))
            spread = m2_sb[:, cols].unsqueeze(1).to_broadcast([P, PACK - 1, HALF_V])
            nc.vector.tensor_tensor(second[:, : PACK - 1, cols], y_fd[:, :, cols], spread, MULT)

        def look_up_fc(s):
            nc.scalar.activation(out=x1_fc[:, s, :], in_=x1[s][:].indirect(fc_sb[:]), func=COPY)

        def look_up_fc_last(h):
            nc.scalar.activation(
                out=x1_fc[:, LAST, HALF_V * h : HALF_V * (h + 1)],
                in_=x1_all[:].indirect(fc_sb[:, HALF_V // 16 * h : HALF_V // 16 * (h + 1)]),
                func=COPY,
            )

        def woven(rows, h):
            return rows[:, :, HALF_V * h : HALF_V * (h + 1)].rearrange("p s (c i) -> p c s i", i=4)

        def grouped(d, h):
            return z_grouped[h][:, d].rearrange("p (c i) s -> p c s i", i=4)

        def weave_z0(h):
            nc.scalar.copy(out=grouped(0, h), in_=woven(x1_all[:].rearrange("p (s v) -> p s v", s=PACK), h))

        def weave_z1(h):
            nc.vector.tensor_tensor(grouped(1, h), woven(x1_fc[:], h), woven(second[:], h), MULT)

        def quantize_z(h, depths):
            quantize(
                z_codes[h][:, depths].rearrange("p d v -> p (d v)"),
                z_planes[h][:, depths].rearrange("p d v -> p (d v)"),
                z_grouped[h][:, depths].rearrange("p d v j -> p (d v j)"),
            )

        def finish(h, copy, queue):
            cols = slice(HALF_V * h, HALF_V * (h + 1))
            acc = bank(h, [P, HALF_V], f"out_acc{h}")
            for d in (1, 0):
                nc.tensor.matmul_mx(
                    out=acc[:],
                    lhsT=t_codes[:, d].bitcast(FP8X4),
                    lhsT_scale=t_planes[:, d],
                    rhs=z_codes[h][:, d].bitcast(FP8X4),
                    rhs_scale=z_planes[h][:, d],
                    start=(d == 1),
                    stop=(d == 0),
                )
            copy(out=result[h][:], in_=acc[:])
            queue.dma_start(out=out[:, cols], in_=result[h][:])

        a, b, c, e = ORDER
        empty_y(3, nc.scalar.copy)
        empty_y(2, nc.scalar.copy)
        empty_y(4, nc.scalar.copy)
        look_up_fa(a)
        empty_y(5, nc.scalar.copy)
        look_up_fa(b)
        empty_y(6, nc.scalar.copy)
        look_up_fa(c)
        look_up_fa(e)
        look_up_fb(a)
        look_up_fb(b)
        multiply(a)
        look_up_fb(c)
        multiply(b)
        sum_pairs(a)
        multiply(c)
        sum_pairs(b)
        sum_pairs(c)
        y_fb[e] = sb([P, S], F32, "y_fb_last", f"p1_{b}")
        look_up_fb(e)
        t_codes = sb([P, 2, N], U32, "t_codes", f"p1_{c}")
        quantize(
            t_codes[:].rearrange("p d n -> p (d n)"),
            t_planes[:].rearrange("p d n -> p (d n)"),
            t_grouped[:].rearrange("p d n j -> p (d n j)"),
        )
        multiply(e, low)
        multiply(e, high)
        for h in range(2):
            sum_pairs_last(h)
        y_fd = sb([P, PACK - 1, V], F32, "y_fd", f"y_fa{c}")
        second = sb([P, PACK, V], F32, "second", f"y_fa{e}")
        for s in (b, c, e):
            look_up_fd(s)
        for s in EARLY:
            look_up_fc(s)
        look_up_fd_weighed(a)
        for h in range(2):
            weigh_second(h)
        for h in range(2):
            look_up_fc_last(h)
        for h in range(2):
            weave_z1(h)
        for h in range(2):
            weave_z0(h)
        quantize_z(0, slice(0, 2))
        quantize_z(1, slice(1, 2))
        quantize_z(1, slice(0, 1))
        finish(0, nc.scalar.copy, nc.scalar)
        finish(1, nc.vector.tensor_copy, nc.sync)
